import numpy as np, ml_dtypes
CORES = [36,164,52,180,100,228,116,244]
N = 8
BF = ml_dtypes.bfloat16
W, H, P, RO, ST, TH = 2560, 1024, 256, 5, 3, 34
def place(o, i):
    return o[np.arange(8)[None, :, None, None], i]
def ground(rng):
    o = np.argsort(rng.random((8, W)), axis=-1); x = np.zeros((N, 8, 16, W), np.int64); top = np.zeros(8, np.int64)
    for g in range(8):
        m = int(rng.choice(np.array([3, 5, 8]))); c = rng.integers(0, 16, (m, 16)); s = np.linspace(0, m, W, endpoint=False)
        i = np.minimum(s.astype(np.int64), m - 1); f = (s - i)[:, None]
        b = np.rint(c[i] * (1 - f) + c[(i + 1) % m] * f).astype(np.int64).T
        y = b[None] + rng.integers(-1, 2, (N, 16, W))
        y = np.where(rng.random((N, 1, W)) < 0.03, rng.integers(0, 16, (N, 16, W)), y)
        x[:, g] = np.clip(y, 0, 15)[:, :, np.argsort(o[g])]; top[g] = W * 28 // (85 * m)
    return o, top, x
def knot(rng, r, share):
    k = (N, 8, 1, r.shape[3]); p = rng.integers(0, 15, k); q = np.minimum(p + rng.integers(1, 5, k), 15)
    hit = (rng.random(k) < share) & (np.arange(16)[None, None, :, None] == q)
    return np.where(hit, np.take_along_axis(r, p, 2), r)
def walk(rng, o, top, n):
    st = np.floor((rng.random((N, 8, 15, n)) * 1.2 - 0.2) * top[None, :, None, None]).astype(np.int64)
    st = st + np.where(rng.random(st.shape) < 0.01, rng.integers(0, W, st.shape), 0)
    a = rng.integers(0, W, (N, 8, 1, n))
    return knot(rng, place(o, np.concatenate([a, a + np.add.accumulate(st, axis=2)], axis=2) % W), 0.4)
def ladder(rng, lev):
    pm = np.argsort(rng.random((8, 16)), axis=-1)
    return np.clip(lev[:, :, None, :] - 15 * pm[None, :, :, None], 0, 15)
def pack(x, c, r):
    return {"x": np.ascontiguousarray(x.reshape(N, 128, W)).astype(np.float32).astype(BF), "c0": np.ascontiguousarray(c.reshape(N, 128, H)).astype(np.int32),
            "r0": np.ascontiguousarray(r.reshape(N, 128, P)).astype(np.int32)}
def setup_inputs(rng):
    o, top, x = ground(rng)
    return pack(x, walk(rng, o, top, H), walk(rng, o, top, P))
def setup_inputs_ties(rng):
    o = np.argsort(rng.random((8, W)), axis=-1); cls = np.argsort(o, axis=-1) % 7
    cr = np.where(rng.random((N, 8, W)) < 0.04, rng.integers(0, 7, (N, 8, W)), cls[None])
    lev = np.array([0, 1, TH, TH + 1, 2 * TH, 2 * TH + 1, 3 * TH + 2])[cr]
    def some(n):
        i = rng.integers(0, 6, (N, 8, n)); rows = [i]
        for p in range(15):
            jump = rng.random((N, 8, n)) < 0.04
            d = np.where(jump, rng.choice(np.array([-3, 3]), (N, 8, n)), rng.choice(np.array([-2, -2, -1, 0, 1, 2, 2]), (N, 8, n)))
            i = np.clip(i + d, 0, 5 + jump.astype(np.int64)); rows.append(i)
        i = np.stack(rows, axis=2)
        return place(o, i + 7 * rng.integers(0, W // 7, i.shape))
    return pack(ladder(rng, lev), some(H), some(P))
def setup_inputs_clash(rng):
    hi = np.arange(W - 64, W); last6 = (hi[:, None] * hi[None, :]) % 64 == 63; over = last6 & (hi[:, None] * (hi[None, :] + 64) > 2 ** 24)
    hu, hv = np.nonzero(over if np.any(over) else last6)
    nm = rng.random((8, W)) < 0.5; a = rng.integers(1, H - 1, 8); row = np.arange(16)[None, :, None]
    r = np.zeros((N, 8, 16, P), np.int64); c = np.zeros((N, 8, 16, H), np.int64); lev = np.zeros((N, 8, W), np.int64)
    for g in range(8):
        sp = np.array([0, H - 1, int(a[g]), int(a[g]) + H]); nm[g, sp] = True
        apart = rng.permutation(H)[:P] + H * rng.integers(0, 2, P)
        if g == 4: nm[g, apart] = True
        if g == 5: nm[g, W - 64:] = True
        ne, fa = np.flatnonzero(nm[g]), np.flatnonzero(~nm[g])
        if g < 2: u, v = sp[2:], np.array([0, 0])
        elif g < 4: u, v = sp[:2], np.array([int(rng.choice(ne)), 0])
        elif g == 4: u, v = apart, np.zeros(P, np.int64)
        elif g == 5: u, v = hi[hu], hi[hv]
        else: u, v = rng.choice(ne, 8), rng.choice(ne, 8)
        i = rng.integers(0, len(u), (N, P)); k = rng.integers(0, 16, (N, P))
        if g == 4: i = np.argsort(rng.random((N, P)), axis=-1)
        if g == 1 or g == 4: k = rng.integers(0, 14, (N, P))
        if g == 0: k[0, :3] = 15; k[0, 3] = 5; k[1] = 15; k[1, P - 1] = 3
        k[2] = np.minimum(k[2], 14)
        at = np.where(k < 15, k, rng.integers(0, 15, (N, P)))
        y = np.where(row > k[:, None], rng.choice(fa, (N, 16, P)), rng.choice(ne, (N, 16, P)))
        y = np.where(row == at[:, None], u[i][:, None], y)
        y[:, 15] = np.where(k == 14, y[:, 15], v[i]); r[:, g] = y
        flip = rng.random((N, W)) < 0.02; flip[:, sp] = False; flip[:3] = False
        lev[:, g] = np.where(nm[g][None] ^ flip, 0, 150) + rng.integers(0, 6, (N, W))
        c[:, g] = np.where(rng.random((N, 1, H)) < 0.5, rng.choice(ne, (N, 16, H)), rng.integers(0, W, (N, 16, H)))
    return pack(ladder(rng, lev), c, r)
def setup_inputs_loops(rng):
    o, top, x = ground(rng); x[:, ::2] = rng.integers(0, 3, (N, 4, 16, W))
    e = np.argsort(o, axis=-1); b = 1 + 2 * int(rng.integers(0, 4)); z = int(rng.integers(0, N))
    x[:, b] = np.where(e[b] % 3 == 0, rng.integers(0, 3, (N, 16, W)), x[:, b])
    def tie(r):
        kd = rng.integers(0, 8, (N, 8, r.shape[3]))
        for p in range(1, 16):
            r[:, :, p] = np.where(kd == 1, r[:, :, 0], r[:, :, p])
            if p > 1: r[:, :, p] = np.where(kd == 7, r[:, :, p % 2], r[:, :, p])
        for m, dst, src in ((2, 15, 0), (3, 15, 14), (4, 5, 0), (4, 9, 0), (5, 4, 1), (5, 6, 2), (6, 12, 3), (6, 8, 5)):
            r[:, :, dst] = np.where(kd == m, r[:, :, src], r[:, :, dst])
        return r
    w = walk(rng, o, top, P); w[z, b] = o[b][e[b][w[z, b]] // 3 * 3]
    return pack(x, tie(walk(rng, o, top, H)), tie(w))
def setup_inputs_calm(rng):
    o, top, x = ground(rng); q = rng.permutation(N)
    x[q[0]] = rng.integers(0, 3, (8, 16, W)); x[q[1]] = 15 * rng.integers(0, 2, (8, 16, W))
    x[:, int(rng.integers(0, 8))] = rng.integers(0, 3, (N, 16, W))
    e = np.argsort(o, axis=-1); home = e[None] % N == np.arange(N)[:, None, None]
    x = np.where(home[:, :, None], rng.integers(0, 3, x.shape), x)
    i = place(e, walk(rng, o, top, P)) // N * N + np.arange(N)[:, None, None, None]
    return pack(x, walk(rng, o, top, H), place(o, np.where(i < W, i, i - N)))
def setup_inputs_spread(rng):
    o = np.argsort(rng.random((8, W)), axis=-1); e = np.argsort(o, axis=-1) % 5
    x = np.floor(rng.random((N, 8, 16, W)) * np.exp2(4.0 - e)[None, :, None, :]).astype(np.int64)
    def some(n):
        k = rng.integers(0, 4, (N, 8, 1, n)); u = rng.random((N, 8, 16, n)); b = 5 * np.floor(u * (W // 5)).astype(np.int64)
        i = np.where(k == 0, np.floor(W * u).astype(np.int64), np.floor(W * u ** 4).astype(np.int64))
        i = np.where(k == 2, b + rng.integers(3, 5, u.shape), np.where(k == 3, b + rng.integers(2, 5, u.shape), i))
        return place(o, np.minimum(i, W - 1))
    return pack(x, some(H), some(P))
def check_inputs(d):
    bad = []; a = np.asarray(d["x"]).astype(np.float32)
    if not np.all((a >= 0) & (a <= 15) & (a == np.floor(a))): bad.append("whole numbers of x")
    for k in ("c0", "r0"):
        if np.min(d[k]) < 0 or np.max(d[k]) > W - 1: bad.append("range of " + k)
    return bad
def look(xs, R):
    return np.take_along_axis(xs, R.reshape(N, 8, 1, 16 * P), axis=3).reshape(N, 8, 16, 16, P)
def far(v, d):
    return np.add.reduce(np.abs(v[:, :, :, :16 - d] - v[:, :, :, d:]), axis=2)
def first(bad):
    return np.where(np.any(bad, axis=2), np.argmax(bad, axis=2), 15)[:, :, None, :]
def reference(x, c0, r0):
    xs = x.astype(np.float32).astype(np.int32).reshape(N, 8, 16, W); C = c0.astype(np.int64).reshape(N, 8, 16, H).copy()
    R = r0.astype(np.int64).reshape(N, 8, 16, P)
    kap = np.zeros(N, np.int64); row = np.arange(16)[None, None, :, None]
    for rnd in range(RO):
        if rnd > 0: R = np.roll(R, ST, axis=0)
        bad = far(look(xs, R), 1) > TH; fail = np.any(bad, axis=2); k = first(bad)
        rk = np.take_along_axis(R, k, 2)[:, :, 0]
        h = (((rk * R[:, :, 15]) >> 6) + rk + kap[:, None, None]) & (H - 1)
        R = np.where((row > k) & (row < 15), np.take_along_axis(C, h[:, :, None, :], 3), R)
        same = R[:, :, :, None] == R[:, :, None]
        q = 15 - np.argmax(same[:, :, :, ::-1], axis=3)
        p = first((q > row)[:, :, :15])
        R = np.where((row >= p) & (row <= np.take_along_axis(q, p, 2)), np.take_along_axis(R, p, 2), R)
        v = look(xs, R); k2 = first(far(v, 1) > TH)
        S = np.where((row > k2) & (row < 15), np.take_along_axis(R, k2, 2), R)
        for j in range(P - 1, -1, -1):
            a, g = np.nonzero(fail[:, :, j])
            C[a, g, :, h[a, g, j]] = S[:, :, :, j][a, g]
        near = far(v, 2) <= TH; R = R.copy()
        R[:, :, 1:14:2] = np.where(near[:, :, 0:13:2], R[:, :, 0:13:2], R[:, :, 1:14:2])
        kap = np.add.reduce(fail.astype(np.int64), axis=(1, 2))
    return {"yc": C.reshape(N, 128, H).astype(np.float32), "yr": R.reshape(N, 128, P).astype(np.float32)}

@@ -1,0 +1,558 @@
+from concourse.bass import DstId, RemoteDMATransfer
+from concourse.mybir import dt, AluOpType as A, AxisListType, ActivationFunctionType as F
+
+NC = 4
+n = 256 // NC
+NL = n // 16
+ROUNDS = 5
+CW = 1408
+MODE1 = "AMMM"
+MODE2 = "AMAM"
+HG = 2
+
+SCRATCH = {
+    "xw": ("sbuf", [128, 2560], "bfloat16"), "ri": ("sbuf", [128, 256], "int32"), "ci": ("sbuf", [128, 1024], "int32"),
+    "cc": ("sbuf", [128, CW], "float32"), "cy": ("sbuf", [128, CW], "float32"),
+    "rf": ("sbuf", [128, 256 * ROUNDS], "float16"), "sd": ("sbuf", [128, 256 * ROUNDS], "float16"),
+    "rl": ("sbuf", [128, 512], "uint16"), "rls": ("sbuf", [128, 512], "uint16"),
+    "rl2": ("sbuf", [128, 512], "uint16"), "rls2": ("sbuf", [128, 512], "uint16"),
+    "v1": ("sbuf", [128, 4096], "bfloat16"), "m1": ("sbuf", [128, 4096], "bfloat16"),
+    "v2": ("sbuf", [128, 4096], "bfloat16"), "m2": ("sbuf", [128, 4096], "bfloat16"), "ad": ("sbuf", [128, 2048], "bfloat16"),
+    "f": ("sbuf", [128, 512], "float16"), "q": ("sbuf", [128, 512], "float16"), "mk": ("sbuf", [128, 512], "float16"),
+    "rn": ("sbuf", [128, 512], "float16"), "cm": ("sbuf", [128, 512], "float16"), "r2": ("sbuf", [128, 512], "float16"),
+    "em": ("sbuf", [128, 4096], "float16"), "hd": ("sbuf", [128, 512], "float16"), "g1": ("sbuf", [128, 512], "float16"),
+    "qd": ("sbuf", [128, 512], "float16"), "eq": ("sbuf", [128, 512], "float16"), "ins": ("sbuf", [128, 512], "float16"),
+    "t3": ("sbuf", [128, 512], "float32"), "r3": ("sbuf", [128, 512], "float16"), "r3c": ("sbuf", [128, 512], "float32"),
+    "fs": ("sbuf", [128, 1024], "float16"), "fz": ("sbuf", [128, 1024], "float16"), "nr": ("sbuf", [128, 512], "float16"),
+    "t4": ("sbuf", [128, 512], "float32"), "q5": ("sbuf", [128, 512], "float16"), "k5": ("sbuf", [128, 512], "float16"),
+    "t5": ("sbuf", [128, 512], "float32"), "yo": ("sbuf", [128, 256], "float32"),
+    "rr": ("sbuf", [128, 16 * ROUNDS], "float32"), "q15": ("sbuf", [128, 256], "float16"),
+    "w": ("sbuf", [128, 32], "float32"), "hi": ("sbuf", [128, 32], "int32"), "hj": ("sbuf", [128, 32], "int32"),
+    "hl": ("sbuf", [128, 32], "uint16"), "nf": ("sbuf", [128, 32], "float32"), "hf": ("sbuf", [128, 32], "float16"),
+    "e3": ("sbuf", [128, 128], "float16"), "lo": ("sbuf", [128, 16], "float32"), "tj": ("sbuf", [128, 16], "float32"),
+    "tm": ("sbuf", [128, 16], "float32"), "ts": ("sbuf", [128, 16], "float32"), "off": ("sbuf", [128, 64], "uint16"),
+    "kc": ("sbuf", [128, ROUNDS], "float32"), "kj": ("sbuf", [128, 64], "float32"),
+    "col": ("sbuf", [128, 8], "float32"), "one": ("sbuf", [128, 128], "bfloat16"),
+    "B8": ("sbuf", [128, 1024], "bfloat16"), "UP": ("sbuf", [128, 1024], "bfloat16"), "UC": ("sbuf", [128, 1024], "bfloat16"),
+    "DD": ("sbuf", [128, 1024], "bfloat16"), "MM": ("sbuf", [128, 1024], "bfloat16"), "MH": ("sbuf", [128, 1024], "bfloat16"),
+    "W2": ("sbuf", [128, 2048], "bfloat16"), "NW": ("sbuf", [128, 2048], "bfloat16"),
+}
+for _k in ("B", "B0", "I", "L", "SH", "SD", "LI", "UI", "US", "LP", "ZN", "ZA", "ZT", "IT", "IK", "I2", "I16", "NI", "NH", "YA",
+           "DS", "R15", "C2", "C19"):
+    SCRATCH[_k] = ("sbuf", [128, 128], "bfloat16")
+for _k in range(8):
+    SCRATCH["b%d" % _k] = ("psum", [128, 512], "float32")
+SEMAPHORES = ["v", "s", "p", "q", "sent", "ar", "dr", "dx", "dc", "oy0", "oy1", "oc"] + \
+    ["a%d_%d" % (t, c) for t in range(1, ROUNDS) for c in range(NC)]
+WIDE = set(k for k in SCRATCH if SCRATCH[k][2] in ("float32", "int32"))
+
+CY, PE, GA, WAKE, OWN, NET = 0.001, 0.0005, 1.6, 0.16, 0.06, 4.0
+TUNE = {
+    'rl': '4341', 'b3': '844484644438', 'rls': '48', 'v1': '87456300', 'm1': '5250527', 'b5': '454860575157', 'b2': '808444432',
+    'f': '23', 'q': '48', 'w': '56', 'hi': '43', 'hj': '56', 'hl': '52', 'nf': '45', 'mk': '72', 'rn': '43', 'cm': '46',
+    'rl2': '4818', 'r2': '8845', 'b1': '4814654663', 'b4': '34347541', 'b6': '4414843', 'b7': '1254548', 'b0': '76842336',
+    'em': '3321', 'rls2': '7', 'v2': '0200455', 'm2': '231700', 'ad': '112', 'hd': '443', 'qd': '7742', 'g1': '663', 'eq': '512',
+    'ins': '68', 't3': '8845', 'r3': '5682', 'fs': '4418', 'fz': '445', 'nr': '4481', 't4': '4608', 'sd': '4846', 'send': '867',
+    'r3c': '3432', 'q5': '341', 'k5': '0446', 't5': '846', 'e3': '5', 'lo': '3', 'cc': '5276642224604340', 'yo': '0447',
+    'dma': '226', 'cy': '36312546568454123'}
+
+
+def R(name, a, b, step=1):
+    return (name, a, b, (slice(None), slice(a, b, step)))
+
+
+def size(r):
+    s = r[3][-1]
+    return len(range(s.start, s.stop, s.step or 1))
+
+
+def ind(win, off):
+    return ("ind", win, off)
+
+
+def isref(x):
+    return isinstance(x, tuple)
+
+
+def make_plan():
+    ops = []
+
+    def op(queue, kind, args, reads, writes, cost, **kw):
+        d = dict(i=len(ops), q=queue, kind=kind, args=args, r=[], w=list(writes), cost=cost, sem=None, pb=0)
+        for x in reads:
+            if isref(x):
+                d["r"] += [x[1], x[2]] if x[0] == "ind" else [x]
+        d.update(kw)
+        ops.append(d)
+        return d
+
+    def boost(x, o):
+        o["pb"] = x
+
+    two = lambda r: r[0] not in WIDE and r[0][0] != "b"
+
+    def ts(out, in0, s1, s2=None, op0=A.add, op1=None):
+        c = max(64, size(in0) * (0.5 if two(out) and two(in0) else 1)) * CY
+        return op("v", "ts", (out, in0, s1, s2, op0, op1), [in0, s1, s2], [out], c)
+
+    def tt(out, in0, in1, o):
+        if out[0] == "ind":
+            return op("v", "tt", (out, in0, in1, o), [in0, in1, out[2]], [out[1]], 0.05 + size(in0) * 3 * CY)
+        if in0[0] == "ind":
+            c = 0.05 + size(in1) * GA * CY
+        else:
+            c = max(64, size(in0) * (1 if in0[0][0] == "b" or in1[0][0] == "b" else 2)) * CY
+        return op("v", "tt", (out, in0, in1, o), [in0, in1], [out], c)
+
+    def cp(out, in_):
+        return op("v", "cp", (out, in_), [in_], [out], max(64, size(out)) * CY)
+
+    def ms(out, val):
+        return op("v", "ms", (out, val), [], [out], max(64, size(out) * (.5 if two(out) else 1)) * CY)
+
+    def act(out, in_, fn, bias=0.0, scale=1.0, acc=None):
+        k = size(out)
+        return op("s", "act", (out, in_, fn, bias, scale, acc), [in_], [out] + ([acc] if acc else []),
+                  (0.065 + k * GA * CY) if in_[0] == "ind" else max(64, k) * CY)
+
+    def K(name):
+        return R(name, 0, 128)
+
+    def grp(out, *pairs):
+        last = len(pairs) - 1
+        return [(out, K(a) if isinstance(a, str) else a, b, i == 0, i == last) for i, (a, b) in enumerate(pairs)]
+
+    def mm(*mms):
+        rd = []
+        for m in mms:
+            rd += [m[1], m[2]]
+        return op("p", "mm", mms, rd, sorted(set((m[0][0], m[0][1], m[0][2]) for m in mms)), sum(max(64, size(m[2])) for m in mms) * PE)
+
+    def sel(out, in_, pat, cmp, fill, base, cm):
+        return op("q", "sel", (out, in_, pat, cmp, fill, base, cm), [in_], [out], 0.17 + 2 * size(out) * CY)
+
+    def dma(sem, out, in_, reads, writes, cost):
+        return op("y", "dma", (out, in_), reads, writes, cost, sem=sem)
+
+    dma("dr", R("ri", 0, 256), ("T", "r0"), [], [R("ri", 0, 256)], 2.2)
+    dma("dx", R("xw", 0, 2560), ("T", "x"), [], [R("xw", 0, 2560)], 5.0)
+    dma("dc", R("ci", 0, 1024), ("T", "c0"), [R("xw", 0, 2560)], [R("ci", 0, 1024)], 4.5)
+    IN = [[-16, 8], [-1, 16]]
+    boost(1000, ms(K("one"), 1.0))
+    sel(K("B0"), K("one"), [[-16, 8], [0, 16]], A.is_ge, 0.0, 0, 1)
+    sel(K("B"), K("B0"), [[16, 8], [0, 16]], A.is_ge, 0.0, 15, -1)
+    boost(200, sel(K("I"), K("B"), IN, A.is_equal, 0.0, 0, 1))
+    boost(100, sel(K("SH"), K("B"), IN, A.is_equal, 0.0, -1, 1))
+    ms(R("W2", 0, 2048), 0.0)
+    boost(90, sel(K("L"), K("B"), [[16, 8], [1, 16]], A.is_gt, 0.0, 0, -1))
+    sel(K("SD"), K("B"), IN, A.is_equal, 0.0, 1, 1)
+    for p in range(16):
+        a = 128 * p
+        ts(("W2", a, a + 128, (slice(None), slice(a + p, a + 128, 16))), R("B", 0, 128, 16), 2.0, None, A.mult)
+    act(K("NI"), K("I"), F.Copy, scale=-1.0)
+    act(K("NH"), K("I"), F.Copy, scale=-0.5)
+    for i in range(4):
+        a = 512 * i
+        o = R("b%d" % i, 0, 512)
+        if i:
+            mm(*grp(o, ("NH", R("W2", a, a + 512)), ("NH", R("W2", a - 128, a + 384))))
+        else:
+            mm(*(grp(R("b0", 0, 128), ("NH", R("W2", 0, 128))) +
+                 grp(R("b0", 128, 512), ("NH", R("W2", 128, 512)), ("NH", R("W2", 0, 384)))))
+        act(R("NW", a, a + 512), o, F.Copy)
+    for c in range(NC):
+        ts(R("rf", c * n, c * n + n), R("ri", c * n, c * n + n), -1280.0)
+    op("v", "red", (R("col", 0, 1), R("I", 15, 128, 16)), [R("I", 15, 128, 16)], [R("col", 0, 1)], .07)
+    op("v", "red", (R("col", 1, 2), R("I", 1, 128, 2)), [R("I", 1, 128, 2)], [R("col", 1, 2)], .07)
+    tt(R("col", 2, 3), R("col", 1, 2), R("col", 0, 1), A.subtract)
+    ts(R("col", 3, 4), R("col", 2, 3), 3.5, -1.0, A.mult, A.add)
+    ts(R("q15", 0, 256), R("rf", 0, 256), R("col", 0, 1), None, A.mult)
+    mm(*grp(R("b4", 256, 272), *[(R("W2", 128 * j, 128 * j + 128), R("q15", j, 256, 16)) for j in range(16)]))
+    ts(R("rr", 0, 16), R("b4", 256, 272), 1.0 / 256, 10.5, A.mult, A.add)
+    op("q", "rsend", (), [R("rr", 0, 16)], [], 1.5)
+    op("n", "arr", (), [], [R("rr", 16, 16 * ROUNDS)], 0.0, sem="ar", tdep=(ops[-1], NET))
+    act(K("ZT"), K("L"), F.Copy, scale=-16384.0)
+    act(K("ZA"), K("I"), F.Copy, scale=8192.0)
+    tt(K("ZA"), K("ZA"), K("ZT"), A.add)
+    act(K("LP"), K("L"), F.Copy)
+    act(R("LP", 15, 128, 16), R("I", 15, 128, 16), F.Copy, scale=0.0)
+    act(K("ZN"), K("LP"), F.Copy, scale=-8192.0)
+    act(K("IT"), K("I"), F.Copy)
+    act(R("IT", 15, 128, 16), R("I", 15, 128, 16), F.Copy, scale=0.0)
+    act(K("IK"), K("IT"), F.Copy, scale=1280.0)
+    ms(K("C2"), 320.0)
+    ms(("C2", 0, 128, (slice(0, 1), slice(0, 128))), 318.0)
+    ms(K("C19"), 150.0)
+    ms(("C19", 0, 128, (slice(0, 1), slice(0, 128))), 149.0)
+    ms(R("kc", 0, 1), -0.4921875)
+    ts(R("cc", 0, 1024), R("ci", 0, 1024), -1280.0)
+    ms(R("cc", 1024, CW), 0.0)
+    ms(R("cy", 1024, CW), 0.0)
+    for h in range(8):
+        ts(R("B8", 128 * h, 128 * h + 128), K("B"), 1.0, None, A.mult)
+    sel(R("UP", 0, 1024), R("B8", 0, 1024), [[-1, 8], [-16, 8], [-1, 16]], A.is_equal, 0.0, -1, 1)
+    sel(R("UC", 0, 1024), R("B8", 0, 1024), [[1, 8], [-16, 8], [-1, 16]], A.is_equal, 0.0, -15, 1)
+    T1 = lambda nm, s: R(nm, 128 * s, 128 * s + 128)
+    for h in range(2):
+        o = "b%d" % (6 + h)
+        mm(*sum([grp(T1(o, i), ("I", T1("UP", 4 * h + i)), (T1("UC", 4 * h + i), K("I")), ("NI", K("I"))) for i in range(4)], []))
+        act(R("DD", 512 * h, 512 * h + 512), R(o, 0, 512), F.Copy)
+    for h in range(2):
+        o = "b%d" % (6 + h)
+        mm(*sum([grp(T1(o, i), (T1("UP", 4 * h + i), T1("UP", 4 * h + i)), ("I", T1("UC", 4 * h + i))) for i in range(4)], []))
+        act(R("MM", 512 * h, 512 * h + 512), R(o, 0, 512), F.Copy)
+    for h in range(2):
+        o = "b%d" % (6 + h)
+        mm(*sum([grp(T1(o, i), (T1("UP", 4 * h + i), K("I")), ("I", T1("UC", 4 * h + i)), ("I", K("I")), ("NI", T1("MM", 4 * h + i)))
+                 for i in range(4)], []))
+        act(R("MH", 512 * h, 512 * h + 512), R(o, 0, 512), F.Copy)
+    tt(K("LI"), K("L"), K("I"), A.add)
+    tt(K("UI"), K("B"), K("L"), A.subtract)
+    tt(K("US"), K("B"), K("LI"), A.subtract)
+    act(K("I2"), K("I"), F.Copy, scale=2.0)
+    act(K("I16"), K("I"), F.Copy, scale=16.0)
+    tt(K("YA"), K("I"), K("SD"), A.add)
+    tt(K("DS"), K("SD"), K("I"), A.subtract)
+    ts(K("R15"), K("one"), R("col", 0, 1), None, A.mult)
+    op("q", "iota", (R("tj", 0, 16), [[16, 16]], 1024, 1), [K("SH")], [R("tj", 0, 16)], 0.17)
+
+    X = R("xw", 0, 2560)
+    sends = {}
+    starts = []
+    for t in range(ROUNDS):
+        starts.append(len(ops))
+        P2 = 256 * (t % 2)
+        last = t == ROUNDS - 1
+
+        def G(name, c, k=n):
+            a = (P2 // 64) * (k * NC // 4) + k * c
+            return R(name, a, a + k)
+
+        def b(c, i, k=n):
+            return R("b%d" % c, 64 * i, 64 * i + k)
+
+        def distances(c, rin, rl, rls, vb, mb, out, mode):
+            v0 = 1024 * c
+            if mode == "M":
+                mm(*grp(b(c, 0), ("SH", rin)))
+                ts(rls, b(c, 0), 1280.0)
+            for h in range(HG):
+                w = 1024 // HG
+                vh, u, z = R(vb, v0 + w * h, v0 + w * h + w), n // HG * h, n // HG * h + n // HG
+                act(vh, ind(X, R(rl[0], rl[1] + u, rl[1] + z)), F.Copy)
+                if mode == "M":
+                    tt(R(mb, v0 + w * h, v0 + w * h + w), ind(X, R(rls[0], rls[1] + u, rls[1] + z)), vh, A.max)
+            red = [(T1("W2", p), R(mb, v0 + p, v0 + 1024, 16)) for p in range(15)]
+            if mode == "M":
+                o = grp(out, *([(T1("NW", p), R(vb, v0 + p, v0 + 1024, 16)) for p in range(16)] + red))
+                mm(*o[:16])
+                return o[16:]
+            for h in range(2):
+                e = "b%d" % (6 + (c + h) % 2)
+                a = v0 + 512 * h
+                mm(*grp(R(e, 0, 511), ("I", R(vb, a + 1, a + 512)), ("NI", R(vb, a, a + 511))))
+                act(R(mb, a, a + 511), R(e, 0, 511), F.Abs, scale=0.5)
+            return grp(out, *red)
+
+        for c in range(NC - 1, -1, -1):
+            rin = R("rf", 256 * t + n * c, 256 * t + n * c + n)
+            if t:
+                op("n", "arr", (), [], [rin], 0.0, sem="a%d_%d" % (t, c), tdep=(sends[t - 1, c], NET))
+            ts(G("rl", c), rin, 1280.0)
+            D = R("b%d" % (4 + c // 2), n * (c % 2), n * (c % 2) + n)
+            mm(*distances(c, rin, G("rl", c), G("rls", c), "v1", "m1", D, MODE1[c]))
+            if c % 2:
+                continue
+            m, d = 2 * n, c // 2
+            rin = R("rf", 256 * t + m * d, 256 * t + m * d + m)
+            g2 = lambda nm: R(nm, P2 + m * d, P2 + m * d + m)
+            l2 = lambda nm: R(nm, 16 * (t % 2) + 2 * NL * d, 16 * (t % 2) + 2 * NL * d + 2 * NL)
+            e = "b%d" % (c + 1)
+            Z1, Z2, Y2 = R(e, 128, 256), R(e, 384, 512), R(e, 0, 2 * NL)
+            ts(g2("f"), R("b%d" % (4 + d), 0, m), 34.5, None, A.is_gt)
+            mm(*(grp(Z1, ("I", rin), ("ZA", g2("f"))) + grp(Z2, ("I", rin), ("ZN", g2("f")))))
+            ts(g2("q"), Z1, 6911.0, -8191.0, A.max, A.add)
+            q0 = g2("q")[1]
+            mm(*grp(Y2, ("C2", R("one", 0, 2 * NL)), *[(T1("W2", j), R("q", q0 + j, q0 + m, 16)) for j in range(16)]))
+            tt(l2("w"), Y2, R("rr", 16 * t + 2 * NL * d, 16 * t + 2 * NL * d + 2 * NL), A.mult)
+            ts(l2("hi"), l2("w"), R("kc", t, t + 1))
+            ts(l2("hj"), l2("hi"), 1023, None, A.bitwise_and)
+            cp(l2("hl"), l2("hj"))
+            ts(l2("nf"), Y2, -1.0, -4096.0, A.is_lt, A.mult)
+            ts(g2("mk"), Z1, -1280.5, None, A.is_lt)
+            ts(g2("rn"), Z2, -1280.0, None, A.max)
+            tt(g2("cm"), ind(R("cc", 0, 1024), l2("hl")), g2("mk"), A.mult)
+            for i in (c + 1, c):
+                mm(*grp(b(i, 4), ("I", G("rn", i)), ("IK", G("mk", i)), ("IT", G("cm", i))))
+                ts(G("rl2", i), b(i, 4), 1280.0)
+                ts(G("r2", i), b(i, 4), 0.0)
+        for c in range(NC - 1, -1, -1):
+            e = "b%d" % (6 + c % 2)
+            mm(*sum([grp(R(e, n * s, n * s + n), (T1("DD", s), G("r2", c))) for s in range(8)], []))
+            em = R("em", 2048 * (t % 2) + 512 * c, 2048 * (t % 2) + 512 * c + 512)
+            ts(em, R(e, 0, 512), 0.0, None, A.is_equal)
+            D = "b%d" % (4 + c % 2)
+            D1 = distances(c, G("r2", c), G("rl2", c), G("rls2", c), "v2", "m2", R(D, 128, 128 + n), MODE2[c])
+            v0 = 1024 * c
+            mm(*grp(R(e, 0, 511), ("I", R("v2", v0 + 2, v0 + 1024, 2)), ("NI", R("v2", v0, v0 + 1022, 2))))
+            act(R("ad", 512 * c, 512 * c + 511), R(e, 0, 511), F.Abs, scale=0.5)
+            mm(*grp(b(c, 5), *[(T1("MM", s), R("em", em[1] + n * s, em[1] + n * s + n)) for s in range(8)]))
+            ts(G("hd", c), b(c, 5), 1.0, None, A.is_ge)
+            mm(*grp(b(c, 6), ("I", G("r2", c)), ("ZA", G("hd", c))))
+            ts(G("qd", c), b(c, 6), 6911.0, -8191.0, A.max, A.add)
+            ts(G("g1", c), b(c, 6), 4000.0, 64.0, A.is_gt, A.mult)
+            mm(*grp(b(c, 0), ("C19", R("one", 0, n)), ("NI", G("r2", c)), ("B", G("qd", c))))
+            ts(G("eq", c), b(c, 0), 0.0, None, A.is_equal)
+            mm(*(grp(b(c, 1), ("LI", G("g1", c)), ("US", G("eq", c))) + grp(b(c, 2), ("LI", G("g1", c)), ("UI", G("eq", c)))))
+            ts(G("ins", c), b(c, 2), 64.5, None, A.is_gt)
+            tt(G("t3", c), b(c, 0), G("ins", c), A.mult)
+            tt(G("r3", c), b(c, 4), G("t3", c), A.add)
+            mm(*D1)
+            mm(*grp(R(D, 192, 192 + n), *[(T1("W2", p + 1), R("ad", 512 * c + p // 2, 512 * c + 512, 8)) for p in range(0, 13, 2)]))
+            fs, fz = G("fs", c, 2 * n), G("fz", c, 2 * n)
+            ts(fs, R(D, 128, 128 + 2 * n), 34.5, 64.5, A.is_gt, A.mult)
+            tt(fz, fs, R("b%d" % c, 64, 64 + 2 * n), A.is_gt)
+            f2, F2 = R("fz", fz[1], fz[1] + n), R("fz", fz[1] + n, fz[1] + 2 * n)
+            mm(*(grp(b(c, 5), ("I2", G("ins", c)), ("YA", f2), ("I16", F2)) + grp(b(c, 6), ("DS", G("r3", c)))))
+            ts(G("nr", c), b(c, 5), R("col", 3, 4), None, A.is_lt)
+            tt(G("t4", c), b(c, 6), G("nr", c), A.mult)
+            if not last:
+                so = R("sd", 256 * t + n * c, 256 * t + n * c + n)
+                tt(so, G("r3", c), G("t4", c), A.add)
+                sends[t, c] = op("q", "send", (t, c), [so], [], 1.0)
+            act(G("r3c", c), G("r3", c), F.Identity if last else F.Copy, bias=1280.0 if last else 0.0)
+            if last:
+                tt(R("yo", n * c, n * c + n), G("r3c", c), G("t4", c), A.add)
+                if c % 2 == 0:
+                    x = n * c
+                    dma("oy%d" % (c // 2), ("T", "yr", x, x + 2 * n), R("yo", x, x + 2 * n), [R("yo", x, x + 2 * n)], [], 2.0)
+            mm(*(grp(b(c, 7), ("I", G("r3", c)), ("ZA", f2)) + grp(b(c, 3), ("LP", f2))))
+            ts(G("q5", c), b(c, 7), 6911.0, -8191.0, A.max, A.add)
+            act(G("k5", c), b(c, 3), F.Sign)
+            mm(*grp(b(c, 0), ("C19", R("one", 0, n)), ("NI", G("r3", c)), ("B", G("q5", c))))
+            tt(G("t5", c), b(c, 0), G("k5", c), A.mult)
+            if c == 2:
+                if not last:
+                    mm(*grp(R("b5", 320, 384), *[("R15", G("mk", i)) for i in range(NC)]))
+                    act(R("kj", 0, 64), R("b5", 320, 384), F.Identity, bias=-0.4921875 / 64, acc=R("kc", t + 1, t + 2))
+                x = 16 * (t % 2)
+                H = lambda nm: R(nm, x, x + 16)
+                tt(H("hf"), H("hj"), H("nf"), A.add)
+                mm(*sum([grp(R("b4", 256 + 16 * e, 272 + 16 * e), (T1("DD", e), H("hf"))) for e in range(8)], []))
+                ts(R("e3", 0, 128), R("b4", 256, 384), 0.0, None, A.is_equal)
+                mm(*grp(R("b5", 256, 272), *[(T1("MH", e), R("e3", 16 * e, 16 * e + 16)) for e in range(8)]))
+                tt(R("lo", 0, 16), R("b5", 256, 272), H("nf"), A.is_gt)
+                tt(R("tm", 0, 16), R("lo", 0, 16), R("tj", 0, 16), A.mult)
+                tt(R("ts", 0, 16), H("hj"), R("tm", 0, 16), A.max)
+                cp(R("off", 2 * x, 2 * x + 32, 2), R("ts", 0, 16))
+                if last:
+                    act(R("cy", 0, 1024), R("cc", 0, 1024), F.Identity, bias=1280.0)
+        for j in range(15, -1, -1):
+            a = P2 + 16 * j
+            tt(ind(R("cy" if last else "cc", 0, CW), R("off", 32 * (t % 2) + 2 * j, 32 * (t % 2) + 2 * j + 1)),
+               R("t5", a, a + 16), R("r3c", a, a + 16), A.add)
+    dma("oc", ("T", "yc", 0, 1024), R("cy", 0, 1024), [R("cy", 0, 1024)], [], 4.0)
+    for t in range(ROUNDS):
+        cnt = {}
+        for o in ops[starts[t]:(starts + [len(ops)])[t + 1]]:
+            if o["kind"] != "arr":
+                nm = o["w"][0][0] if o["w"] else o["kind"]
+                k = cnt.get(nm, 0)
+                cnt[nm] = k + 1
+                s = TUNE.get(nm, "")
+                o["pb"] += int(s[k]) - 4 if k < len(s) else 0
+    return ops
+
+
+def link(ops):
+    seen = {}
+    for o in ops:
+        dep = set()
+        acc = [(r, False) for r in o["r"]] + [(w, True) for w in o["w"]]
+        for r, wr in acc:
+            name, a, b = r[0], r[1], r[2]
+            ps = SCRATCH[name][0] == "psum"
+            for (x, y, pw, po) in seen.get(name, ()):
+                if po is not o and ((a < y and x < b and (wr or pw)) or (ps and (po["q"] != o["q"] or name in ("b4", "b5")))):
+                    dep.add(po["i"])
+        for r, wr in acc:
+            name, a, b = r[0], r[1], r[2]
+            keep = [e for e in seen.get(name, ()) if e[3] is o or not (wr and a <= e[0] and e[1] <= b)]
+            keep.append((a, b, wr, o))
+            seen[name] = keep
+        o["dep"] = sorted(dep)
+
+
+def schedule(ops):
+    N = len(ops)
+    succ = [[] for _ in range(N)]
+    need = [0] * N
+    for o in ops:
+        for d in o["dep"]:
+            succ[d].append((o["i"], OWN if ops[d]["q"] == o["q"] else WAKE))
+            need[o["i"]] += 1
+        if o.get("tdep"):
+            succ[o["tdep"][0]["i"]].append((o["i"], o["tdep"][1]))
+            need[o["i"]] += 1
+    pri = [0.0] * N
+    for i in range(N - 1, -1, -1):
+        pri[i] = ops[i]["cost"] + max([lat + pri[j] for j, lat in succ[i]] + [0.0])
+    pri = [x + o["pb"] for x, o in zip(pri, ops)]
+    est = [0.0] * N
+    ready = {}
+    for o in ops:
+        if not need[o["i"]]:
+            ready.setdefault(o["q"], []).append(o["i"])
+    free, busy, order = {}, {}, []
+    while len(order) < N:
+        best = None
+        for q, L in ready.items():
+            if L:
+                f = free.get(q, 0.0)
+                s = min(max(f, est[i]) for i in L)
+                if best is None or s < best[0]:
+                    best = (s, q)
+        s, q = best
+        f = free.get(q, 0.0)
+        i = max([i for i in ready[q] if max(f, est[i]) <= s + 1e-9], key=lambda k: (pri[k], -k))
+        ready[q].remove(i)
+        o = ops[i]
+        o["t0"] = s
+        end = s + o["cost"]
+        free[q] = s if o["kind"] == "arr" else (s + 0.05 if o["kind"] == "dma" else end)
+        busy[q] = busy.get(q, 0.0) + o["cost"]
+        order.append(i)
+        for j, lat in succ[i]:
+            est[j] = max(est[j], end + lat)
+            need[j] -= 1
+            if not need[j]:
+                ready.setdefault(ops[j]["q"], []).append(j)
+    return order, max(o["t0"] + o["cost"] for o in ops), busy
+
+
+def waits(ops, order):
+    cnt, know = {}, {}
+    for i in order:
+        o = ops[i]
+        q = o["q"]
+        kn = know.setdefault(q, {})
+        w = {}
+        for d in o["dep"]:
+            s, v = ops[d]["done"]
+            if kn.get(s, 0) < v and w.get(s, (0,))[0] < v:
+                w[s] = (v, d)
+        o["waits"] = []
+        for s in sorted(w, key=lambda k: -ops[w[k][1]]["t0"]):
+            v, d = w[s]
+            if kn.get(s, 0) >= v:
+                continue
+            o["waits"].append((s, v))
+            for a, z in ops[d]["snap"].items():
+                kn[a] = max(kn.get(a, 0), z)
+            kn[s] = max(kn.get(s, 0), v)
+        if o["kind"] in ("arr", "dma"):
+            o["done"] = (o["sem"], 16)
+        elif o["kind"] in ("send", "rsend"):
+            o["done"] = ("sent", 0)
+        else:
+            cnt[q] = cnt.get(q, 0) + 1
+            o["done"] = (q, cnt[q])
+        o["snap"] = dict(kn)
+    return cnt
+
+
+PLAN = {}
+
+
+def plan():
+    if not PLAN:
+        ops = make_plan()
+        link(ops)
+        order, total, busy = schedule(ops)
+        PLAN.update(ops=ops, order=order, cnt=waits(ops, order), total=total, busy=busy)
+    return PLAN
+
+
+def rank_program(g, core, T, topo):
+    rank = T.rank_of(core)
+    if rank is None:
+        return
+    pl = plan()
+    ops = pl["ops"]
+    N = len(T.cores)
+    queue = {"v": g.vector, "s": g.scalar, "p": g.tensor, "q": g, "y": g.sync}
+
+    def ap(r):
+        if not isref(r):
+            return r
+        if r[0] == "ind":
+            return ap(r[1]).indirect(ap(r[2]))
+        return T[r[0]][r[3]]
+
+    def side(r):
+        if r[0] == "T":
+            return T[r[1]][:, r[2]:r[3]] if len(r) > 2 else T[r[1]][:]
+        return ap(r)
+
+    nxt = T.cores[(rank + 3) % N]
+    sent = [0]
+    narr = {}
+    for t in range(1, ROUNDS):
+        for c in range(NC):
+            narr["a%d_%d" % (t, c)] = len(topo.engines(T.cores[(rank - 3) % N], core))
+    narr["ar"] = sum(len(topo.engines(T.cores[(rank - 3 * t) % N], core)) for t in range(1, ROUNDS))
+    for i in pl["order"]:
+        o = ops[i]
+        k, a = o["kind"], o["args"]
+        if k == "arr":
+            continue
+        Q = queue[o["q"]]
+        for s, v in o["waits"]:
+            Q.wait_ge(T.sem[s], narr.get(s, v))
+        if k == "ts":
+            r = Q.tensor_scalar(ap(a[0]), ap(a[1]), ap(a[2]), ap(a[3]), a[4]) if a[5] is None else \
+                Q.tensor_scalar(ap(a[0]), ap(a[1]), ap(a[2]), ap(a[3]), a[4], a[5])
+        elif k == "tt":
+            r = Q.tensor_tensor(ap(a[0]), ap(a[1]), ap(a[2]), a[3])
+        elif k == "cp":
+            r = Q.tensor_copy(ap(a[0]), ap(a[1]))
+        elif k == "ms":
+            r = Q.memset(ap(a[0]), a[1])
+        elif k == "red":
+            r = Q.tensor_reduce(ap(a[0]), ap(a[1]), AxisListType.X, A.add)
+        elif k == "act":
+            r = Q.activation(ap(a[0]), ap(a[1]), a[2], bias=ap(a[3]), scale=a[4], accum_out=ap(a[5]))
+        elif k == "mm":
+            for m in a:
+                r = Q.matmul(ap(m[0]), ap(m[1]), ap(m[2]), m[3], m[4])
+        elif k == "iota":
+            r = Q.iota(ap(a[0]), a[1], a[2], a[3], allow_small_or_imprecise_dtypes=True)
+        elif k == "sel":
+            r = Q.affine_select(ap(a[0]), ap(a[1]), a[2], a[3], a[4], a[5], a[6])
+        elif k == "dma":
+            Q.dma_start(side(a[0]), side(a[1])).then_inc(T.sem[o["sem"]], 16)
+            continue
+        elif k == "send":
+            rid, pid = topo.addr(nxt, core)
+            src = R("sd", 256 * a[0] + n * a[1], 256 * a[0] + n * a[1] + n)
+            dst = R("rf", 256 * (a[0] + 1) + n * a[1], 256 * (a[0] + 1) + n * a[1] + n)
+            Q.remote_dma(ap(dst), ap(src), T.sem["a%d_%d" % (a[0] + 1, a[1])], T.sem["sent"], pid, rid, topo.mask(core, nxt))
+            sent[0] += len(topo.engines(core, nxt))
+            continue
+        else:
+            ids, dsts = [], []
+            for t in range(1, ROUNDS):
+                d = T.cores[(rank + 3 * t) % N]
+                rid, pid = topo.addr(d, core)
+                ids.append(DstId(rid=rid, pnc=pid))
+                dsts.append(ap(R("rr", 16 * t, 16 * t + 16)))
+            Q.remote_dma_fused([RemoteDMATransfer(dst_ids=ids, dma_engine_mask=topo.mask(core, nxt), remote_sem=T.sem["ar"],
+                                                  srcs=[ap(R("rr", 0, 16))], dsts=dsts)], local_sem=T.sem["sent"])
+            sent[0] += len(topo.engines(core, nxt))
+            continue
+        r.then_inc(T.sem[o["q"]], 1)
+    for s in sorted(pl["cnt"]):
+        g.wait_ge(T.sem[s], pl["cnt"][s])
+    g.wait_ge(T.sem["sent"], sent[0])
+    for s in ("dr", "dx", "dc", "oy0", "oy1", "oc"):
+        g.sync.wait_ge(T.sem[s], 16)

@@ -1,60 +1,49 @@
 from concourse.bass import DstId, RemoteDMATransfer
 from concourse.mybir import dt, AluOpType as A, AxisListType, ActivationFunctionType as F
 
-NC = 4
-n = 256 // NC
-NL = n // 16
+NC = 2
+n = 128
 ROUNDS = 5
-CW = 1408
-MODE1 = "AMMM"
-MODE2 = "AMAM"
-HG = 2
+CW = 1152
+ABS1 = "VV"
+ABS2 = "SS"
+OPEN = False
 
+f16, b16, f32, i32, u16 = "float16", "bfloat16", "float32", "int32", "uint16"
 SCRATCH = {
-    "xw": ("sbuf", [128, 2560], "bfloat16"), "ri": ("sbuf", [128, 256], "int32"), "ci": ("sbuf", [128, 1024], "int32"),
-    "cc": ("sbuf", [128, CW], "float32"), "cy": ("sbuf", [128, CW], "float32"),
-    "rf": ("sbuf", [128, 256 * ROUNDS], "float16"), "sd": ("sbuf", [128, 256 * ROUNDS], "float16"),
-    "rl": ("sbuf", [128, 512], "uint16"), "rls": ("sbuf", [128, 512], "uint16"),
-    "rl2": ("sbuf", [128, 512], "uint16"), "rls2": ("sbuf", [128, 512], "uint16"),
-    "v1": ("sbuf", [128, 4096], "bfloat16"), "m1": ("sbuf", [128, 4096], "bfloat16"),
-    "v2": ("sbuf", [128, 4096], "bfloat16"), "m2": ("sbuf", [128, 4096], "bfloat16"), "ad": ("sbuf", [128, 2048], "bfloat16"),
-    "f": ("sbuf", [128, 512], "float16"), "q": ("sbuf", [128, 512], "float16"), "mk": ("sbuf", [128, 512], "float16"),
-    "rn": ("sbuf", [128, 512], "float16"), "cm": ("sbuf", [128, 512], "float16"), "r2": ("sbuf", [128, 512], "float16"),
-    "em": ("sbuf", [128, 4096], "float16"), "hd": ("sbuf", [128, 512], "float16"), "g1": ("sbuf", [128, 512], "float16"),
-    "qd": ("sbuf", [128, 512], "float16"), "eq": ("sbuf", [128, 512], "float16"), "ins": ("sbuf", [128, 512], "float16"),
-    "t3": ("sbuf", [128, 512], "float32"), "r3": ("sbuf", [128, 512], "float16"), "r3c": ("sbuf", [128, 512], "float32"),
-    "fs": ("sbuf", [128, 1024], "float16"), "fz": ("sbuf", [128, 1024], "float16"), "nr": ("sbuf", [128, 512], "float16"),
-    "t4": ("sbuf", [128, 512], "float32"), "q5": ("sbuf", [128, 512], "float16"), "k5": ("sbuf", [128, 512], "float16"),
-    "t5": ("sbuf", [128, 512], "float32"), "yo": ("sbuf", [128, 256], "float32"),
-    "rr": ("sbuf", [128, 16 * ROUNDS], "float32"), "q15": ("sbuf", [128, 256], "float16"),
-    "w": ("sbuf", [128, 32], "float32"), "hi": ("sbuf", [128, 32], "int32"), "hj": ("sbuf", [128, 32], "int32"),
-    "hl": ("sbuf", [128, 32], "uint16"), "nf": ("sbuf", [128, 32], "float32"), "hf": ("sbuf", [128, 32], "float16"),
-    "e3": ("sbuf", [128, 128], "float16"), "lo": ("sbuf", [128, 16], "float32"), "tj": ("sbuf", [128, 16], "float32"),
-    "tm": ("sbuf", [128, 16], "float32"), "ts": ("sbuf", [128, 16], "float32"), "off": ("sbuf", [128, 64], "uint16"),
-    "kc": ("sbuf", [128, ROUNDS], "float32"), "kj": ("sbuf", [128, 64], "float32"),
-    "col": ("sbuf", [128, 8], "float32"), "one": ("sbuf", [128, 128], "bfloat16"),
-    "B8": ("sbuf", [128, 1024], "bfloat16"), "UP": ("sbuf", [128, 1024], "bfloat16"), "UC": ("sbuf", [128, 1024], "bfloat16"),
-    "DD": ("sbuf", [128, 1024], "bfloat16"), "MM": ("sbuf", [128, 1024], "bfloat16"), "MH": ("sbuf", [128, 1024], "bfloat16"),
-    "W2": ("sbuf", [128, 2048], "bfloat16"), "NW": ("sbuf", [128, 2048], "bfloat16"),
+    "xw": ("sbuf", [128, 2560], b16), "ri": ("sbuf", [128, 256], i32), "ci": ("sbuf", [128, 1024], i32),
+    "cc": ("sbuf", [128, CW], f32), "cy": ("sbuf", [128, CW], f32), "rf": ("sbuf", [128, 256], f16),
+    "lst": ("sbuf", [128, 256 * ROUNDS], u16), "sd": ("sbuf", [128, 256 * ROUNDS], u16), "l2": ("sbuf", [128, 256], u16),
+    "em": ("sbuf", [128, 2048], b16), "yo": ("sbuf", [128, 256], f32), "sv": ("sbuf", [128, 256], f32),
+    "t3": ("sbuf", [128, 256], f32), "t4": ("sbuf", [128, 256], f32),
+    "rr": ("sbuf", [128, 16 * ROUNDS], f32), "w": ("sbuf", [128, 16], f32), "hi": ("sbuf", [128, 16], i32),
+    "hj": ("sbuf", [128, 16], i32), "hl": ("sbuf", [128, 16], u16), "hf": ("sbuf", [128, 16], f16),
+    "e3": ("sbuf", [128, 128], b16), "sk": ("sbuf", [128, 16], b16), "off": ("sbuf", [128, 32], u16),
+    "kc": ("sbuf", [128, ROUNDS], f32), "kj": ("sbuf", [128, 16], f32), "col": ("sbuf", [128, 8], f32),
+    "one": ("sbuf", [128, 256], b16), "Iz": ("sbuf", [128, 272], b16), "Q": ("sbuf", [128, 512], b16),
+    "Bw1": ("sbuf", [128, 256], b16), "Bw2": ("sbuf", [128, 192], b16), "P1": ("sbuf", [128, 192], b16),
+    "CC": ("sbuf", [128, 272], b16),
 }
-for _k in ("B", "B0", "I", "L", "SH", "SD", "LI", "UI", "US", "LP", "ZN", "ZA", "ZT", "IT", "IK", "I2", "I16", "NI", "NH", "YA",
-           "DS", "R15", "C2", "C19"):
-    SCRATCH[_k] = ("sbuf", [128, 128], "bfloat16")
+for _k in ("e1", "d1", "a1", "w1", "e2", "d2", "a2", "w2", "u2"):
+    SCRATCH[_k] = ("sbuf", [128, 2048], b16)
+for _k in ("reo", "q", "ym", "aa", "cm", "r2", "qd", "r3", "so", "sf"):
+    SCRATCH[_k] = ("sbuf", [128, 256], f16)
+for _k in ("f", "g3", "eq", "ow", "fz", "sg"):
+    SCRATCH[_k] = ("sbuf", [128, 256], b16)
+for _k in ("x1", "f2", "x2"):
+    SCRATCH[_k] = ("sbuf", [128, 272], b16)
+for _k in ("B8", "UP", "UW", "DD", "ML", "MH"):
+    SCRATCH[_k] = ("sbuf", [128, 1024], b16)
+for _k in ("B", "B0", "I", "NI", "LI", "UI", "SH", "SD", "I8k", "N16k", "T16", "M16", "R15", "HB", "HI", "NH", "NDS", "ND2", "D256",
+           "SD64", "DSh", "YAh", "Ie", "I16", "B2", "NB", "sg1", "sg2", "half"):
+    SCRATCH[_k] = ("sbuf", [128, 128], b16)
 for _k in range(8):
-    SCRATCH["b%d" % _k] = ("psum", [128, 512], "float32")
+    SCRATCH["b%d" % _k] = ("psum", [128, 512], f32)
 SEMAPHORES = ["v", "s", "p", "q", "sent", "ar", "dr", "dx", "dc", "oy0", "oy1", "oc"] + \
-    ["a%d_%d" % (t, c) for t in range(1, ROUNDS) for c in range(NC)]
-WIDE = set(k for k in SCRATCH if SCRATCH[k][2] in ("float32", "int32"))
+    ["%s%d_%d" % (k, t, c) for k in "eo" for t in range(1, ROUNDS) for c in range(NC)]
+WIDE = set(k for k in SCRATCH if SCRATCH[k][2] in (f32, i32))
 
-CY, PE, GA, WAKE, OWN, NET = 0.001, 0.0005, 1.6, 0.16, 0.06, 4.0
-TUNE = {
-    'rl': '4341', 'b3': '844484644438', 'rls': '48', 'v1': '87456300', 'm1': '5250527', 'b5': '454860575157', 'b2': '808444432',
-    'f': '23', 'q': '48', 'w': '56', 'hi': '43', 'hj': '56', 'hl': '52', 'nf': '45', 'mk': '72', 'rn': '43', 'cm': '46',
-    'rl2': '4818', 'r2': '8845', 'b1': '4814654663', 'b4': '34347541', 'b6': '4414843', 'b7': '1254548', 'b0': '76842336',
-    'em': '3321', 'rls2': '7', 'v2': '0200455', 'm2': '231700', 'ad': '112', 'hd': '443', 'qd': '7742', 'g1': '663', 'eq': '512',
-    'ins': '68', 't3': '8845', 'r3': '5682', 'fs': '4418', 'fz': '445', 'nr': '4481', 't4': '4608', 'sd': '4846', 'send': '867',
-    'r3c': '3432', 'q5': '341', 'k5': '0446', 't5': '846', 'e3': '5', 'lo': '3', 'cc': '5276642224604340', 'yo': '0447',
-    'dma': '226', 'cy': '36312546568454123'}
+EST = dict(CY=0.001, PE=0.0005, GA=1.6, SC=3.5, WAKE=0.16, OWN=0.06, NET=4.0, LEAD=4.0)
 
 
 def R(name, a, b, step=1):
@@ -74,11 +63,14 @@ def isref(x):
     return isinstance(x, tuple)
 
 
-def make_plan():
+def make_plan(est):
     ops = []
+    cur = [None]
+    CY, PE, GA, NET = est["CY"], est["PE"], est["GA"], est["NET"]
 
     def op(queue, kind, args, reads, writes, cost, **kw):
-        d = dict(i=len(ops), q=queue, kind=kind, args=args, r=[], w=list(writes), cost=cost, sem=None, pb=0)
+        d = dict(i=len(ops), q=queue, kind=kind, args=args, r=[], w=list(writes), cost=cost, sem=None, pb=est["LEAD"] * (cur[0] == 1),
+                 c=cur[0])
         for x in reads:
             if isref(x):
                 d["r"] += [x[1], x[2]] if x[0] == "ind" else [x]
@@ -89,38 +81,41 @@ def make_plan():
     def boost(x, o):
         o["pb"] = x
 
-    two = lambda r: r[0] not in WIDE and r[0][0] != "b"
+    two = lambda r: r[0] not in WIDE
 
     def ts(out, in0, s1, s2=None, op0=A.add, op1=None):
         c = max(64, size(in0) * (0.5 if two(out) and two(in0) else 1)) * CY
         return op("v", "ts", (out, in0, s1, s2, op0, op1), [in0, s1, s2], [out], c)
 
     def tt(out, in0, in1, o):
-        if out[0] == "ind":
-            return op("v", "tt", (out, in0, in1, o), [in0, in1, out[2]], [out[1]], 0.05 + size(in0) * 3 * CY)
         if in0[0] == "ind":
             c = 0.05 + size(in1) * GA * CY
         else:
             c = max(64, size(in0) * (1 if in0[0][0] == "b" or in1[0][0] == "b" else 2)) * CY
         return op("v", "tt", (out, in0, in1, o), [in0, in1], [out], c)
 
-    def cp(out, in_):
-        return op("v", "cp", (out, in_), [in_], [out], max(64, size(out)) * CY)
+    def scan(out, d0, d1, init, op0, op1):
+        c = max(64, size(out) * (0.5 if two(out) and two(d0) and two(d1) else 1)) * CY
+        return op("v", "scan", (out, d0, d1, init, op0, op1), [d0, d1], [out], c)
+
+    def scatter(win, off, in_):
+        return op("v", "cp", (ind(win, off), in_), [in_, off], [win], 0.05 + size(in_) * est["SC"] * CY)
 
     def ms(out, val):
         return op("v", "ms", (out, val), [], [out], max(64, size(out) * (.5 if two(out) else 1)) * CY)
 
     def act(out, in_, fn, bias=0.0, scale=1.0, acc=None):
         k = size(out)
-        return op("s", "act", (out, in_, fn, bias, scale, acc), [in_], [out] + ([acc] if acc else []),
-                  (0.065 + k * GA * CY) if in_[0] == "ind" else max(64, k) * CY)
+        return op("s", "act", (out, in_, fn, bias, scale, acc), [in_, bias], [out] + ([acc] if acc else []),
+                  (0.065 + k * GA * CY) if in_[0] == "ind" else max(64, k) * CY + (0.02 if acc else 0))
 
     def K(name):
         return R(name, 0, 128)
 
     def grp(out, *pairs):
         last = len(pairs) - 1
-        return [(out, K(a) if isinstance(a, str) else a, b, i == 0, i == last) for i, (a, b) in enumerate(pairs)]
+        kk = lambda a: K(a) if isinstance(a, str) else a
+        return [(p[2] if len(p) > 2 else out, kk(p[0]), kk(p[1]), i == 0, i == last) for i, p in enumerate(pairs)]
 
     def mm(*mms):
         rd = []
@@ -134,262 +129,303 @@ def make_plan():
     def dma(sem, out, in_, reads, writes, cost):
         return op("y", "dma", (out, in_), reads, writes, cost, sem=sem)
 
+    def scaled(out, in_, x):
+        return act(K(out), K(in_), F.Copy, scale=x)
+
     dma("dr", R("ri", 0, 256), ("T", "r0"), [], [R("ri", 0, 256)], 2.2)
     dma("dx", R("xw", 0, 2560), ("T", "x"), [], [R("xw", 0, 2560)], 5.0)
     dma("dc", R("ci", 0, 1024), ("T", "c0"), [R("xw", 0, 2560)], [R("ci", 0, 1024)], 4.5)
     IN = [[-16, 8], [-1, 16]]
-    boost(1000, ms(K("one"), 1.0))
-    sel(K("B0"), K("one"), [[-16, 8], [0, 16]], A.is_ge, 0.0, 0, 1)
-    sel(K("B"), K("B0"), [[16, 8], [0, 16]], A.is_ge, 0.0, 15, -1)
-    boost(200, sel(K("I"), K("B"), IN, A.is_equal, 0.0, 0, 1))
-    boost(100, sel(K("SH"), K("B"), IN, A.is_equal, 0.0, -1, 1))
-    ms(R("W2", 0, 2048), 0.0)
-    boost(90, sel(K("L"), K("B"), [[16, 8], [1, 16]], A.is_gt, 0.0, 0, -1))
+    boost(1000, ms(R("one", 0, 256), 1.0))
+    ms(R("Iz", 0, 16), 0.0)
+    boost(900, sel(R("Iz", 16, 272), R("one", 0, 256), [[-16, 8], [-200, 2], [-1, 16]], A.is_equal, 0.0, 0, 1))
+    boost(800, sel(K("I"), K("one"), [[-1, 128]], A.is_equal, 0.0, 0, 1))
+    boost(700, sel(K("B0"), K("one"), [[-16, 8], [0, 16]], A.is_ge, 0.0, 0, 1))
+    boost(600, sel(K("B"), K("B0"), [[16, 8], [0, 16]], A.is_ge, 0.0, 15, -1))
+    boost(500, sel(K("T16"), K("one"), [[0, 8], [-1, 16]], A.is_equal, 0.0, 0, 1))
+    for j in range(2):
+        sel(R("Q", 256 * j, 256 * j + 256), R("one", 0, 256), [[1, 2], [-32, 8], [-1, 16]], A.is_equal, 0.0, -16 * j, 2)
+    sel(K("SH"), K("B"), IN, A.is_equal, 0.0, -1, 1)
     sel(K("SD"), K("B"), IN, A.is_equal, 0.0, 1, 1)
-    for p in range(16):
-        a = 128 * p
-        ts(("W2", a, a + 128, (slice(None), slice(a + p, a + 128, 16))), R("B", 0, 128, 16), 2.0, None, A.mult)
-    act(K("NI"), K("I"), F.Copy, scale=-1.0)
-    act(K("NH"), K("I"), F.Copy, scale=-0.5)
-    for i in range(4):
-        a = 512 * i
-        o = R("b%d" % i, 0, 512)
-        if i:
-            mm(*grp(o, ("NH", R("W2", a, a + 512)), ("NH", R("W2", a - 128, a + 384))))
-        else:
-            mm(*(grp(R("b0", 0, 128), ("NH", R("W2", 0, 128))) +
-                 grp(R("b0", 128, 512), ("NH", R("W2", 128, 512)), ("NH", R("W2", 0, 384)))))
-        act(R("NW", a, a + 512), o, F.Copy)
-    for c in range(NC):
-        ts(R("rf", c * n, c * n + n), R("ri", c * n, c * n + n), -1280.0)
+    sel(K("LI"), K("B"), [[16, 8], [1, 16]], A.is_ge, 0.0, 0, -1)
+    sel(K("UI"), K("B"), IN, A.is_ge, 0.0, 0, 1)
+    op("q", "iota", (R("col", 4, 5), [[0, 1]], 1024, 1), [], [R("col", 4, 5)], 0.14)
+    PZ = lambda j, i: R("Iz", 16 - 16 * j + i, 272 - 16 * j, 2)
+    T1 = lambda nm, s: R(nm, 128 * s, 128 * s + 128)
+    BC = lambda nm: R(nm, 0, 128, 16)
+    C720, C32, C10 = R("CC", 0, 128), R("CC", 128, 256), R("CC", 256, 264)
+
+    def W(c, h):
+        return "b%d" % (4 * c + h)
+
+    def Lb(c, a, b, step=1):
+        return R("b%d" % (4 * c + 2), a, b, step)
+
+    def Sb(c, a, b, step=1):
+        return R("b%d" % (4 * c + 3), a, b, step)
+
+    def G(name, c):
+        return R(name, n * c, n * c + n)
+
+    def GP(name, c, shift):
+        return R(name, 136 * c + 8 - shift, 136 * c + 136 - shift)
+
+    def to_list(out, src, i):
+        return grp(out, *[(PZ(j, i), R(src[0], src[1] + j, src[2], 2)) for j in range(2)])
+
+    def lanes(c, bc):
+        tt(G("ym", c), bc, K("M16"), A.mult)
+        mm(*grp(Sb(c, 0, 8), (G("ym", c), BC("B")), ("one", C10)))
+
+    ts(R("rf", 0, 256), R("ri", 0, 256), -1280.0)
+    for c in range(NC - 1, -1, -1):
+        mm(*(to_list(Lb(c, 0, 64), G("rf", c), 0) + to_list(Lb(c, 64, 128), G("rf", c), 1)))
+        ts(G("lst", c), Lb(c, 0, 128), 1280.0)
+    scaled("NI", "I", -1.0)
+    ms(C720, 720.0)
+    ms(C32, -32.0)
+    ms(C10, 10.0)
+    mm(*grp(R("b0", 0, 128), ("T16", "T16")))
+    act(K("M16"), R("b0", 0, 128), F.Copy)
     op("v", "red", (R("col", 0, 1), R("I", 15, 128, 16)), [R("I", 15, 128, 16)], [R("col", 0, 1)], .07)
     op("v", "red", (R("col", 1, 2), R("I", 1, 128, 2)), [R("I", 1, 128, 2)], [R("col", 1, 2)], .07)
     tt(R("col", 2, 3), R("col", 1, 2), R("col", 0, 1), A.subtract)
-    ts(R("col", 3, 4), R("col", 2, 3), 3.5, -1.0, A.mult, A.add)
-    ts(R("q15", 0, 256), R("rf", 0, 256), R("col", 0, 1), None, A.mult)
-    mm(*grp(R("b4", 256, 272), *[(R("W2", 128 * j, 128 * j + 128), R("q15", j, 256, 16)) for j in range(16)]))
-    ts(R("rr", 0, 16), R("b4", 256, 272), 1.0 / 256, 10.5, A.mult, A.add)
+    ts(R("col", 3, 4), R("col", 2, 3), -99.5, 100.0, A.mult, A.add)
+    ts(K("R15"), K("B"), R("col", 0, 1), None, A.mult)
+    for c in range(NC):
+        mm(*grp(Sb(c, 384, 512), (G("rf", c), "R15")))
+        lanes(c, Sb(c, 384, 512))
+        ts(R("rr", 8 * c, 8 * c + 8), Sb(c, 0, 8), 1.0 / 64, 1.0, A.mult, A.add)
     op("q", "rsend", (), [R("rr", 0, 16)], [], 1.5)
     op("n", "arr", (), [], [R("rr", 16, 16 * ROUNDS)], 0.0, sem="ar", tdep=(ops[-1], NET))
-    act(K("ZT"), K("L"), F.Copy, scale=-16384.0)
-    act(K("ZA"), K("I"), F.Copy, scale=8192.0)
-    tt(K("ZA"), K("ZA"), K("ZT"), A.add)
-    act(K("LP"), K("L"), F.Copy)
-    act(R("LP", 15, 128, 16), R("I", 15, 128, 16), F.Copy, scale=0.0)
-    act(K("ZN"), K("LP"), F.Copy, scale=-8192.0)
-    act(K("IT"), K("I"), F.Copy)
-    act(R("IT", 15, 128, 16), R("I", 15, 128, 16), F.Copy, scale=0.0)
-    act(K("IK"), K("IT"), F.Copy, scale=1280.0)
-    ms(K("C2"), 320.0)
-    ms(("C2", 0, 128, (slice(0, 1), slice(0, 128))), 318.0)
-    ms(K("C19"), 150.0)
-    ms(("C19", 0, 128, (slice(0, 1), slice(0, 128))), 149.0)
+    scaled("B2", "B", 2.0)
+    scaled("NB", "B", -1.0)
+    ms(R("Bw1", 0, 256), 0.0)
+    ts(R("Bw1", 0, 128, 16), BC("B"), 1.0, None, A.mult)
+    ts(R("Bw1", 128, 256, 16), BC("B"), 2.0, None, A.mult)
+    ms(R("Bw2", 0, 192), 0.0)
+    ts(R("Bw2", 128, 192, 8), BC("B"), 1.0, None, A.mult)
+    scaled("I8k", "I", 8192.0)
+    scaled("N16k", "I", -16384.0)
+    ms(K("sg1"), 1.0)
+    ms(K("sg2"), 0.0)
+    for p in (14, 15):
+        ms(R("sg1", p, 128, 16), 0.0)
+        ms(R("sg2", p, 128, 16), -4096.0)
+    ms(R("x1", 0, 272), 0.0)
+    ms(R("f2", 0, 272), 0.0)
+    ms(R("x2", 0, 272), -4096.0)
+    ms(R("fz", 0, 256), 0.0)
     ms(R("kc", 0, 1), -0.4921875)
-    ts(R("cc", 0, 1024), R("ci", 0, 1024), -1280.0)
+    ms(K("half"), 0.5)
+    act(R("cc", 0, 1024), R("ci", 0, 1024), F.Identity, bias=-1280.0)
     ms(R("cc", 1024, CW), 0.0)
     ms(R("cy", 1024, CW), 0.0)
     for h in range(8):
-        ts(R("B8", 128 * h, 128 * h + 128), K("B"), 1.0, None, A.mult)
-    sel(R("UP", 0, 1024), R("B8", 0, 1024), [[-1, 8], [-16, 8], [-1, 16]], A.is_equal, 0.0, -1, 1)
-    sel(R("UC", 0, 1024), R("B8", 0, 1024), [[1, 8], [-16, 8], [-1, 16]], A.is_equal, 0.0, -15, 1)
-    T1 = lambda nm, s: R(nm, 128 * s, 128 * s + 128)
-    for h in range(2):
-        o = "b%d" % (6 + h)
-        mm(*sum([grp(T1(o, i), ("I", T1("UP", 4 * h + i)), (T1("UC", 4 * h + i), K("I")), ("NI", K("I"))) for i in range(4)], []))
-        act(R("DD", 512 * h, 512 * h + 512), R(o, 0, 512), F.Copy)
-    for h in range(2):
-        o = "b%d" % (6 + h)
-        mm(*sum([grp(T1(o, i), (T1("UP", 4 * h + i), T1("UP", 4 * h + i)), ("I", T1("UC", 4 * h + i))) for i in range(4)], []))
-        act(R("MM", 512 * h, 512 * h + 512), R(o, 0, 512), F.Copy)
-    for h in range(2):
-        o = "b%d" % (6 + h)
-        mm(*sum([grp(T1(o, i), (T1("UP", 4 * h + i), K("I")), ("I", T1("UC", 4 * h + i)), ("I", K("I")), ("NI", T1("MM", 4 * h + i)))
-                 for i in range(4)], []))
-        act(R("MH", 512 * h, 512 * h + 512), R(o, 0, 512), F.Copy)
-    tt(K("LI"), K("L"), K("I"), A.add)
-    tt(K("UI"), K("B"), K("L"), A.subtract)
-    tt(K("US"), K("B"), K("LI"), A.subtract)
-    act(K("I2"), K("I"), F.Copy, scale=2.0)
-    act(K("I16"), K("I"), F.Copy, scale=16.0)
-    tt(K("YA"), K("I"), K("SD"), A.add)
-    tt(K("DS"), K("SD"), K("I"), A.subtract)
-    ts(K("R15"), K("one"), R("col", 0, 1), None, A.mult)
-    op("q", "iota", (R("tj", 0, 16), [[16, 16]], 1024, 1), [K("SH")], [R("tj", 0, 16)], 0.17)
+        ts(T1("B8", h), K("B"), 1.0, None, A.mult)
+    P3 = [[-1, 8], [-16, 8], [-1, 16]]
+    sel(R("UP", 0, 1024), R("B8", 0, 1024), P3, A.is_equal, 0.0, -1, 1)
+    sel(R("UW", 0, 1024), R("B8", 0, 1024), P3, A.is_equal, 0.0, 15, 1)
+    for nm, x, terms in (
+            ("DD", 1.0, lambda s: (("I", T1("UP", s)), ("I", T1("UW", s)), ("NI", "I"))),
+            ("ML", 1.0, lambda s: (("I", "LI"), (T1("UW", s), "LI"))),
+            ("MH", 2048.0, lambda s: ((T1("UP", s), "I"), (T1("UW", s), T1("UW", s))))):
+        for h in range(2):
+            mm(*sum([grp(T1(W(0, h), i), *terms(4 * h + i)) for i in range(4)], []))
+            act(R(nm, 512 * h, 512 * h + 512), R(W(0, h), 0, 512), F.Copy, scale=x)
+    scaled("HB", "B", 0.5)
+    scaled("HI", "I", 0.5)
+    scaled("NH", "I", -0.5)
+    tt(K("NDS"), K("I"), K("SD"), A.subtract)
+    tt(K("YAh"), K("I"), K("SD"), A.add)
+    scaled("YAh", "YAh", 0.5)
+    scaled("ND2", "NDS", 2.0)
+    scaled("D256", "NDS", -256.0)
+    scaled("DSh", "NDS", -0.5)
+    scaled("SD64", "SD", 64.0)
+    scaled("Ie", "I", 1.0 / 4096)
+    scaled("I16", "I", 16.0)
+    scaled("P1", "SH", -128.0)
+    act(R("P1", 128, 192), R("I", 1, 128, 2), F.Copy, scale=-128.0)
 
     X = R("xw", 0, 2560)
     sends = {}
-    starts = []
+
+    def gathers(c, lst, e, d, a, w, u, eng):
+        v0 = 1024 * c
+        pc = lambda nm, h, k=512, s=0: R(nm, v0 + 512 * h + s, v0 + 512 * h + s + k)
+        rest = []
+        for h in range(2):
+            act(pc(e, h), ind(X, R(lst[0], lst[1] + 32 * h, lst[1] + 32 * h + 32)), F.Copy)
+            o = grp(R(W(c, h), 0, 511), ("I", pc(e, h, 511, 1)), ("NI", pc(e, h, 511)), ("NI", pc(d, h, 511)))
+            if u and not OPEN:
+                mm(*grp(R(W(c, h), 0, 511), ("I", pc(e, h, 511, 1)), ("NI", pc(e, h, 511))))
+                rest.append(o)
+            else:
+                mm(o[0], o[1][:4] + (bool(u),))
+                rest.append(o[2:])
+            if u:
+                act(pc(u, h, 511), R(W(c, h), 0, 511), F.Abs)
+        for h in range(2):
+            tt(pc(d, h), ind(X, R(lst[0], lst[1] + 64 + 32 * h, lst[1] + 96 + 32 * h)), pc(e, h), A.subtract)
+            mm(*rest[h])
+            act(pc(w, h, 511), R(W(c, h), 0, 511), F.Abs)
+            if eng == "S":
+                act(pc(a, h), pc(d, h), F.Abs)
+            else:
+                ts(pc(a, h), pc(d, h), 0.0, None, A.max)
+
+    def sums(c, src, ms_, col, step, mat="B"):
+        return [(R(src, 1024 * c + m, 1024 * c + 1024, 8), BC(mat), Sb(c, col(m), col(m) + 8 * step - step + 1, step)) for m in ms_]
+
     for t in range(ROUNDS):
-        starts.append(len(ops))
-        P2 = 256 * (t % 2)
         last = t == ROUNDS - 1
-
-        def G(name, c, k=n):
-            a = (P2 // 64) * (k * NC // 4) + k * c
-            return R(name, a, a + k)
-
-        def b(c, i, k=n):
-            return R("b%d" % c, 64 * i, 64 * i + k)
-
-        def distances(c, rin, rl, rls, vb, mb, out, mode):
-            v0 = 1024 * c
-            if mode == "M":
-                mm(*grp(b(c, 0), ("SH", rin)))
-                ts(rls, b(c, 0), 1280.0)
-            for h in range(HG):
-                w = 1024 // HG
-                vh, u, z = R(vb, v0 + w * h, v0 + w * h + w), n // HG * h, n // HG * h + n // HG
-                act(vh, ind(X, R(rl[0], rl[1] + u, rl[1] + z)), F.Copy)
-                if mode == "M":
-                    tt(R(mb, v0 + w * h, v0 + w * h + w), ind(X, R(rls[0], rls[1] + u, rls[1] + z)), vh, A.max)
-            red = [(T1("W2", p), R(mb, v0 + p, v0 + 1024, 16)) for p in range(15)]
-            if mode == "M":
-                o = grp(out, *([(T1("NW", p), R(vb, v0 + p, v0 + 1024, 16)) for p in range(16)] + red))
-                mm(*o[:16])
-                return o[16:]
-            for h in range(2):
-                e = "b%d" % (6 + (c + h) % 2)
-                a = v0 + 512 * h
-                mm(*grp(R(e, 0, 511), ("I", R(vb, a + 1, a + 512)), ("NI", R(vb, a, a + 511))))
-                act(R(mb, a, a + 511), R(e, 0, 511), F.Abs, scale=0.5)
-            return grp(out, *red)
-
         for c in range(NC - 1, -1, -1):
-            rin = R("rf", 256 * t + n * c, 256 * t + n * c + n)
+            cur[0] = c
+            l0 = 256 * t + n * c
             if t:
-                op("n", "arr", (), [], [rin], 0.0, sem="a%d_%d" % (t, c), tdep=(sends[t - 1, c], NET))
-            ts(G("rl", c), rin, 1280.0)
-            D = R("b%d" % (4 + c // 2), n * (c % 2), n * (c % 2) + n)
-            mm(*distances(c, rin, G("rl", c), G("rls", c), "v1", "m1", D, MODE1[c]))
-            if c % 2:
-                continue
-            m, d = 2 * n, c // 2
-            rin = R("rf", 256 * t + m * d, 256 * t + m * d + m)
-            g2 = lambda nm: R(nm, P2 + m * d, P2 + m * d + m)
-            l2 = lambda nm: R(nm, 16 * (t % 2) + 2 * NL * d, 16 * (t % 2) + 2 * NL * d + 2 * NL)
-            e = "b%d" % (c + 1)
-            Z1, Z2, Y2 = R(e, 128, 256), R(e, 384, 512), R(e, 0, 2 * NL)
-            ts(g2("f"), R("b%d" % (4 + d), 0, m), 34.5, None, A.is_gt)
-            mm(*(grp(Z1, ("I", rin), ("ZA", g2("f"))) + grp(Z2, ("I", rin), ("ZN", g2("f")))))
-            ts(g2("q"), Z1, 6911.0, -8191.0, A.max, A.add)
-            q0 = g2("q")[1]
-            mm(*grp(Y2, ("C2", R("one", 0, 2 * NL)), *[(T1("W2", j), R("q", q0 + j, q0 + m, 16)) for j in range(16)]))
-            tt(l2("w"), Y2, R("rr", 16 * t + 2 * NL * d, 16 * t + 2 * NL * d + 2 * NL), A.mult)
-            ts(l2("hi"), l2("w"), R("kc", t, t + 1))
-            ts(l2("hj"), l2("hi"), 1023, None, A.bitwise_and)
-            cp(l2("hl"), l2("hj"))
-            ts(l2("nf"), Y2, -1.0, -4096.0, A.is_lt, A.mult)
-            ts(g2("mk"), Z1, -1280.5, None, A.is_lt)
-            ts(g2("rn"), Z2, -1280.0, None, A.max)
-            tt(g2("cm"), ind(R("cc", 0, 1024), l2("hl")), g2("mk"), A.mult)
-            for i in (c + 1, c):
-                mm(*grp(b(i, 4), ("I", G("rn", i)), ("IK", G("mk", i)), ("IT", G("cm", i))))
-                ts(G("rl2", i), b(i, 4), 1280.0)
-                ts(G("r2", i), b(i, 4), 0.0)
+                op("n", "arr", (), [], [R("lst", l0, l0 + 64)], 0.0, sem="e%d_%d" % (t, c), tdep=(sends[t - 1, c, 0], NET))
+                op("n", "arr", (), [], [R("lst", l0 + 64, l0 + 128)], 0.0, sem="o%d_%d" % (t, c), tdep=(sends[t - 1, c, 1], NET))
+            gathers(c, R("lst", l0, l0 + n), "e1", "d1", "a1", "w1", None, ABS1[c])
+            ts(G("reo", c), R("lst", l0, l0 + n), -1280.0)
+            ev = lambda m: 2 * m
+            od = lambda m: 2 * m + 1
+            if ABS1[c] == "S":
+                s0 = [(R("a1", 1024 * c, 1024 * c + 1024, 8), R("Bw1", 0, 128))] + sums(c, "a1", range(1, 8), ev, 16)
+            else:
+                s0 = [(R("a1", 1024 * c, 1024 * c + 1024, 8), R("Bw1", 128, 256))] + sums(c, "a1", range(1, 8), ev, 16, "B2") + \
+                    sums(c, "d1", range(8), ev, 16, "NB")
+            o = grp(Sb(c, 0, 128), *(s0 + sums(c, "w1", range(7), od, 16)))
+            mm(*o[:len(s0)])
+            mm(*o[len(s0):])
+            ts(G("f", c), Sb(c, 0, 128), 34.5, None, A.is_gt)
+            scan(GP("x1", c, 0), G("f", c), K("sg1"), 0.0, A.max, A.mult)
+            back = lambda a: [(T1("Q", 2 * j + i), R("reo", n * c + 64 * i, n * c + 64 * i + 64), Sb(c, a + j, a + 128, 2))
+                              for j in range(2) for i in range(2)]
+            mm(*grp(Sb(c, 128, 256), (GP("x1", c, 1), "N16k"), (G("f", c), "I8k"), *back(128)))
+            ts(G("q", c), Sb(c, 128, 256), 2048.0, -8192.0, A.max, A.add)
+            mm(*grp(Sb(c, 384, 512), ("one", C720), (G("q", c), "B")))
+            lanes(c, Sb(c, 384, 512))
+            l8 = lambda nm: R(nm, 8 * c, 8 * c + 8)
+            tt(l8("w"), Sb(c, 0, 8), R("rr", 16 * t + 8 * c, 16 * t + 8 * c + 8), A.mult)
+            mm(*grp(Lb(c, 256, 384), (GP("x1", c, 1), "I8k"), *[(a, b, Lb(c, o[1], o[2], 2)) for a, b, o in back(256)]))
+            act(G("aa", c), Lb(c, 256, 384), F.Identity, bias=4096.0, scale=-1.0)
+            ts(l8("hi"), l8("w"), R("kc", t, t + 1))
+            ts(l8("hj"), l8("hi"), 1023 + 2 ** 23, None, A.bitwise_and)
+            ts(l8("hl"), l8("hj"), 1023.0, None, A.min)
+            tt(G("cm", c), ind(R("cc", 0, 1024), l8("hl")), G("aa", c), A.max)
+            tt(G("r2", c), Lb(c, 256, 384), G("cm", c), A.min)
+            for i in range(2):
+                mm(*to_list(Sb(c, 128 + 64 * i, 192 + 64 * i), G("r2", c), i))
+            for i in range(2):
+                ts(R("l2", n * c + 64 * i, n * c + 64 * i + 64), Sb(c, 128 + 64 * i, 192 + 64 * i), 1280.0)
+        H = lambda nm: R(nm, 0, 16)
+        ts(H("hf"), H("hj"), 2048.0, None, A.min)
+        mm(*sum([grp(Sb(0, 384 + 16 * s, 400 + 16 * s), (T1("DD", s), H("hf"))) for s in range(8)], []))
+        ts(K("e3"), Sb(0, 384, 512), 0.0, None, A.is_equal)
+        mm(*grp(Sb(0, 0, 16), ("I", H("hf")), *[(T1("MH", s), R("e3", 16 * s, 16 * s + 16)) for s in range(8)]))
+        ts(R("off", 0, 32, 2), Sb(0, 0, 16), R("col", 4, 5), None, A.min)
+        if not last:
+            act(H("sk"), H("hf"), F.Sign, bias=1500.0, scale=-1.0)
+            mm(*grp(Sb(0, 16, 32), ("half", H("sk"))))
+            act(H("kj"), Sb(0, 16, 32), F.Identity, bias=1023.5078125 / 16, acc=R("kc", t + 1, t + 2))
+        else:
+            act(R("cy", 0, 1024), R("cc", 0, 1024), F.Identity, bias=1280.0)
         for c in range(NC - 1, -1, -1):
-            e = "b%d" % (6 + c % 2)
-            mm(*sum([grp(R(e, n * s, n * s + n), (T1("DD", s), G("r2", c))) for s in range(8)], []))
-            em = R("em", 2048 * (t % 2) + 512 * c, 2048 * (t % 2) + 512 * c + 512)
-            ts(em, R(e, 0, 512), 0.0, None, A.is_equal)
-            D = "b%d" % (4 + c % 2)
-            D1 = distances(c, G("r2", c), G("rl2", c), G("rls2", c), "v2", "m2", R(D, 128, 128 + n), MODE2[c])
-            v0 = 1024 * c
-            mm(*grp(R(e, 0, 511), ("I", R("v2", v0 + 2, v0 + 1024, 2)), ("NI", R("v2", v0, v0 + 1022, 2))))
-            act(R("ad", 512 * c, 512 * c + 511), R(e, 0, 511), F.Abs, scale=0.5)
-            mm(*grp(b(c, 5), *[(T1("MM", s), R("em", em[1] + n * s, em[1] + n * s + n)) for s in range(8)]))
-            ts(G("hd", c), b(c, 5), 1.0, None, A.is_ge)
-            mm(*grp(b(c, 6), ("I", G("r2", c)), ("ZA", G("hd", c))))
-            ts(G("qd", c), b(c, 6), 6911.0, -8191.0, A.max, A.add)
-            ts(G("g1", c), b(c, 6), 4000.0, 64.0, A.is_gt, A.mult)
-            mm(*grp(b(c, 0), ("C19", R("one", 0, n)), ("NI", G("r2", c)), ("B", G("qd", c))))
-            ts(G("eq", c), b(c, 0), 0.0, None, A.is_equal)
-            mm(*(grp(b(c, 1), ("LI", G("g1", c)), ("US", G("eq", c))) + grp(b(c, 2), ("LI", G("g1", c)), ("UI", G("eq", c)))))
-            ts(G("ins", c), b(c, 2), 64.5, None, A.is_gt)
-            tt(G("t3", c), b(c, 0), G("ins", c), A.mult)
-            tt(G("r3", c), b(c, 4), G("t3", c), A.add)
-            mm(*D1)
-            mm(*grp(R(D, 192, 192 + n), *[(T1("W2", p + 1), R("ad", 512 * c + p // 2, 512 * c + 512, 8)) for p in range(0, 13, 2)]))
-            fs, fz = G("fs", c, 2 * n), G("fz", c, 2 * n)
-            ts(fs, R(D, 128, 128 + 2 * n), 34.5, 64.5, A.is_gt, A.mult)
-            tt(fz, fs, R("b%d" % c, 64, 64 + 2 * n), A.is_gt)
-            f2, F2 = R("fz", fz[1], fz[1] + n), R("fz", fz[1] + n, fz[1] + 2 * n)
-            mm(*(grp(b(c, 5), ("I2", G("ins", c)), ("YA", f2), ("I16", F2)) + grp(b(c, 6), ("DS", G("r3", c)))))
-            ts(G("nr", c), b(c, 5), R("col", 3, 4), None, A.is_lt)
-            tt(G("t4", c), b(c, 6), G("nr", c), A.mult)
+            cur[0] = c
+            for h in range(2):
+                e = W(c, 1) if h else "b%d" % (4 * c + 2)
+                mm(*sum([grp(T1(e, s), (T1("DD", 4 * h + s), G("r2", c))) for s in range(4)], []))
+                ts(R("em", 1024 * c + 512 * h, 1024 * c + 512 * h + 512), R(e, 0, 512), 0.0, None, A.is_equal)
+            gathers(c, G("l2", c), "e2", "d2", "a2", "w2", "u2", ABS2[c])
+            mm(*grp(Lb(c, 0, 128), *[(T1("ML", s), T1("em", 8 * c + s)) for s in range(8)]))
+            act(G("g3", c), Lb(c, 0, 128), F.Sign)
+            mm(*grp(Lb(c, 128, 256), ("NDS", G("g3", c))))
+            tt(G("qd", c), Lb(c, 128, 256), G("r2", c), A.mult)
+            mm(*(grp(Lb(c, 256, 384), ("HB", G("qd", c)), ("NH", G("r2", c))) +
+                 grp(Lb(c, 384, 512), ("HB", G("qd", c)), ("HI", G("r2", c)))))
+            ts(G("eq", c), Lb(c, 256, 384), 0.0, None, A.is_equal)
+            mm(*grp(Lb(c, 0, 128), ("UI", G("eq", c)), ("SD64", G("g3", c))))
+            act(G("ow", c), Lb(c, 0, 128), F.Sign, bias=-64.5)
+            tt(G("t3", c), Lb(c, 256, 384), G("ow", c), A.mult)
+            tt(G("r3", c), Lb(c, 384, 512), G("t3", c), A.add)
+            s0 = 256 * t + n * c
             if not last:
-                so = R("sd", 256 * t + n * c, 256 * t + n * c + n)
-                tt(so, G("r3", c), G("t4", c), A.add)
-                sends[t, c] = op("q", "send", (t, c), [so], [], 1.0)
-            act(G("r3c", c), G("r3", c), F.Identity if last else F.Copy, bias=1280.0 if last else 0.0)
-            if last:
-                tt(R("yo", n * c, n * c + n), G("r3c", c), G("t4", c), A.add)
-                if c % 2 == 0:
-                    x = n * c
-                    dma("oy%d" % (c // 2), ("T", "yr", x, x + 2 * n), R("yo", x, x + 2 * n), [R("yo", x, x + 2 * n)], [], 2.0)
-            mm(*(grp(b(c, 7), ("I", G("r3", c)), ("ZA", f2)) + grp(b(c, 3), ("LP", f2))))
-            ts(G("q5", c), b(c, 7), 6911.0, -8191.0, A.max, A.add)
-            act(G("k5", c), b(c, 3), F.Sign)
-            mm(*grp(b(c, 0), ("C19", R("one", 0, n)), ("NI", G("r3", c)), ("B", G("q5", c))))
-            tt(G("t5", c), b(c, 0), G("k5", c), A.mult)
-            if c == 2:
-                if not last:
-                    mm(*grp(R("b5", 320, 384), *[("R15", G("mk", i)) for i in range(NC)]))
-                    act(R("kj", 0, 64), R("b5", 320, 384), F.Identity, bias=-0.4921875 / 64, acc=R("kc", t + 1, t + 2))
-                x = 16 * (t % 2)
-                H = lambda nm: R(nm, x, x + 16)
-                tt(H("hf"), H("hj"), H("nf"), A.add)
-                mm(*sum([grp(R("b4", 256 + 16 * e, 272 + 16 * e), (T1("DD", e), H("hf"))) for e in range(8)], []))
-                ts(R("e3", 0, 128), R("b4", 256, 384), 0.0, None, A.is_equal)
-                mm(*grp(R("b5", 256, 272), *[(T1("MH", e), R("e3", 16 * e, 16 * e + 16)) for e in range(8)]))
-                tt(R("lo", 0, 16), R("b5", 256, 272), H("nf"), A.is_gt)
-                tt(R("tm", 0, 16), R("lo", 0, 16), R("tj", 0, 16), A.mult)
-                tt(R("ts", 0, 16), H("hj"), R("tm", 0, 16), A.max)
-                cp(R("off", 2 * x, 2 * x + 32, 2), R("ts", 0, 16))
-                if last:
-                    act(R("cy", 0, 1024), R("cc", 0, 1024), F.Identity, bias=1280.0)
-        for j in range(15, -1, -1):
-            a = P2 + 16 * j
-            tt(ind(R("cy" if last else "cc", 0, CW), R("off", 32 * (t % 2) + 2 * j, 32 * (t % 2) + 2 * j + 1)),
-               R("t5", a, a + 16), R("r3c", a, a + 16), A.add)
+                mm(*to_list(Lb(c, 0, 64), G("r3", c), 0))
+                ts(R("sd", s0, s0 + 64), Lb(c, 0, 64), 1280.0)
+                sends[t, c, 0] = op("q", "send", (t, c, 0), [R("sd", s0, s0 + 64)], [], 1.0)
+            mm(*(grp(Lb(c, 128, 256), ("DSh", G("r3", c))) + grp(Lb(c, 256, 384), ("YAh", G("r3", c)))))
+            parts = [[(R("u2", 1024 * c, 1024 * c + 1024, 8), R("Bw2", 0, 192))] + sums(c, "u2", range(1, 7), lambda m: 128 + m, 8),
+                     sums(c, "a2", range(7), ev, 16) if ABS2[c] == "S" else
+                     sums(c, "a2", range(7), ev, 16, "B2") + sums(c, "d2", range(7), ev, 16, "NB"),
+                     [(G("ow", c), R("P1", 0, 192)), (G("g3", c), R("D256", 1, 128, 2), Sb(c, 128, 192))],
+                     sums(c, "w2", range(7), od, 16)]
+            o = grp(Sb(c, 0, 192), *sum(parts, []))
+            for p in parts:
+                mm(*o[:len(p)])
+                o = o[len(p):]
+            ts(GP("f2", c, 0), Sb(c, 0, 128), 162.5, -4096.0, A.is_le, A.mult)
+            ts(R("fz", n * c + 1, n * c + n, 2), Sb(c, 128, 192), 162.5, None, A.is_gt)
+            mm(*grp(Sb(c, 192, 320), ("I", G("ow", c)), ("ND2", G("g3", c)), (GP("f2", c, 1), "Ie"), (GP("f2", c, 0), "Ie"),
+                    (G("fz", c), "I16")))
+            act(G("sg", c), Sb(c, 192, 320), F.Sign, bias=R("col", 3, 4))
+            tt(G("t4", c), Lb(c, 128, 256), G("sg", c), A.mult)
+            tt(G("so", c), Lb(c, 256, 384), G("t4", c), A.subtract)
+            if not last:
+                mm(*to_list(Sb(c, 320, 384), G("so", c), 1))
+                ts(R("sd", s0 + 64, s0 + 128), Sb(c, 320, 384), 1280.0)
+                sends[t, c, 1] = op("q", "send", (t, c, 1), [R("sd", s0 + 64, s0 + 128)], [], 1.0)
+            else:
+                act(G("yo", c), G("so", c), F.Identity, bias=1280.0)
+                dma("oy%d" % c, ("T", "yr", n * c, n * c + n), G("yo", c), [G("yo", c)], [], 2.0)
+            scan(GP("x2", c, 0), GP("f2", c, 0), K("sg2"), -4096.0, A.max, A.min)
+            mm(*grp(Lb(c, 384, 512), (G("r3", c), "I"), ("one", C32), ("NI", GP("x2", c, 1))))
+            scan(G("sf", c), GP("x2", c, 1), Lb(c, 384, 512), 0.0, A.add, A.max)
+            mm(*grp(Lb(c, 0, 128), (G("sf", c), "I")))
+            act(G("sv", c), Lb(c, 0, 128), F.Identity, bias=1280.0 if last else 0.0)
+            for j in range(8 * c + 7, 8 * c - 1, -1):
+                scatter(R("cy" if last else "cc", 0, CW), R("off", 2 * j, 2 * j + 1), R("sv", 16 * j, 16 * j + 16))
     dma("oc", ("T", "yc", 0, 1024), R("cy", 0, 1024), [R("cy", 0, 1024)], [], 4.0)
-    for t in range(ROUNDS):
-        cnt = {}
-        for o in ops[starts[t]:(starts + [len(ops)])[t + 1]]:
-            if o["kind"] != "arr":
-                nm = o["w"][0][0] if o["w"] else o["kind"]
-                k = cnt.get(nm, 0)
-                cnt[nm] = k + 1
-                s = TUNE.get(nm, "")
-                o["pb"] += int(s[k]) - 4 if k < len(s) else 0
     return ops
 
 
 def link(ops):
     seen = {}
     for o in ops:
-        dep = set()
+        dep, keep_order = set(), set()
         acc = [(r, False) for r in o["r"]] + [(w, True) for w in o["w"]]
         for r, wr in acc:
             name, a, b = r[0], r[1], r[2]
             ps = SCRATCH[name][0] == "psum"
             for (x, y, pw, po) in seen.get(name, ()):
-                if po is not o and ((a < y and x < b and (wr or pw)) or (ps and (po["q"] != o["q"] or name in ("b4", "b5")))):
+                if po is o:
+                    continue
+                if ps and po["q"] == o["q"] == "p":
+                    keep_order.add(po["i"])
+                elif (a < y and x < b and (wr or pw)) or (ps and po["q"] != o["q"]):
                     dep.add(po["i"])
         for r, wr in acc:
             name, a, b = r[0], r[1], r[2]
-            keep = [e for e in seen.get(name, ()) if e[3] is o or not (wr and a <= e[0] and e[1] <= b)]
+            full = wr and (len(r) < 4 or r[3][-1].step == 1) and SCRATCH[name][0] != "psum"
+            keep = [e for e in seen.get(name, ()) if e[3] is o or not (full and a <= e[0] and e[1] <= b)]
+            if SCRATCH[name][0] == "psum":
+                keep = keep[-12:]
             keep.append((a, b, wr, o))
             seen[name] = keep
         o["dep"] = sorted(dep)
+        o["ord"] = sorted(keep_order)
 
 
-def schedule(ops):
+def schedule(ops, est):
     N = len(ops)
     succ = [[] for _ in range(N)]
     need = [0] * N
     for o in ops:
         for d in o["dep"]:
-            succ[d].append((o["i"], OWN if ops[d]["q"] == o["q"] else WAKE))
+            succ[d].append((o["i"], est["OWN"] if ops[d]["q"] == o["q"] else est["WAKE"]))
+            need[o["i"]] += 1
+        for d in o["ord"]:
+            succ[d].append((o["i"], 0.0))
             need[o["i"]] += 1
         if o.get("tdep"):
             succ[o["tdep"][0]["i"]].append((o["i"], o["tdep"][1]))
@@ -398,7 +434,7 @@ def schedule(ops):
     for i in range(N - 1, -1, -1):
         pri[i] = ops[i]["cost"] + max([lat + pri[j] for j, lat in succ[i]] + [0.0])
     pri = [x + o["pb"] for x, o in zip(pri, ops)]
-    est = [0.0] * N
+    start = [0.0] * N
     ready = {}
     for o in ops:
         if not need[o["i"]]:
@@ -408,13 +444,11 @@ def schedule(ops):
         best = None
         for q, L in ready.items():
             if L:
-                f = free.get(q, 0.0)
-                s = min(max(f, est[i]) for i in L)
+                s = max(free.get(q, 0.0), min(start[i] for i in L))
                 if best is None or s < best[0]:
                     best = (s, q)
         s, q = best
-        f = free.get(q, 0.0)
-        i = max([i for i in ready[q] if max(f, est[i]) <= s + 1e-9], key=lambda k: (pri[k], -k))
+        i = max([i for i in ready[q] if start[i] <= s + 1e-9], key=lambda k: (pri[k], -k))
         ready[q].remove(i)
         o = ops[i]
         o["t0"] = s
@@ -423,7 +457,7 @@ def schedule(ops):
         busy[q] = busy.get(q, 0.0) + o["cost"]
         order.append(i)
         for j, lat in succ[i]:
-            est[j] = max(est[j], end + lat)
+            start[j] = max(start[j], end + lat)
             need[j] -= 1
             if not need[j]:
                 ready.setdefault(ops[j]["q"], []).append(j)
@@ -466,9 +500,9 @@ PLAN = {}
 
 def plan():
     if not PLAN:
-        ops = make_plan()
+        ops = make_plan(EST)
         link(ops)
-        order, total, busy = schedule(ops)
+        order, total, busy = schedule(ops, EST)
         PLAN.update(ops=ops, order=order, cnt=waits(ops, order), total=total, busy=busy)
     return PLAN
 
@@ -499,7 +533,8 @@ def rank_program(g, core, T, topo):
     narr = {}
     for t in range(1, ROUNDS):
         for c in range(NC):
-            narr["a%d_%d" % (t, c)] = len(topo.engines(T.cores[(rank - 3) % N], core))
+            for k in "eo":
+                narr["%s%d_%d" % (k, t, c)] = len(topo.engines(T.cores[(rank - 3) % N], core))
     narr["ar"] = sum(len(topo.engines(T.cores[(rank - 3 * t) % N], core)) for t in range(1, ROUNDS))
     for i in pl["order"]:
         o = ops[i]
@@ -514,6 +549,8 @@ def rank_program(g, core, T, topo):
                 Q.tensor_scalar(ap(a[0]), ap(a[1]), ap(a[2]), ap(a[3]), a[4], a[5])
         elif k == "tt":
             r = Q.tensor_tensor(ap(a[0]), ap(a[1]), ap(a[2]), a[3])
+        elif k == "scan":
+            r = Q.tensor_tensor_scan(ap(a[0]), ap(a[1]), ap(a[2]), a[3], a[4], a[5])
         elif k == "cp":
             r = Q.tensor_copy(ap(a[0]), ap(a[1]))
         elif k == "ms":
@@ -534,9 +571,9 @@ def rank_program(g, core, T, topo):
             continue
         elif k == "send":
             rid, pid = topo.addr(nxt, core)
-            src = R("sd", 256 * a[0] + n * a[1], 256 * a[0] + n * a[1] + n)
-            dst = R("rf", 256 * (a[0] + 1) + n * a[1], 256 * (a[0] + 1) + n * a[1] + n)
-            Q.remote_dma(ap(dst), ap(src), T.sem["a%d_%d" % (a[0] + 1, a[1])], T.sem["sent"], pid, rid, topo.mask(core, nxt))
+            x = 256 * a[0] + n * a[1] + 64 * a[2]
+            Q.remote_dma(ap(R("lst", x + 256, x + 320)), ap(R("sd", x, x + 64)), T.sem["%s%d_%d" % ("eo"[a[2]], a[0] + 1, a[1])],
+                         T.sem["sent"], pid, rid, topo.mask(core, nxt))
             sent[0] += len(topo.engines(core, nxt))
             continue
         else:

@@ -1,3 +1,4 @@
+import math
 from concourse.bass import DstId, RemoteDMATransfer
 from concourse.mybir import dt, AluOpType as A, AxisListType, ActivationFunctionType as F
 
@@ -5,45 +6,53 @@ NC = 2
 n = 128
 ROUNDS = 5
 CW = 1152
-ABS1 = "VV"
-ABS2 = "SS"
-OPEN = False
+TRIES = 3000
+EVEN1, EVEN2 = "VV", "SS"
+SPLIT = 0
+ODD0, ODD1, ODD2 = "PP", "PP", "VV"
+CUT1 = CUT2 = [0, 512, 1024]
+EM = ("VV", "VV")
+INORDER = False
+PENLAST = True
 
 f16, b16, f32, i32, u16 = "float16", "bfloat16", "float32", "int32", "uint16"
 SCRATCH = {
     "xw": ("sbuf", [128, 2560], b16), "ri": ("sbuf", [128, 256], i32), "ci": ("sbuf", [128, 1024], i32),
     "cc": ("sbuf", [128, CW], f32), "cy": ("sbuf", [128, CW], f32), "rf": ("sbuf", [128, 256], f16),
-    "lst": ("sbuf", [128, 256 * ROUNDS], u16), "sd": ("sbuf", [128, 256 * ROUNDS], u16), "l2": ("sbuf", [128, 256], u16),
+    "lst": ("sbuf", [128, 256 * ROUNDS], u16), "l2": ("sbuf", [128, 256 * ROUNDS], u16),
+    "fs": ("sbuf", [128, 1024 * ROUNDS], f16), "fr": ("sbuf", [128, 1024 * ROUNDS], f16), "bn": ("sbuf", [128, 640], b16),
+    "PO": ("sbuf", [128, 320], b16), "PS": ("sbuf", [128, 320], b16), "PG": ("sbuf", [128, 192], b16),
+    "init": ("sbuf", [128, 320], b16), "BB": ("sbuf", [128, 60], b16),
     "em": ("sbuf", [128, 2048], b16), "yo": ("sbuf", [128, 256], f32), "sv": ("sbuf", [128, 256], f32),
     "t3": ("sbuf", [128, 256], f32), "t4": ("sbuf", [128, 256], f32),
     "rr": ("sbuf", [128, 16 * ROUNDS], f32), "w": ("sbuf", [128, 16], f32), "hi": ("sbuf", [128, 16], i32),
     "hj": ("sbuf", [128, 16], i32), "hl": ("sbuf", [128, 16], u16), "hf": ("sbuf", [128, 16], f16),
     "e3": ("sbuf", [128, 128], b16), "sk": ("sbuf", [128, 16], b16), "off": ("sbuf", [128, 32], u16),
     "kc": ("sbuf", [128, ROUNDS], f32), "kj": ("sbuf", [128, 16], f32), "col": ("sbuf", [128, 8], f32),
-    "one": ("sbuf", [128, 256], b16), "Iz": ("sbuf", [128, 272], b16), "Q": ("sbuf", [128, 512], b16),
-    "Bw1": ("sbuf", [128, 256], b16), "Bw2": ("sbuf", [128, 192], b16), "P1": ("sbuf", [128, 192], b16),
-    "CC": ("sbuf", [128, 272], b16),
+    "j256": ("sbuf", [128, 256], b16), "ki": ("sbuf", [128, 4], i32), "Iz": ("sbuf", [128, 272], b16),
+    "zero": ("sbuf", [128, 192], b16), "EL": ("sbuf", [128, 72], b16),
+    "CC": ("sbuf", [128, 400], b16), "gi": ("sbuf", [128, 256], i32),
 }
-for _k in ("e1", "d1", "a1", "w1", "e2", "d2", "a2", "w2", "u2"):
+for _k in ("e1", "d1", "a1", "w1", "u1", "e2", "d2", "a2", "w2", "u2"):
     SCRATCH[_k] = ("sbuf", [128, 2048], b16)
-for _k in ("reo", "q", "ym", "aa", "cm", "r2", "qd", "r3", "so", "sf"):
+for _k in ("q", "ym", "aa", "cm", "r2", "qd", "r3", "sf"):
     SCRATCH[_k] = ("sbuf", [128, 256], f16)
-for _k in ("f", "g3", "eq", "ow", "fz", "sg"):
+for _k in ("f", "eq", "fz"):
     SCRATCH[_k] = ("sbuf", [128, 256], b16)
 for _k in ("x1", "f2", "x2"):
     SCRATCH[_k] = ("sbuf", [128, 272], b16)
 for _k in ("B8", "UP", "UW", "DD", "ML", "MH"):
     SCRATCH[_k] = ("sbuf", [128, 1024], b16)
-for _k in ("B", "B0", "I", "NI", "LI", "UI", "SH", "SD", "I8k", "N16k", "T16", "M16", "R15", "HB", "HI", "NH", "NDS", "ND2", "D256",
-           "SD64", "DSh", "YAh", "Ie", "I16", "B2", "NB", "sg1", "sg2", "half"):
+for _k in ("one", "km", "B", "I", "NI", "LI", "UI", "SH", "SD", "I8k", "N16k", "M16", "R15", "HB", "HI", "NH", "NDS", "ND2",
+           "SD64", "DSh", "YAh", "Ie", "I16", "sg1", "sg2", "half"):
     SCRATCH[_k] = ("sbuf", [128, 128], b16)
 for _k in range(8):
     SCRATCH["b%d" % _k] = ("psum", [128, 512], f32)
 SEMAPHORES = ["v", "s", "p", "q", "sent", "ar", "dr", "dx", "dc", "oy0", "oy1", "oc"] + \
-    ["%s%d_%d" % (k, t, c) for k in "eo" for t in range(1, ROUNDS) for c in range(NC)]
+    ["%s%d_%d" % (k, t, c) for k in "emo" for t in range(1, ROUNDS) for c in range(NC)]
 WIDE = set(k for k in SCRATCH if SCRATCH[k][2] in (f32, i32))
 
-EST = dict(CY=0.001, PE=0.0005, GA=1.6, SC=3.5, WAKE=0.16, OWN=0.06, NET=4.0, LEAD=4.0)
+EST = dict(CY=0.00083, PE=0.00042, GA=1.56, SC=3.5, WAKE=0.2, OWN=0.1, NET=5.0, LEAD=7.0)
 
 
 def R(name, a, b, step=1):
@@ -123,8 +132,8 @@ def make_plan(est):
             rd += [m[1], m[2]]
         return op("p", "mm", mms, rd, sorted(set((m[0][0], m[0][1], m[0][2]) for m in mms)), sum(max(64, size(m[2])) for m in mms) * PE)
 
-    def sel(out, in_, pat, cmp, fill, base, cm):
-        return op("q", "sel", (out, in_, pat, cmp, fill, base, cm), [in_], [out], 0.17 + 2 * size(out) * CY)
+    def iota(out, pat, base, cm):
+        return op("q", "iota", (out, pat, base, cm), [], [out], 0.13 + 2 * size(out) * CY)
 
     def dma(sem, out, in_, reads, writes, cost):
         return op("y", "dma", (out, in_), reads, writes, cost, sem=sem)
@@ -135,21 +144,26 @@ def make_plan(est):
     dma("dr", R("ri", 0, 256), ("T", "r0"), [], [R("ri", 0, 256)], 2.2)
     dma("dx", R("xw", 0, 2560), ("T", "x"), [], [R("xw", 0, 2560)], 5.0)
     dma("dc", R("ci", 0, 1024), ("T", "c0"), [R("xw", 0, 2560)], [R("ci", 0, 1024)], 4.5)
-    IN = [[-16, 8], [-1, 16]]
-    boost(1000, ms(R("one", 0, 256), 1.0))
+    col = lambda i: R("col", i, i + 1)
+    boost(1000, iota(R("ki", 0, 1), [[0, 1]], 0, 1))
+    boost(900, iota(R("j256", 0, 256), [[-1, 256]], 0, 0))
+    boost(800, iota(K("km"), [[-32, 8], [-1, 16]], 0, 0))
+    boost(700, iota(K("M16"), [[0, 8], [-1, 16]], 0, 0))
+    boost(600, iota(R("B8", 0, 1024), [[-1, 8], [-32, 8], [-1, 16]], -1, 0))
+    ts(R("ki", 1, 2), R("ki", 0, 1), 15, None, A.bitwise_and)
+    ts(col(6), R("ki", 1, 2), 0.0)
+    ts(col(7), R("ki", 0, 1), 2.0, col(6), A.mult, A.subtract)
+    ts(col(4), R("ki", 0, 1), 1024.0)
+    ms(K("one"), 1.0)
     ms(R("Iz", 0, 16), 0.0)
-    boost(900, sel(R("Iz", 16, 272), R("one", 0, 256), [[-16, 8], [-200, 2], [-1, 16]], A.is_equal, 0.0, 0, 1))
-    boost(800, sel(K("I"), K("one"), [[-1, 128]], A.is_equal, 0.0, 0, 1))
-    boost(700, sel(K("B0"), K("one"), [[-16, 8], [0, 16]], A.is_ge, 0.0, 0, 1))
-    boost(600, sel(K("B"), K("B0"), [[16, 8], [0, 16]], A.is_ge, 0.0, 15, -1))
-    boost(500, sel(K("T16"), K("one"), [[0, 8], [-1, 16]], A.is_equal, 0.0, 0, 1))
-    for j in range(2):
-        sel(R("Q", 256 * j, 256 * j + 256), R("one", 0, 256), [[1, 2], [-32, 8], [-1, 16]], A.is_equal, 0.0, -16 * j, 2)
-    sel(K("SH"), K("B"), IN, A.is_equal, 0.0, -1, 1)
-    sel(K("SD"), K("B"), IN, A.is_equal, 0.0, 1, 1)
-    sel(K("LI"), K("B"), [[16, 8], [1, 16]], A.is_ge, 0.0, 0, -1)
-    sel(K("UI"), K("B"), IN, A.is_ge, 0.0, 0, 1)
-    op("q", "iota", (R("col", 4, 5), [[0, 1]], 1024, 1), [], [R("col", 4, 5)], 0.14)
+    ts(R("Iz", 16, 272), R("j256", 0, 256), col(7), 0.0, A.add, A.is_equal)
+    ts(K("M16"), K("M16"), col(6), 0.0, A.add, A.is_equal)
+    for nm, x in (("I", 0.0), ("SH", 1.0), ("SD", -1.0)):
+        ts(K(nm), K("km"), col(7), x, A.add, A.is_equal)
+    ts(K("km"), K("km"), col(7))
+    for nm, x, z in (("B", 0.0, 16.0), ("LI", 7.5, 8.0), ("UI", -7.5, 8.0)):
+        act(K(nm), K("km"), F.Abs, bias=x)
+        ts(K(nm), K(nm), z, None, A.is_lt)
     PZ = lambda j, i: R("Iz", 16 - 16 * j + i, 272 - 16 * j, 2)
     T1 = lambda nm, s: R(nm, 128 * s, 128 * s + 128)
     BC = lambda nm: R(nm, 0, 128, 16)
@@ -185,26 +199,27 @@ def make_plan(est):
     ms(C720, 720.0)
     ms(C32, -32.0)
     ms(C10, 10.0)
-    mm(*grp(R("b0", 0, 128), ("T16", "T16")))
-    act(K("M16"), R("b0", 0, 128), F.Copy)
-    op("v", "red", (R("col", 0, 1), R("I", 15, 128, 16)), [R("I", 15, 128, 16)], [R("col", 0, 1)], .07)
-    op("v", "red", (R("col", 1, 2), R("I", 1, 128, 2)), [R("I", 1, 128, 2)], [R("col", 1, 2)], .07)
-    tt(R("col", 2, 3), R("col", 1, 2), R("col", 0, 1), A.subtract)
-    ts(R("col", 3, 4), R("col", 2, 3), -99.5, 100.0, A.mult, A.add)
-    ts(K("R15"), K("B"), R("col", 0, 1), None, A.mult)
+    ms(R("CC", 272, 400), -8.0)
+    ms(R("col", 5, 6), -5.5413)
+    ts(col(0), col(6), 15.0, None, A.is_equal)
+    ts(R("ki", 2, 3), R("ki", 0, 1), 1, None, A.bitwise_and)
+    ts(col(2), R("ki", 2, 3), col(0), None, A.subtract)
+    ts(col(3), col(2), -99.5, 100.0, A.mult, A.add)
+    ts(K("R15"), K("B"), col(0), None, A.mult)
     for c in range(NC):
         mm(*grp(Sb(c, 384, 512), (G("rf", c), "R15")))
         lanes(c, Sb(c, 384, 512))
         ts(R("rr", 8 * c, 8 * c + 8), Sb(c, 0, 8), 1.0 / 64, 1.0, A.mult, A.add)
     op("q", "rsend", (), [R("rr", 0, 16)], [], 1.5)
     op("n", "arr", (), [], [R("rr", 16, 16 * ROUNDS)], 0.0, sem="ar", tdep=(ops[-1], NET))
-    scaled("B2", "B", 2.0)
-    scaled("NB", "B", -1.0)
-    ms(R("Bw1", 0, 256), 0.0)
-    ts(R("Bw1", 0, 128, 16), BC("B"), 1.0, None, A.mult)
-    ts(R("Bw1", 128, 256, 16), BC("B"), 2.0, None, A.mult)
-    ms(R("Bw2", 0, 192), 0.0)
-    ts(R("Bw2", 128, 192, 8), BC("B"), 1.0, None, A.mult)
+    ms(R("BB", 0, 60), 0.0)
+    for i, x in enumerate((1.0, 2.0, -1.0)):
+        for a in (0, 12):
+            ts(R("BB", 20 * i + a, 20 * i + a + 8), BC("B"), x, None, A.mult)
+    ms(R("zero", 0, 192), 0.0)
+    ms(R("EL", 0, 72), 0.0)
+    ts(R("EL", 7, 71, 8), BC("B"), -1.0, None, A.mult)
+    ts(R("EL", 8, 72, 8), BC("B"), 1.0, None, A.mult)
     scaled("I8k", "I", 8192.0)
     scaled("N16k", "I", -16384.0)
     ms(K("sg1"), 1.0)
@@ -221,18 +236,18 @@ def make_plan(est):
     act(R("cc", 0, 1024), R("ci", 0, 1024), F.Identity, bias=-1280.0)
     ms(R("cc", 1024, CW), 0.0)
     ms(R("cy", 1024, CW), 0.0)
-    for h in range(8):
-        ts(T1("B8", h), K("B"), 1.0, None, A.mult)
-    P3 = [[-1, 8], [-16, 8], [-1, 16]]
-    sel(R("UP", 0, 1024), R("B8", 0, 1024), P3, A.is_equal, 0.0, -1, 1)
-    sel(R("UW", 0, 1024), R("B8", 0, 1024), P3, A.is_equal, 0.0, 15, 1)
-    for nm, x, terms in (
-            ("DD", 1.0, lambda s: (("I", T1("UP", s)), ("I", T1("UW", s)), ("NI", "I"))),
-            ("ML", 1.0, lambda s: (("I", "LI"), (T1("UW", s), "LI"))),
-            ("MH", 2048.0, lambda s: ((T1("UP", s), "I"), (T1("UW", s), T1("UW", s))))):
-        for h in range(2):
-            mm(*sum([grp(T1(W(0, h), i), *terms(4 * h + i)) for i in range(4)], []))
-            act(R(nm, 512 * h, 512 * h + 512), R(W(0, h), 0, 512), F.Copy, scale=x)
+    ts(R("UP", 0, 1024), R("B8", 0, 1024), col(7), 0.0, A.add, A.is_equal)
+    ts(R("UW", 0, 1024), R("B8", 0, 1024), col(7), -16.0, A.add, A.is_equal)
+    for nm, x, banks, terms in (
+            ("DD", 1.0, "b4 b5", lambda s: (("I", T1("UP", s)), ("I", T1("UW", s)), ("NI", "I"))),
+            ("ML", 1.0, "b0 b1", lambda s: (("I", "LI"), (T1("UW", s), "LI"))),
+            ("MH", 2048.0, "b2 b6", lambda s: ((T1("UP", s), "I"), (T1("UW", s), T1("UW", s))))):
+        for h, e in enumerate(banks.split()):
+            mm(*sum([grp(T1(e, i), *terms(4 * h + i)) for i in range(4)], []))
+            if h:
+                ts(R(nm, 512, 1024), R(e, 0, 512), x, None, A.mult)
+            else:
+                act(R(nm, 0, 512), R(e, 0, 512), F.Copy, scale=x)
     scaled("HB", "B", 0.5)
     scaled("HI", "I", 0.5)
     scaled("NH", "I", -0.5)
@@ -240,40 +255,77 @@ def make_plan(est):
     tt(K("YAh"), K("I"), K("SD"), A.add)
     scaled("YAh", "YAh", 0.5)
     scaled("ND2", "NDS", 2.0)
-    scaled("D256", "NDS", -256.0)
     scaled("DSh", "NDS", -0.5)
     scaled("SD64", "SD", 64.0)
     scaled("Ie", "I", 1.0 / 4096)
     scaled("I16", "I", 16.0)
-    scaled("P1", "SH", -128.0)
-    act(R("P1", 128, 192), R("I", 1, 128, 2), F.Copy, scale=-128.0)
+    odd = lambda nm: R(nm, 1, 128, 2)
+    for out, src, x in ((R("PO", 0, 128), K("SH"), -128.0), (R("PO", 128, 192), odd("I"), -128.0), (R("PG", 0, 64), odd("NDS"), -256.0),
+                        (R("PG", 64, 192, 2), odd("NDS"), 256.0), (R("PG", 65, 192, 2), odd("NDS"), 256.0),
+                        (R("PS", 0, 128, 2), odd("I"), 128.0), (R("PS", 1, 128, 2), odd("I"), 128.0), (R("PS", 128, 192), odd("I"), -128.0),
+                        (R("PS", 192, 320), R("PS", 0, 128), -1.0)):
+        act(out, src, F.Copy, scale=x)
+    tt(R("PO", 192, 320), R("PO", 0, 128), R("PS", 0, 128), A.add)
+    ms(R("init", 0, 192), 0.0)
+    ms(R("init", 192, 320), -1.0)
 
     X = R("xw", 0, 2560)
     sends = {}
 
-    def gathers(c, lst, e, d, a, w, u, eng):
+    def gathers(c, lst, e, d, a, w, u, even, odd, cuts):
         v0 = 1024 * c
-        pc = lambda nm, h, k=512, s=0: R(nm, v0 + 512 * h + s, v0 + 512 * h + s + k)
+        pc = lambda nm, x, z, s=0: R(nm, v0 + x + s, v0 + z + s)
         rest = []
         for h in range(2):
-            act(pc(e, h), ind(X, R(lst[0], lst[1] + 32 * h, lst[1] + 32 * h + 32)), F.Copy)
-            o = grp(R(W(c, h), 0, 511), ("I", pc(e, h, 511, 1)), ("NI", pc(e, h, 511)), ("NI", pc(d, h, 511)))
-            if u and not OPEN:
-                mm(*grp(R(W(c, h), 0, 511), ("I", pc(e, h, 511, 1)), ("NI", pc(e, h, 511))))
+            x, z = 512 * h, 512 * h + 511
+            for y0, y1 in zip(cuts, cuts[1:]):
+                if y0 // 512 == h:
+                    act(pc(e, y0, y1), ind(X, R(lst[0], lst[1] + y0 // 16, lst[1] + y1 // 16)), F.Copy)
+            o = grp(R(W(c, h), 0, 511), ("I", pc(e, x, z, 1)), ("NI", pc(e, x, z)), ("NI", pc(d, x, z)))
+            if u or odd == "V":
+                mm(o[0], o[1][:4] + (True,))
                 rest.append(o)
             else:
-                mm(o[0], o[1][:4] + (bool(u),))
+                mm(*o[:2])
                 rest.append(o[2:])
             if u:
-                act(pc(u, h, 511), R(W(c, h), 0, 511), F.Abs)
-        for h in range(2):
-            tt(pc(d, h), ind(X, R(lst[0], lst[1] + 64 + 32 * h, lst[1] + 96 + 32 * h)), pc(e, h), A.subtract)
-            mm(*rest[h])
-            act(pc(w, h, 511), R(W(c, h), 0, 511), F.Abs)
-            if eng == "S":
-                act(pc(a, h), pc(d, h), F.Abs)
+                act(pc(u, x, z), R(W(c, h), 0, 511), F.Abs)
+        for y0, y1 in zip(cuts, cuts[1:]):
+            h = y0 // 512
+            tt(pc(d, y0, y1), ind(X, R(lst[0], lst[1] + 64 + y0 // 16, lst[1] + 64 + y1 // 16)), pc(e, y0, y1), A.subtract)
+            if odd == "V":
+                tt(pc(w, y0, y1 - 1), R(W(c, h), y0 - 512 * h, y1 - 1 - 512 * h), pc(d, y0, y1 - 1), A.max)
+            elif y1 % 512 == 0:
+                mm(*rest[h])
+                act(pc(w, y1 - 512, y1 - 1), R(W(c, h), 0, 511), F.Abs)
+            if even == "S":
+                act(pc(a, y0, y1), pc(d, y0, y1), F.Abs)
             else:
-                ts(pc(a, h), pc(d, h), 0.0, None, A.max)
+                ts(pc(a, y0, y1), pc(d, y0, y1), 0.0, None, A.max)
+
+    def FL(name, t, c, i):
+        a = 1024 * t + 512 * c + 128 * i
+        return R(name, a, a + 128)
+
+    def send(t, c, src, dst, kind):
+        sends[t, c].append(op("q", "send", (src, dst, "%s%d_%d" % (kind, t + 1, c)), [src], [], 1.0))
+
+    def steps(c, e, d, a, w, even, odd, k, twice=False):
+        def put(src, ms_, par, x):
+            z = 20 if twice else 8
+            return [(R(src, 1024 * c + m, 1024 * c + 1024, 8), R("BB", 20 * x, 20 * x + z), Sb(c, 2 * m + par, 2 * m + par + 16 * z - 15, 16))
+                    for m in ms_]
+        pe = [(R(e, 1024 * c + m, 1024 * c + 1024, 8), R("EL", 8 - m, 72 - m), Sb(c, x + 1, x + 128, 2))
+              for m in range(8) for x in ((0, 192) if twice else (0,))] if odd == "V" else []
+        pd = (put(d, range(k), 0, 2) if even == "V" else []) + (put(d, range(7), 1, 2) if odd == "V" else [])
+        return [pe, pd, put(a, range(k), 0, even == "V"), put(w, range(7), 1, odd == "V")]
+
+    def group(out, parts):
+        o = grp(out, *sum(parts, []))
+        for p in parts:
+            if p:
+                mm(*o[:len(p)])
+                o = o[len(p):]
 
     def sums(c, src, ms_, col, step, mat="B"):
         return [(R(src, 1024 * c + m, 1024 * c + 1024, 8), BC(mat), Sb(c, col(m), col(m) + 8 * step - step + 1, step)) for m in ms_]
@@ -283,32 +335,32 @@ def make_plan(est):
         for c in range(NC - 1, -1, -1):
             cur[0] = c
             l0 = 256 * t + n * c
-            if t:
-                op("n", "arr", (), [], [R("lst", l0, l0 + 64)], 0.0, sem="e%d_%d" % (t, c), tdep=(sends[t - 1, c, 0], NET))
-                op("n", "arr", (), [], [R("lst", l0 + 64, l0 + 128)], 0.0, sem="o%d_%d" % (t, c), tdep=(sends[t - 1, c, 1], NET))
-            gathers(c, R("lst", l0, l0 + n), "e1", "d1", "a1", "w1", None, ABS1[c])
-            ts(G("reo", c), R("lst", l0, l0 + n), -1280.0)
-            ev = lambda m: 2 * m
-            od = lambda m: 2 * m + 1
-            if ABS1[c] == "S":
-                s0 = [(R("a1", 1024 * c, 1024 * c + 1024, 8), R("Bw1", 0, 128))] + sums(c, "a1", range(1, 8), ev, 16)
+            if t == 0:
+                rin = G("rf", c)
+                gathers(c, R("lst", l0, l0 + n), "e1", "d1", "a1", "w1", None, EVEN1[c], ODD0[c], CUT1)
+                group(Sb(c, 0, 128), [[("I", R("zero", 0, 128))]] + steps(c, "e1", "d1", "a1", "w1", EVEN1[c], ODD0[c], 8))
+                ts(G("f", c), Sb(c, 0, 128), 34.5, None, A.is_gt)
             else:
-                s0 = [(R("a1", 1024 * c, 1024 * c + 1024, 8), R("Bw1", 128, 256))] + sums(c, "a1", range(1, 8), ev, 16, "B2") + \
-                    sums(c, "d1", range(8), ev, 16, "NB")
-            o = grp(Sb(c, 0, 128), *(s0 + sums(c, "w1", range(7), od, 16)))
-            mm(*o[:len(s0)])
-            mm(*o[len(s0):])
-            ts(G("f", c), Sb(c, 0, 128), 34.5, None, A.is_gt)
+                for o in sends[t - 1, c]:
+                    op("n", "arr", (), [], [o["args"][1]], 0.0, sem=o["args"][2], tdep=(o, NET))
+                ow, g3, sg, rin = [FL("fr", t - 1, c, i) for i in range(4)]
+                gathers(c, R("lst", l0, l0 + n), "e1", "d1", "a1", "w1", "u1", EVEN1[c], ODD1[c], CUT1)
+                pe, pd, pa, pw = steps(c, "e1", "d1", "a1", "w1", EVEN1[c], ODD1[c], 8, True)
+                group(Sb(c, 0, 320), [[("one", R("init", 0, 320))], pe, sums(c, "u1", range(7), lambda m: 128 + m, 8), pd, pa, pw,
+                                      [(g3, R("PG", 0, 192), Sb(c, 128, 320)), (ow, R("PO", 0, 320))], [(sg, R("PS", 0, 320))]])
+                a = 320 * c
+                ts(R("bn", a, a + 320), Sb(c, 0, 320), 290.5, None, A.is_gt)
+                mm(*grp(Lb(c, 0, 128), ("I", R("bn", a, a + 128)), ("I", R("bn", a + 128, a + 192), Lb(c, 1, 128, 2)),
+                        ("I", R("bn", a + 192, a + 320, 2), Lb(c, 1, 128, 2)), ("I", R("bn", a + 193, a + 320, 2), Lb(c, 1, 128, 2))))
+                ts(G("f", c), Lb(c, 0, 128), 0.0)
             scan(GP("x1", c, 0), G("f", c), K("sg1"), 0.0, A.max, A.mult)
-            back = lambda a: [(T1("Q", 2 * j + i), R("reo", n * c + 64 * i, n * c + 64 * i + 64), Sb(c, a + j, a + 128, 2))
-                              for j in range(2) for i in range(2)]
-            mm(*grp(Sb(c, 128, 256), (GP("x1", c, 1), "N16k"), (G("f", c), "I8k"), *back(128)))
+            group(Sb(c, 128, 256), [[("I", rin), (G("f", c), "I8k")], [(GP("x1", c, 1), "N16k")]])
             ts(G("q", c), Sb(c, 128, 256), 2048.0, -8192.0, A.max, A.add)
             mm(*grp(Sb(c, 384, 512), ("one", C720), (G("q", c), "B")))
             lanes(c, Sb(c, 384, 512))
             l8 = lambda nm: R(nm, 8 * c, 8 * c + 8)
             tt(l8("w"), Sb(c, 0, 8), R("rr", 16 * t + 8 * c, 16 * t + 8 * c + 8), A.mult)
-            mm(*grp(Lb(c, 256, 384), (GP("x1", c, 1), "I8k"), *[(a, b, Lb(c, o[1], o[2], 2)) for a, b, o in back(256)]))
+            mm(*grp(Lb(c, 256, 384), (GP("x1", c, 1), "I8k"), ("I", rin)))
             act(G("aa", c), Lb(c, 256, 384), F.Identity, bias=4096.0, scale=-1.0)
             ts(l8("hi"), l8("w"), R("kc", t, t + 1))
             ts(l8("hj"), l8("hi"), 1023 + 2 ** 23, None, A.bitwise_and)
@@ -318,7 +370,10 @@ def make_plan(est):
             for i in range(2):
                 mm(*to_list(Sb(c, 128 + 64 * i, 192 + 64 * i), G("r2", c), i))
             for i in range(2):
-                ts(R("l2", n * c + 64 * i, n * c + 64 * i + 64), Sb(c, 128 + 64 * i, 192 + 64 * i), 1280.0)
+                ts(R("l2", l0 + 64 * i, l0 + 64 * i + 64), Sb(c, 128 + 64 * i, 192 + 64 * i), 1280.0)
+            sends[t, c] = []
+            if not last:
+                send(t, c, R("l2", l0, l0 + n), R("lst", l0 + 256, l0 + 256 + n), "e")
         H = lambda nm: R(nm, 0, 16)
         ts(H("hf"), H("hj"), 2048.0, None, A.min)
         mm(*sum([grp(Sb(0, 384 + 16 * s, 400 + 16 * s), (T1("DD", s), H("hf"))) for s in range(8)], []))
@@ -336,47 +391,49 @@ def make_plan(est):
             for h in range(2):
                 e = W(c, 1) if h else "b%d" % (4 * c + 2)
                 mm(*sum([grp(T1(e, s), (T1("DD", 4 * h + s), G("r2", c))) for s in range(4)], []))
-                ts(R("em", 1024 * c + 512 * h, 1024 * c + 512 * h + 512), R(e, 0, 512), 0.0, None, A.is_equal)
-            gathers(c, G("l2", c), "e2", "d2", "a2", "w2", "u2", ABS2[c])
-            mm(*grp(Lb(c, 0, 128), *[(T1("ML", s), T1("em", 8 * c + s)) for s in range(8)]))
-            act(G("g3", c), Lb(c, 0, 128), F.Sign)
-            mm(*grp(Lb(c, 128, 256), ("NDS", G("g3", c))))
+                em = R("em", 1024 * c + 512 * h, 1024 * c + 512 * h + 512)
+                if EM[c][h] == "V":
+                    ts(em, R(e, 0, 512), 0.0, 1.0 / 256 if "S" in EM[c] else 1.0, A.is_equal, A.mult)
+                else:
+                    act(em, R(e, 0, 512), F.Sigmoid, bias=R("col", 5, 6), scale=128.0)
+            l0 = 256 * t + n * c
+            ow, g3, sg, so = [FL("fs", t, c, i) for i in range(4)]
+            gathers(c, R("l2", l0, l0 + n), "e2", "d2", "a2", "w2", "u2", EVEN2[c], ODD2[c], CUT2)
+            ml = [(T1("ML", s), T1("em", 8 * c + s)) for s in range(8)]
+            if "S" in EM[c]:
+                mm(*grp(Lb(c, 0, 128), ("Ie", R("CC", 272, 400)), *ml))
+                ts(G("gi", c), Lb(c, 0, 128), -0.496)
+                tt(g3, Lb(c, 0, 128), G("gi", c), A.is_gt)
+            else:
+                mm(*grp(Lb(c, 0, 128), *ml))
+                act(g3, Lb(c, 0, 128), F.Sign)
+            mm(*grp(Lb(c, 128, 256), ("NDS", g3)))
             tt(G("qd", c), Lb(c, 128, 256), G("r2", c), A.mult)
             mm(*(grp(Lb(c, 256, 384), ("HB", G("qd", c)), ("NH", G("r2", c))) +
                  grp(Lb(c, 384, 512), ("HB", G("qd", c)), ("HI", G("r2", c)))))
             ts(G("eq", c), Lb(c, 256, 384), 0.0, None, A.is_equal)
-            mm(*grp(Lb(c, 0, 128), ("UI", G("eq", c)), ("SD64", G("g3", c))))
-            act(G("ow", c), Lb(c, 0, 128), F.Sign, bias=-64.5)
-            tt(G("t3", c), Lb(c, 256, 384), G("ow", c), A.mult)
+            mm(*grp(Lb(c, 0, 128), ("UI", G("eq", c)), ("SD64", g3)))
+            act(ow, Lb(c, 0, 128), F.Sign, bias=-64.5)
+            both = lambda nm, i, k: R(nm, FL(nm, t, c, i)[1], FL(nm, t, c, k)[2])
+            if SPLIT and not last:
+                send(t, c, both("fs", 0, 1), both("fr", 0, 1), "m")
+            tt(G("t3", c), Lb(c, 256, 384), ow, A.mult)
             tt(G("r3", c), Lb(c, 384, 512), G("t3", c), A.add)
-            s0 = 256 * t + n * c
-            if not last:
-                mm(*to_list(Lb(c, 0, 64), G("r3", c), 0))
-                ts(R("sd", s0, s0 + 64), Lb(c, 0, 64), 1280.0)
-                sends[t, c, 0] = op("q", "send", (t, c, 0), [R("sd", s0, s0 + 64)], [], 1.0)
             mm(*(grp(Lb(c, 128, 256), ("DSh", G("r3", c))) + grp(Lb(c, 256, 384), ("YAh", G("r3", c)))))
-            parts = [[(R("u2", 1024 * c, 1024 * c + 1024, 8), R("Bw2", 0, 192))] + sums(c, "u2", range(1, 7), lambda m: 128 + m, 8),
-                     sums(c, "a2", range(7), ev, 16) if ABS2[c] == "S" else
-                     sums(c, "a2", range(7), ev, 16, "B2") + sums(c, "d2", range(7), ev, 16, "NB"),
-                     [(G("ow", c), R("P1", 0, 192)), (G("g3", c), R("D256", 1, 128, 2), Sb(c, 128, 192))],
-                     sums(c, "w2", range(7), od, 16)]
-            o = grp(Sb(c, 0, 192), *sum(parts, []))
-            for p in parts:
-                mm(*o[:len(p)])
-                o = o[len(p):]
+            pe, pd, pa, pw = steps(c, "e2", "d2", "a2", "w2", EVEN2[c], ODD2[c], 7)
+            pen = [(ow, R("PO", 0, 192)), (g3, R("PG", 0, 64), Sb(c, 128, 192))]
+            group(Sb(c, 0, 192), [[("I", R("zero", 0, 192))], pe, sums(c, "u2", range(7), lambda m: 128 + m, 8), pd, pa] +
+                  ([pw, pen] if PENLAST else [pen, pw]))
             ts(GP("f2", c, 0), Sb(c, 0, 128), 162.5, -4096.0, A.is_le, A.mult)
             ts(R("fz", n * c + 1, n * c + n, 2), Sb(c, 128, 192), 162.5, None, A.is_gt)
-            mm(*grp(Sb(c, 192, 320), ("I", G("ow", c)), ("ND2", G("g3", c)), (GP("f2", c, 1), "Ie"), (GP("f2", c, 0), "Ie"),
-                    (G("fz", c), "I16")))
-            act(G("sg", c), Sb(c, 192, 320), F.Sign, bias=R("col", 3, 4))
-            tt(G("t4", c), Lb(c, 128, 256), G("sg", c), A.mult)
-            tt(G("so", c), Lb(c, 256, 384), G("t4", c), A.subtract)
+            group(Lb(c, 0, 128), [[("I", ow), ("ND2", g3)], [(GP("f2", c, 1), "Ie"), (GP("f2", c, 0), "Ie")], [(G("fz", c), "I16")]])
+            act(sg, Lb(c, 0, 128), F.Sign, bias=R("col", 3, 4))
+            tt(G("t4", c), Lb(c, 128, 256), sg, A.mult)
+            tt(so, Lb(c, 256, 384), G("t4", c), A.subtract)
             if not last:
-                mm(*to_list(Sb(c, 320, 384), G("so", c), 1))
-                ts(R("sd", s0 + 64, s0 + 128), Sb(c, 320, 384), 1280.0)
-                sends[t, c, 1] = op("q", "send", (t, c, 1), [R("sd", s0 + 64, s0 + 128)], [], 1.0)
+                send(t, c, both("fs", 2 * SPLIT, 3), both("fr", 2 * SPLIT, 3), "o")
             else:
-                act(G("yo", c), G("so", c), F.Identity, bias=1280.0)
+                act(G("yo", c), so, F.Identity, bias=1280.0)
                 dma("oy%d" % c, ("T", "yr", n * c, n * c + n), G("yo", c), [G("yo", c)], [], 2.0)
             scan(GP("x2", c, 0), GP("f2", c, 0), K("sg2"), -4096.0, A.max, A.min)
             mm(*grp(Lb(c, 384, 512), (G("r3", c), "I"), ("one", C32), ("NI", GP("x2", c, 1))))
@@ -402,6 +459,9 @@ def link(ops):
                     continue
                 if ps and po["q"] == o["q"] == "p":
                     keep_order.add(po["i"])
+                elif INORDER and wr and po["q"] == o["q"] and o["q"] in "vs":
+                    if a < y and x < b:
+                        keep_order.add(po["i"])
                 elif (a < y and x < b and (wr or pw)) or (ps and po["q"] != o["q"]):
                     dep.add(po["i"])
         for r, wr in acc:
@@ -464,6 +524,84 @@ def schedule(ops, est):
     return order, max(o["t0"] + o["cost"] for o in ops), busy
 
 
+def place(ops, pred, key, back):
+    N = len(ops)
+    span = range(N - 1, -1, -1) if back else range(N)
+    key = list(key)
+    for i in span:
+        for d, _ in pred[i]:
+            if key[d] >= key[i]:
+                key[i] = key[d] + 1e-7
+    st, end, line = [0.0] * N, [0.0] * N, {}
+    for i in sorted(span, key=lambda k: key[k]):
+        o = ops[i]
+        s = 0.0
+        for d, lat in pred[i]:
+            if end[d] + lat > s:
+                s = end[d] + lat
+        hold = o["hold"]
+        if hold:
+            L = line.setdefault(o["q"], [])
+            k = len(L)
+            while k and L[k - 1][0] > s:
+                k -= 1
+            if k and L[k - 1][1] > s:
+                s = L[k - 1][1]
+            while k < len(L) and L[k][0] < s + hold - 1e-9:
+                s = L[k][1]
+                k += 1
+            L.insert(k, (s, s + hold))
+        st[i], end[i] = s, s + o["cost"]
+    return st, end
+
+
+def improve(ops, est, tries):
+    N = len(ops)
+    pred, succ = [[] for _ in range(N)], [[] for _ in range(N)]
+    for o in ops:
+        o["hold"] = 0.0 if o["kind"] == "arr" else 0.05 if o["kind"] == "dma" else o["cost"]
+        e = [(d, est["OWN"] if ops[d]["q"] == o["q"] else est["WAKE"]) for d in o["dep"]] + [(d, 0.0) for d in o["ord"]]
+        if o.get("tdep"):
+            e.append((o["tdep"][0]["i"], o["tdep"][1]))
+        for d, lat in e:
+            pred[o["i"]].append((d, lat))
+            succ[d].append((o["i"], lat))
+
+    def passes(key, k):
+        best = None
+        for j in range(k):
+            st, end = place(ops, pred, key, False)
+            if best is None or max(end) < best[0] - 1e-9:
+                best = (max(end), st)
+            if j < k - 1:
+                key = [-e for e in place(ops, succ, [-e for e in end], True)[1]]
+        return best
+
+    seed = [1]
+
+    def rnd():
+        seed[0] = (seed[0] * 1103515245 + 12345) % 2 ** 31
+        return seed[0] / 2 ** 31
+
+    best = cur = passes([o["t0"] for o in ops], 6)
+    for k in range(tries):
+        lo = rnd() * cur[0]
+        if rnd() < 0.5:
+            amp, hi = (0.2, 0.5, 1.0, 2.0)[int(4 * rnd())], lo + 3 + 12 * rnd()
+            key = [s + (amp * (2 * rnd() - 1) if lo < s < hi else 0.0) for s in cur[1]]
+        else:
+            c, hi, d, q = int(2 * rnd()), lo + 1 + 8 * rnd(), 5 * (rnd() - rnd()), ("v", "s", "p", "vsp")[int(4 * rnd())]
+            key = [s + (d if lo < s < hi and o["c"] == c and o["q"] in q else 0.0) for s, o in zip(cur[1], ops)]
+        new = passes(key, 2)
+        if new[0] - cur[0] <= -(0.15 * (1 - k / tries) + 0.02) * math.log(1 - rnd()):
+            cur = new
+        if new[0] < best[0]:
+            best = new
+    for o in ops:
+        o["t0"] = best[1][o["i"]]
+    return sorted(range(N), key=lambda i: (best[1][i], i)), best[0]
+
+
 def waits(ops, order):
     cnt, know = {}, {}
     for i in order:
@@ -503,6 +641,7 @@ def plan():
         ops = make_plan(EST)
         link(ops)
         order, total, busy = schedule(ops, EST)
+        order, total = improve(ops, EST, TRIES)
         PLAN.update(ops=ops, order=order, cnt=waits(ops, order), total=total, busy=busy)
     return PLAN
 
@@ -533,7 +672,7 @@ def rank_program(g, core, T, topo):
     narr = {}
     for t in range(1, ROUNDS):
         for c in range(NC):
-            for k in "eo":
+            for k in "emo":
                 narr["%s%d_%d" % (k, t, c)] = len(topo.engines(T.cores[(rank - 3) % N], core))
     narr["ar"] = sum(len(topo.engines(T.cores[(rank - 3 * t) % N], core)) for t in range(1, ROUNDS))
     for i in pl["order"]:
@@ -555,8 +694,6 @@ def rank_program(g, core, T, topo):
             r = Q.tensor_copy(ap(a[0]), ap(a[1]))
         elif k == "ms":
             r = Q.memset(ap(a[0]), a[1])
-        elif k == "red":
-            r = Q.tensor_reduce(ap(a[0]), ap(a[1]), AxisListType.X, A.add)
         elif k == "act":
             r = Q.activation(ap(a[0]), ap(a[1]), a[2], bias=ap(a[3]), scale=a[4], accum_out=ap(a[5]))
         elif k == "mm":
@@ -564,16 +701,12 @@ def rank_program(g, core, T, topo):
                 r = Q.matmul(ap(m[0]), ap(m[1]), ap(m[2]), m[3], m[4])
         elif k == "iota":
             r = Q.iota(ap(a[0]), a[1], a[2], a[3], allow_small_or_imprecise_dtypes=True)
-        elif k == "sel":
-            r = Q.affine_select(ap(a[0]), ap(a[1]), a[2], a[3], a[4], a[5], a[6])
         elif k == "dma":
             Q.dma_start(side(a[0]), side(a[1])).then_inc(T.sem[o["sem"]], 16)
             continue
         elif k == "send":
             rid, pid = topo.addr(nxt, core)
-            x = 256 * a[0] + n * a[1] + 64 * a[2]
-            Q.remote_dma(ap(R("lst", x + 256, x + 320)), ap(R("sd", x, x + 64)), T.sem["%s%d_%d" % ("eo"[a[2]], a[0] + 1, a[1])],
-                         T.sem["sent"], pid, rid, topo.mask(core, nxt))
+            Q.remote_dma(ap(a[1]), ap(a[0]), T.sem[a[2]], T.sem["sent"], pid, rid, topo.mask(core, nxt))
             sent[0] += len(topo.engines(core, nxt))
             continue
         else:

@@ -6,12 +6,14 @@ NC = 2
 n = 128
 ROUNDS = 5
 CW = 1152
+LEADS = (0.0, 3.0, 5.0, 7.0, 9.0)
 TRIES = 3000
-EVEN1, EVEN2 = "VV", "SS"
-SPLIT = 0
+EVEN1, EVEN2 = "SV", "SS"
+SPLIT = 1
 ODD0, ODD1, ODD2 = "PP", "PP", "VV"
 CUT1 = CUT2 = [0, 512, 1024]
-EM = ("VV", "VV")
+FS = 1
+NOINIT = 0
 INORDER = False
 PENLAST = True
 
@@ -20,9 +22,9 @@ SCRATCH = {
     "xw": ("sbuf", [128, 2560], b16), "ri": ("sbuf", [128, 256], i32), "ci": ("sbuf", [128, 1024], i32),
     "cc": ("sbuf", [128, CW], f32), "cy": ("sbuf", [128, CW], f32), "rf": ("sbuf", [128, 256], f16),
     "lst": ("sbuf", [128, 256 * ROUNDS], u16), "l2": ("sbuf", [128, 256 * ROUNDS], u16),
-    "fs": ("sbuf", [128, 1024 * ROUNDS], f16), "fr": ("sbuf", [128, 1024 * ROUNDS], f16), "bn": ("sbuf", [128, 640], b16),
-    "PO": ("sbuf", [128, 320], b16), "PS": ("sbuf", [128, 320], b16), "PG": ("sbuf", [128, 192], b16),
-    "init": ("sbuf", [128, 320], b16), "BB": ("sbuf", [128, 60], b16),
+    "fs": ("sbuf", [128, 768 * ROUNDS], f16), "fr": ("sbuf", [128, 768 * ROUNDS], f16), "bn": ("sbuf", [128, 640], b16),
+    "PO": ("sbuf", [128, 192], b16), "PS": ("sbuf", [128, 320], b16), "PG": ("sbuf", [128, 64], b16),
+    "BB": ("sbuf", [128, 60], b16),
     "em": ("sbuf", [128, 2048], b16), "yo": ("sbuf", [128, 256], f32), "sv": ("sbuf", [128, 256], f32),
     "t3": ("sbuf", [128, 256], f32), "t4": ("sbuf", [128, 256], f32),
     "rr": ("sbuf", [128, 16 * ROUNDS], f32), "w": ("sbuf", [128, 16], f32), "hi": ("sbuf", [128, 16], i32),
@@ -30,21 +32,21 @@ SCRATCH = {
     "e3": ("sbuf", [128, 128], b16), "sk": ("sbuf", [128, 16], b16), "off": ("sbuf", [128, 32], u16),
     "kc": ("sbuf", [128, ROUNDS], f32), "kj": ("sbuf", [128, 16], f32), "col": ("sbuf", [128, 8], f32),
     "j256": ("sbuf", [128, 256], b16), "ki": ("sbuf", [128, 4], i32), "Iz": ("sbuf", [128, 272], b16),
-    "zero": ("sbuf", [128, 192], b16), "EL": ("sbuf", [128, 72], b16),
-    "CC": ("sbuf", [128, 400], b16), "gi": ("sbuf", [128, 256], i32),
+    "zero": ("sbuf", [128, 320], b16), "EL": ("sbuf", [128, 72], b16),
+    "CC": ("sbuf", [128, 264], b16),
 }
 for _k in ("e1", "d1", "a1", "w1", "u1", "e2", "d2", "a2", "w2", "u2"):
     SCRATCH[_k] = ("sbuf", [128, 2048], b16)
-for _k in ("q", "ym", "aa", "cm", "r2", "qd", "r3", "sf"):
+for _k in ("q", "ym", "aa", "cm", "r2", "qd", "so", "sf"):
     SCRATCH[_k] = ("sbuf", [128, 256], f16)
-for _k in ("f", "eq", "fz"):
+for _k in ("f", "eq", "fz", "g3"):
     SCRATCH[_k] = ("sbuf", [128, 256], b16)
 for _k in ("x1", "f2", "x2"):
     SCRATCH[_k] = ("sbuf", [128, 272], b16)
 for _k in ("B8", "UP", "UW", "DD", "ML", "MH"):
     SCRATCH[_k] = ("sbuf", [128, 1024], b16)
 for _k in ("one", "km", "B", "I", "NI", "LI", "UI", "SH", "SD", "I8k", "N16k", "M16", "R15", "HB", "HI", "NH", "NDS", "ND2",
-           "SD64", "DSh", "YAh", "Ie", "I16", "sg1", "sg2", "half"):
+           "SD64", "DSh", "YAh", "Ie", "I16", "IO", "OD", "sg1", "sg2", "half"):
     SCRATCH[_k] = ("sbuf", [128, 128], b16)
 for _k in range(8):
     SCRATCH["b%d" % _k] = ("psum", [128, 512], f32)
@@ -52,7 +54,8 @@ SEMAPHORES = ["v", "s", "p", "q", "sent", "ar", "dr", "dx", "dc", "oy0", "oy1", 
     ["%s%d_%d" % (k, t, c) for k in "emo" for t in range(1, ROUNDS) for c in range(NC)]
 WIDE = set(k for k in SCRATCH if SCRATCH[k][2] in (f32, i32))
 
-EST = dict(CY=0.00083, PE=0.00042, GA=1.56, SC=3.5, WAKE=0.2, OWN=0.1, NET=5.0, LEAD=7.0)
+EST = dict(CY=0.00083, PE=0.00042, GA=1.56, SC=3.5, WAKE=0.2, OWN=0.1, NET=4.5, LINK=0.004, LEAD=7.0)
+SLOW = dict(CY=0.00125, PE=0.00062, GA=2.0, SC=5.0)
 
 
 def R(name, a, b, step=1):
@@ -73,13 +76,13 @@ def isref(x):
 
 
 def make_plan(est):
-    ops = []
+    ops, sends = [], {}
     cur = [None]
     CY, PE, GA, NET = est["CY"], est["PE"], est["GA"], est["NET"]
 
     def op(queue, kind, args, reads, writes, cost, **kw):
         d = dict(i=len(ops), q=queue, kind=kind, args=args, r=[], w=list(writes), cost=cost, sem=None, pb=est["LEAD"] * (cur[0] == 1),
-                 c=cur[0])
+                 c=cur[0], t=len(sends) // 2)
         for x in reads:
             if isref(x):
                 d["r"] += [x[1], x[2]] if x[0] == "ind" else [x]
@@ -199,12 +202,8 @@ def make_plan(est):
     ms(C720, 720.0)
     ms(C32, -32.0)
     ms(C10, 10.0)
-    ms(R("CC", 272, 400), -8.0)
-    ms(R("col", 5, 6), -5.5413)
     ts(col(0), col(6), 15.0, None, A.is_equal)
-    ts(R("ki", 2, 3), R("ki", 0, 1), 1, None, A.bitwise_and)
-    ts(col(2), R("ki", 2, 3), col(0), None, A.subtract)
-    ts(col(3), col(2), -99.5, 100.0, A.mult, A.add)
+    ts(col(3), col(0), 99.5, 0.5, A.mult, A.add)
     ts(K("R15"), K("B"), col(0), None, A.mult)
     for c in range(NC):
         mm(*grp(Sb(c, 384, 512), (G("rf", c), "R15")))
@@ -216,7 +215,7 @@ def make_plan(est):
     for i, x in enumerate((1.0, 2.0, -1.0)):
         for a in (0, 12):
             ts(R("BB", 20 * i + a, 20 * i + a + 8), BC("B"), x, None, A.mult)
-    ms(R("zero", 0, 192), 0.0)
+    ms(R("zero", 0, 320), 0.0)
     ms(R("EL", 0, 72), 0.0)
     ts(R("EL", 7, 71, 8), BC("B"), -1.0, None, A.mult)
     ts(R("EL", 8, 72, 8), BC("B"), 1.0, None, A.mult)
@@ -252,36 +251,37 @@ def make_plan(est):
     scaled("HI", "I", 0.5)
     scaled("NH", "I", -0.5)
     tt(K("NDS"), K("I"), K("SD"), A.subtract)
-    tt(K("YAh"), K("I"), K("SD"), A.add)
-    scaled("YAh", "YAh", 0.5)
-    scaled("ND2", "NDS", 2.0)
-    scaled("DSh", "NDS", -0.5)
     scaled("SD64", "SD", 64.0)
     scaled("Ie", "I", 1.0 / 4096)
     scaled("I16", "I", 16.0)
-    odd = lambda nm: R(nm, 1, 128, 2)
-    for out, src, x in ((R("PO", 0, 128), K("SH"), -128.0), (R("PO", 128, 192), odd("I"), -128.0), (R("PG", 0, 64), odd("NDS"), -256.0),
-                        (R("PG", 64, 192, 2), odd("NDS"), 256.0), (R("PG", 65, 192, 2), odd("NDS"), 256.0),
-                        (R("PS", 0, 128, 2), odd("I"), 128.0), (R("PS", 1, 128, 2), odd("I"), 128.0), (R("PS", 128, 192), odd("I"), -128.0),
-                        (R("PS", 192, 320), R("PS", 0, 128), -1.0)):
+    even, odd = lambda nm: R(nm, 0, 128, 2), lambda nm: R(nm, 1, 128, 2)
+    tt(R("OD", 0, 64), even("I"), odd("I"), A.add)
+    ms(even("DSh"), 0.0)
+    for out, src, x in ((K("PO"), K("SH"), -128.0), (R("PO", 128, 192), odd("I"), -128.0), (R("PG", 0, 64), odd("NDS"), -256.0),
+                        (even("PS"), odd("I"), 128.0), (odd("PS"), odd("I"), 128.0), (R("PS", 128, 192), R("OD", 0, 64), -128.0),
+                        (R("PS", 192, 320, 2), odd("NDS"), -128.0), (R("PS", 193, 320, 2), odd("NDS"), -128.0),
+                        (odd("DSh"), odd("NDS"), -0.5), (odd("YAh"), R("OD", 0, 64), 0.5), (even("YAh"), even("I"), 1.0),
+                        (odd("IO"), odd("I"), 1.0), (even("IO"), odd("I"), 4.0),
+                        (odd("ND2"), odd("NDS"), 2.0), (even("ND2"), odd("NDS"), 8.0)):
         act(out, src, F.Copy, scale=x)
-    tt(R("PO", 192, 320), R("PO", 0, 128), R("PS", 0, 128), A.add)
-    ms(R("init", 0, 192), 0.0)
-    ms(R("init", 192, 320), -1.0)
+    ts(K("OD"), K("R15"), -128.0, None, A.mult)
+    tt(R("PS", 192, 320), R("PS", 192, 320), K("OD"), A.add)
 
     X = R("xw", 0, 2560)
-    sends = {}
 
-    def gathers(c, lst, e, d, a, w, u, even, odd, cuts):
+    def gathers(c, lst, e, d, a, w, u, even, odd, cuts, k=8):
         v0 = 1024 * c
-        pc = lambda nm, x, z, s=0: R(nm, v0 + x + s, v0 + z + s)
+        pc = lambda nm, x, z: R(nm, v0 + x, v0 + z)
+        p7 = lambda nm, x, z, s=0: R(nm, v0 + x + s, v0 + z + s - 1)
+        w7 = lambda h, x=0, z=512: R(W(c, h), x, z - 1)
+        pa = p7 if k == 7 else pc
         rest = []
         for h in range(2):
-            x, z = 512 * h, 512 * h + 511
+            x, z = 512 * h, 512 * h + 512
             for y0, y1 in zip(cuts, cuts[1:]):
                 if y0 // 512 == h:
                     act(pc(e, y0, y1), ind(X, R(lst[0], lst[1] + y0 // 16, lst[1] + y1 // 16)), F.Copy)
-            o = grp(R(W(c, h), 0, 511), ("I", pc(e, x, z, 1)), ("NI", pc(e, x, z)), ("NI", pc(d, x, z)))
+            o = grp(w7(h), ("I", p7(e, x, z, 1)), ("NI", p7(e, x, z)), ("NI", p7(d, x, z)))
             if u or odd == "V":
                 mm(o[0], o[1][:4] + (True,))
                 rest.append(o)
@@ -289,23 +289,28 @@ def make_plan(est):
                 mm(*o[:2])
                 rest.append(o[2:])
             if u:
-                act(pc(u, x, z), R(W(c, h), 0, 511), F.Abs)
+                act(p7(u, x, z), w7(h), F.Abs)
         for y0, y1 in zip(cuts, cuts[1:]):
             h = y0 // 512
             tt(pc(d, y0, y1), ind(X, R(lst[0], lst[1] + 64 + y0 // 16, lst[1] + 64 + y1 // 16)), pc(e, y0, y1), A.subtract)
             if odd == "V":
-                tt(pc(w, y0, y1 - 1), R(W(c, h), y0 - 512 * h, y1 - 1 - 512 * h), pc(d, y0, y1 - 1), A.max)
+                tt(p7(w, y0, y1), w7(h, y0 - 512 * h, y1 - 512 * h), p7(d, y0, y1), A.max)
             elif y1 % 512 == 0:
                 mm(*rest[h])
-                act(pc(w, y1 - 512, y1 - 1), R(W(c, h), 0, 511), F.Abs)
+                act(p7(w, y1 - 512, y1), w7(h), F.Abs)
             if even == "S":
-                act(pc(a, y0, y1), pc(d, y0, y1), F.Abs)
+                act(pa(a, y0, y1), pa(d, y0, y1), F.Abs)
             else:
-                ts(pc(a, y0, y1), pc(d, y0, y1), 0.0, None, A.max)
+                ts(pa(a, y0, y1), pa(d, y0, y1), 0.0, None, A.max)
 
     def FL(name, t, c, i):
-        a = 1024 * t + 512 * c + 128 * i
+        a = 768 * t + 384 * c + 128 * i
         return R(name, a, a + 128)
+
+    def shortcut(c, r3, sg):
+        mm(*(grp(Lb(c, 128, 256), ("DSh", r3)) + grp(Lb(c, 256, 384), ("YAh", r3))))
+        tt(G("t4", c), Lb(c, 128, 256), sg, A.mult)
+        tt(G("so", c), Lb(c, 256, 384), G("t4", c), A.subtract)
 
     def send(t, c, src, dst, kind):
         sends[t, c].append(op("q", "send", (src, dst, "%s%d_%d" % (kind, t + 1, c)), [src], [], 1.0))
@@ -342,17 +347,23 @@ def make_plan(est):
                 ts(G("f", c), Sb(c, 0, 128), 34.5, None, A.is_gt)
             else:
                 for o in sends[t - 1, c]:
-                    op("n", "arr", (), [], [o["args"][1]], 0.0, sem=o["args"][2], tdep=(o, NET))
-                ow, g3, sg, rin = [FL("fr", t - 1, c, i) for i in range(4)]
+                    op("n", "arr", (), [], [o["args"][1]], 0.0, sem=o["args"][2], tdep=(o, NET + est["LINK"] * size(o["args"][1])))
+                ow, r3, sg = [FL("fr", t - 1, c, i) for i in range(3)]
+                rin = G("so", c)
                 gathers(c, R("lst", l0, l0 + n), "e1", "d1", "a1", "w1", "u1", EVEN1[c], ODD1[c], CUT1)
+                shortcut(c, r3, sg)
                 pe, pd, pa, pw = steps(c, "e1", "d1", "a1", "w1", EVEN1[c], ODD1[c], 8, True)
-                group(Sb(c, 0, 320), [[("one", R("init", 0, 320))], pe, sums(c, "u1", range(7), lambda m: 128 + m, 8), pd, pa, pw,
-                                      [(g3, R("PG", 0, 192), Sb(c, 128, 320)), (ow, R("PO", 0, 320))], [(sg, R("PS", 0, 320))]])
+                group(Sb(c, 0, 320), [[] if NOINIT else [("I", R("zero", 0, 320))], pe, sums(c, "u1", range(7), lambda m: 128 + m, 8), pd, pa, pw,
+                                      [(ow, K("PO"), Sb(c, x, x + 128)) for x in (0, 192)], [(sg, R("PS", 0, 320))]])
                 a = 320 * c
                 ts(R("bn", a, a + 320), Sb(c, 0, 320), 290.5, None, A.is_gt)
-                mm(*grp(Lb(c, 0, 128), ("I", R("bn", a, a + 128)), ("I", R("bn", a + 128, a + 192), Lb(c, 1, 128, 2)),
-                        ("I", R("bn", a + 192, a + 320, 2), Lb(c, 1, 128, 2)), ("I", R("bn", a + 193, a + 320, 2), Lb(c, 1, 128, 2))))
-                ts(G("f", c), Lb(c, 0, 128), 0.0)
+                o = R(W(c, 0), 1, 128, 2)
+                mm(*grp(K(W(c, 0)), ("I", R("bn", a, a + 128)), ("I", R("bn", a + 128, a + 192), o),
+                        ("I", R("bn", a + 192, a + 320, 2), o), ("I", R("bn", a + 193, a + 320, 2), o)))
+                if FS:
+                    act(G("f", c), K(W(c, 0)), F.Copy)
+                else:
+                    ts(G("f", c), K(W(c, 0)), 0.0)
             scan(GP("x1", c, 0), G("f", c), K("sg1"), 0.0, A.max, A.mult)
             group(Sb(c, 128, 256), [[("I", rin), (G("f", c), "I8k")], [(GP("x1", c, 1), "N16k")]])
             ts(G("q", c), Sb(c, 128, 256), 2048.0, -8192.0, A.max, A.add)
@@ -380,66 +391,57 @@ def make_plan(est):
         ts(K("e3"), Sb(0, 384, 512), 0.0, None, A.is_equal)
         mm(*grp(Sb(0, 0, 16), ("I", H("hf")), *[(T1("MH", s), R("e3", 16 * s, 16 * s + 16)) for s in range(8)]))
         ts(R("off", 0, 32, 2), Sb(0, 0, 16), R("col", 4, 5), None, A.min)
-        if not last:
-            act(H("sk"), H("hf"), F.Sign, bias=1500.0, scale=-1.0)
-            mm(*grp(Sb(0, 16, 32), ("half", H("sk"))))
-            act(H("kj"), Sb(0, 16, 32), F.Identity, bias=1023.5078125 / 16, acc=R("kc", t + 1, t + 2))
-        else:
+        if last:
             act(R("cy", 0, 1024), R("cc", 0, 1024), F.Identity, bias=1280.0)
         for c in range(NC - 1, -1, -1):
             cur[0] = c
             for h in range(2):
-                e = W(c, 1) if h else "b%d" % (4 * c + 2)
+                e = W(c, h)
                 mm(*sum([grp(T1(e, s), (T1("DD", 4 * h + s), G("r2", c))) for s in range(4)], []))
-                em = R("em", 1024 * c + 512 * h, 1024 * c + 512 * h + 512)
-                if EM[c][h] == "V":
-                    ts(em, R(e, 0, 512), 0.0, 1.0 / 256 if "S" in EM[c] else 1.0, A.is_equal, A.mult)
-                else:
-                    act(em, R(e, 0, 512), F.Sigmoid, bias=R("col", 5, 6), scale=128.0)
+                ts(R("em", 1024 * c + 512 * h, 1024 * c + 512 * h + 512), R(e, 0, 512), 0.0, None, A.is_equal)
             l0 = 256 * t + n * c
-            ow, g3, sg, so = [FL("fs", t, c, i) for i in range(4)]
-            gathers(c, R("l2", l0, l0 + n), "e2", "d2", "a2", "w2", "u2", EVEN2[c], ODD2[c], CUT2)
+            ow, r3, sg = [FL("fs", t, c, i) for i in range(3)]
+            g3 = G("g3", c)
+            gathers(c, R("l2", l0, l0 + n), "e2", "d2", "a2", "w2", "u2", EVEN2[c], ODD2[c], CUT2, 7)
             ml = [(T1("ML", s), T1("em", 8 * c + s)) for s in range(8)]
-            if "S" in EM[c]:
-                mm(*grp(Lb(c, 0, 128), ("Ie", R("CC", 272, 400)), *ml))
-                ts(G("gi", c), Lb(c, 0, 128), -0.496)
-                tt(g3, Lb(c, 0, 128), G("gi", c), A.is_gt)
-            else:
-                mm(*grp(Lb(c, 0, 128), *ml))
-                act(g3, Lb(c, 0, 128), F.Sign)
+            group(Lb(c, 0, 128), [ml[:4], ml[4:]])
+            act(g3, Lb(c, 0, 128), F.Sign)
             mm(*grp(Lb(c, 128, 256), ("NDS", g3)))
             tt(G("qd", c), Lb(c, 128, 256), G("r2", c), A.mult)
-            mm(*(grp(Lb(c, 256, 384), ("HB", G("qd", c)), ("NH", G("r2", c))) +
-                 grp(Lb(c, 384, 512), ("HB", G("qd", c)), ("HI", G("r2", c)))))
+            mm(*grp(Lb(c, 256, 384), ("NH", G("r2", c)), ("HB", G("qd", c))))
             ts(G("eq", c), Lb(c, 256, 384), 0.0, None, A.is_equal)
-            mm(*grp(Lb(c, 0, 128), ("UI", G("eq", c)), ("SD64", g3)))
+            mm(*grp(Lb(c, 0, 128), ("SD64", g3), ("UI", G("eq", c))))
+            mm(*grp(Lb(c, 384, 512), ("HB", G("qd", c)), ("HI", G("r2", c))))
             act(ow, Lb(c, 0, 128), F.Sign, bias=-64.5)
             both = lambda nm, i, k: R(nm, FL(nm, t, c, i)[1], FL(nm, t, c, k)[2])
+            tt(G("t3", c), Lb(c, 256, 384), ow, A.mult)
+            tt(r3, Lb(c, 384, 512), G("t3", c), A.add)
             if SPLIT and not last:
                 send(t, c, both("fs", 0, 1), both("fr", 0, 1), "m")
-            tt(G("t3", c), Lb(c, 256, 384), ow, A.mult)
-            tt(G("r3", c), Lb(c, 384, 512), G("t3", c), A.add)
-            mm(*(grp(Lb(c, 128, 256), ("DSh", G("r3", c))) + grp(Lb(c, 256, 384), ("YAh", G("r3", c)))))
             pe, pd, pa, pw = steps(c, "e2", "d2", "a2", "w2", EVEN2[c], ODD2[c], 7)
             pen = [(ow, R("PO", 0, 192)), (g3, R("PG", 0, 64), Sb(c, 128, 192))]
-            group(Sb(c, 0, 192), [[("I", R("zero", 0, 192))], pe, sums(c, "u2", range(7), lambda m: 128 + m, 8), pd, pa] +
+            group(Sb(c, 0, 192), [[] if NOINIT else [("I", R("zero", 0, 192))], pe, sums(c, "u2", range(7), lambda m: 128 + m, 8), pd, pa] +
                   ([pw, pen] if PENLAST else [pen, pw]))
             ts(GP("f2", c, 0), Sb(c, 0, 128), 162.5, -4096.0, A.is_le, A.mult)
             ts(R("fz", n * c + 1, n * c + n, 2), Sb(c, 128, 192), 162.5, None, A.is_gt)
-            group(Lb(c, 0, 128), [[("I", ow), ("ND2", g3)], [(GP("f2", c, 1), "Ie"), (GP("f2", c, 0), "Ie")], [(G("fz", c), "I16")]])
+            group(Lb(c, 0, 128), [[("IO", ow), ("ND2", g3)], [(GP("f2", c, 1), "Ie"), (GP("f2", c, 0), "Ie")], [(G("fz", c), "I16")]])
             act(sg, Lb(c, 0, 128), F.Sign, bias=R("col", 3, 4))
-            tt(G("t4", c), Lb(c, 128, 256), sg, A.mult)
-            tt(so, Lb(c, 256, 384), G("t4", c), A.subtract)
             if not last:
-                send(t, c, both("fs", 2 * SPLIT, 3), both("fr", 2 * SPLIT, 3), "o")
+                send(t, c, both("fs", 2 * SPLIT, 2), both("fr", 2 * SPLIT, 2), "o")
             else:
-                act(G("yo", c), so, F.Identity, bias=1280.0)
+                shortcut(c, r3, sg)
+                act(G("yo", c), G("so", c), F.Identity, bias=1280.0)
                 dma("oy%d" % c, ("T", "yr", n * c, n * c + n), G("yo", c), [G("yo", c)], [], 2.0)
+            if c == 0 and not last:
+                act(H("sk"), H("hf"), F.Sign, bias=1500.0, scale=-1.0)
+                mm(*grp(Sb(0, 192, 208), ("half", H("sk"))))
+                act(H("kj"), Sb(0, 192, 208), F.Identity, bias=1023.5078125 / 16, acc=R("kc", t + 1, t + 2))
             scan(GP("x2", c, 0), GP("f2", c, 0), K("sg2"), -4096.0, A.max, A.min)
-            mm(*grp(Lb(c, 384, 512), (G("r3", c), "I"), ("one", C32), ("NI", GP("x2", c, 1))))
-            scan(G("sf", c), GP("x2", c, 1), Lb(c, 384, 512), 0.0, A.add, A.max)
-            mm(*grp(Lb(c, 0, 128), (G("sf", c), "I")))
-            act(G("sv", c), Lb(c, 0, 128), F.Identity, bias=1280.0 if last else 0.0)
+            x, z = (K(W(c, 0)), K(W(c, 1))) if last else (Sb(c, 256, 384), Sb(c, 384, 512))
+            group(x, [[(r3, "I"), ("one", C32)], [("NI", GP("x2", c, 1))]])
+            scan(G("sf", c), GP("x2", c, 1), x, 0.0, A.add, A.max)
+            mm(*grp(z, (G("sf", c), "I")))
+            act(G("sv", c), z, F.Identity, bias=1280.0 if last else 0.0)
             for j in range(8 * c + 7, 8 * c - 1, -1):
                 scatter(R("cy" if last else "cc", 0, CW), R("off", 2 * j, 2 * j + 1), R("sv", 16 * j, 16 * j + 16))
     dma("oc", ("T", "yc", 0, 1024), R("cy", 0, 1024), [R("cy", 0, 1024)], [], 4.0)
@@ -466,7 +468,7 @@ def link(ops):
                     dep.add(po["i"])
         for r, wr in acc:
             name, a, b = r[0], r[1], r[2]
-            full = wr and (len(r) < 4 or r[3][-1].step == 1) and SCRATCH[name][0] != "psum"
+            full = wr and (len(r) < 4 or r[3][-1].step == 1) and len(r) < 5 and SCRATCH[name][0] != "psum"
             keep = [e for e in seen.get(name, ()) if e[3] is o or not (full and a <= e[0] and e[1] <= b)]
             if SCRATCH[name][0] == "psum":
                 keep = keep[-12:]
@@ -567,6 +569,20 @@ def improve(ops, est, tries):
             pred[o["i"]].append((d, lat))
             succ[d].append((o["i"], lat))
 
+    slow = [o["cost"] for o in make_plan(dict(est, **SLOW))]
+
+    def replay(st):
+        end, free = [0.0] * N, {}
+        for i in sorted(range(N), key=lambda k: (st[k], k)):
+            o = ops[i]
+            s = free.get(o["q"], 0.0) if o["hold"] else 0.0
+            for d, lat in pred[i]:
+                if end[d] + lat > s:
+                    s = end[d] + lat
+            end[i] = s + slow[i]
+            free[o["q"]] = s + (slow[i] if o["hold"] == o["cost"] else o["hold"])
+        return max(end)
+
     def passes(key, k):
         best = None
         for j in range(k):
@@ -575,7 +591,7 @@ def improve(ops, est, tries):
                 best = (max(end), st)
             if j < k - 1:
                 key = [-e for e in place(ops, succ, [-e for e in end], True)[1]]
-        return best
+        return (math.sqrt(best[0] * replay(best[1]) / 1.4), best[1])
 
     seed = [1]
 
@@ -638,9 +654,13 @@ PLAN = {}
 
 def plan():
     if not PLAN:
-        ops = make_plan(EST)
-        link(ops)
-        order, total, busy = schedule(ops, EST)
+        first = []
+        for lead in LEADS:
+            ops = make_plan(dict(EST, LEAD=lead))
+            link(ops)
+            busy = schedule(ops, EST)[2]
+            first.append((improve(ops, EST, TRIES // 20)[1], lead, ops))
+        ops = min(first, key=lambda x: x[:2])[2]
         order, total = improve(ops, EST, TRIES)
         PLAN.update(ops=ops, order=order, cnt=waits(ops, order), total=total, busy=busy)
     return PLAN

@@ -7,12 +7,13 @@ n = 128
 ROUNDS = 5
 CW = 1152
 LEADS = (0.0, 3.0, 5.0, 7.0, 9.0)
-TRIES = 3000
+TRIES = 4000
 EVEN1, EVEN2 = "SV", "SS"
 SPLIT = 1
 ODD0, ODD1, ODD2 = "PP", "PP", "VV"
 CUT1 = CUT2 = [0, 512, 1024]
-FS = 1
+HS = 0
+L2ONE = 0
 NOINIT = 0
 INORDER = False
 PENLAST = True
@@ -27,17 +28,17 @@ SCRATCH = {
     "BB": ("sbuf", [128, 60], b16),
     "em": ("sbuf", [128, 2048], b16), "yo": ("sbuf", [128, 256], f32), "sv": ("sbuf", [128, 256], f32),
     "t3": ("sbuf", [128, 256], f32), "t4": ("sbuf", [128, 256], f32),
-    "rr": ("sbuf", [128, 16 * ROUNDS], f32), "w": ("sbuf", [128, 16], f32), "hi": ("sbuf", [128, 16], i32),
-    "hj": ("sbuf", [128, 16], i32), "hl": ("sbuf", [128, 16], u16), "hf": ("sbuf", [128, 16], f16),
+    "rr": ("sbuf", [128, 256 * ROUNDS], f32), "w": ("sbuf", [128, 256], f32), "hi": ("sbuf", [128, 256], i32),
+    "hj": ("sbuf", [128, 256], i32), "hl": ("sbuf", [128, 16], u16), "hf": ("sbuf", [128, 16], f16),
     "e3": ("sbuf", [128, 128], b16), "sk": ("sbuf", [128, 16], b16), "off": ("sbuf", [128, 32], u16),
     "kc": ("sbuf", [128, ROUNDS], f32), "kj": ("sbuf", [128, 16], f32), "col": ("sbuf", [128, 8], f32),
     "j256": ("sbuf", [128, 256], b16), "ki": ("sbuf", [128, 4], i32), "Iz": ("sbuf", [128, 272], b16),
     "zero": ("sbuf", [128, 320], b16), "EL": ("sbuf", [128, 72], b16),
-    "CC": ("sbuf", [128, 264], b16),
+    "CC": ("sbuf", [128, 264], b16), "W16": ("sbuf", [128, 2048], b16),
 }
 for _k in ("e1", "d1", "a1", "w1", "u1", "e2", "d2", "a2", "w2", "u2"):
     SCRATCH[_k] = ("sbuf", [128, 2048], b16)
-for _k in ("q", "ym", "aa", "cm", "r2", "qd", "so", "sf"):
+for _k in ("q", "hn", "aa", "cm", "r2", "qd", "so", "sf"):
     SCRATCH[_k] = ("sbuf", [128, 256], f16)
 for _k in ("f", "eq", "fz", "g3"):
     SCRATCH[_k] = ("sbuf", [128, 256], b16)
@@ -45,7 +46,7 @@ for _k in ("x1", "f2", "x2"):
     SCRATCH[_k] = ("sbuf", [128, 272], b16)
 for _k in ("B8", "UP", "UW", "DD", "ML", "MH"):
     SCRATCH[_k] = ("sbuf", [128, 1024], b16)
-for _k in ("one", "km", "B", "I", "NI", "LI", "UI", "SH", "SD", "I8k", "N16k", "M16", "R15", "HB", "HI", "NH", "NDS", "ND2",
+for _k in ("one", "km", "B", "I", "NI", "LI", "UI", "SH", "SD", "I8k", "N16k", "R15", "HB", "HI", "NH", "NDS", "ND2",
            "SD64", "DSh", "YAh", "Ie", "I16", "IO", "OD", "sg1", "sg2", "half"):
     SCRATCH[_k] = ("sbuf", [128, 128], b16)
 for _k in range(8):
@@ -54,7 +55,7 @@ SEMAPHORES = ["v", "s", "p", "q", "sent", "ar", "dr", "dx", "dc", "oy0", "oy1", 
     ["%s%d_%d" % (k, t, c) for k in "emo" for t in range(1, ROUNDS) for c in range(NC)]
 WIDE = set(k for k in SCRATCH if SCRATCH[k][2] in (f32, i32))
 
-EST = dict(CY=0.00083, PE=0.00042, GA=1.56, SC=3.5, WAKE=0.2, OWN=0.1, NET=4.5, LINK=0.004, LEAD=7.0)
+EST = dict(CY=0.00083, PE=0.00042, GA=1.56, SC=3.5, WAKE=0.28, OWN=0.13, NET=4.8, LINK=0.004, LEAD=7.0)
 SLOW = dict(CY=0.00125, PE=0.00062, GA=2.0, SC=5.0)
 
 
@@ -151,16 +152,19 @@ def make_plan(est):
     boost(1000, iota(R("ki", 0, 1), [[0, 1]], 0, 1))
     boost(900, iota(R("j256", 0, 256), [[-1, 256]], 0, 0))
     boost(800, iota(K("km"), [[-32, 8], [-1, 16]], 0, 0))
-    boost(700, iota(K("M16"), [[0, 8], [-1, 16]], 0, 0))
     boost(600, iota(R("B8", 0, 1024), [[-1, 8], [-32, 8], [-1, 16]], -1, 0))
     ts(R("ki", 1, 2), R("ki", 0, 1), 15, None, A.bitwise_and)
     ts(col(6), R("ki", 1, 2), 0.0)
     ts(col(7), R("ki", 0, 1), 2.0, col(6), A.mult, A.subtract)
     ts(col(4), R("ki", 0, 1), 1024.0)
+    tt(col(5), col(7), col(6), A.subtract)
+    for h in range(2):
+        a = R("W16", 1024 * h, 1024 * h + 1024)
+        boost(500, iota(a, [[1, 8], [-32, 8], [-1, 16]], 8 * h, 0))
+        ts(a, a, col(5), 0.0, A.add, A.is_equal)
     ms(K("one"), 1.0)
     ms(R("Iz", 0, 16), 0.0)
     ts(R("Iz", 16, 272), R("j256", 0, 256), col(7), 0.0, A.add, A.is_equal)
-    ts(K("M16"), K("M16"), col(6), 0.0, A.add, A.is_equal)
     for nm, x in (("I", 0.0), ("SH", 1.0), ("SD", -1.0)):
         ts(K(nm), K("km"), col(7), x, A.add, A.is_equal)
     ts(K("km"), K("km"), col(7))
@@ -170,7 +174,7 @@ def make_plan(est):
     PZ = lambda j, i: R("Iz", 16 - 16 * j + i, 272 - 16 * j, 2)
     T1 = lambda nm, s: R(nm, 128 * s, 128 * s + 128)
     BC = lambda nm: R(nm, 0, 128, 16)
-    C720, C32, C10 = R("CC", 0, 128), R("CC", 128, 256), R("CC", 256, 264)
+    C10, C32, C720 = R("CC", 0, 128), R("CC", 128, 256), R("CC", 256, 264)
 
     def W(c, h):
         return "b%d" % (4 * c + h)
@@ -190,10 +194,6 @@ def make_plan(est):
     def to_list(out, src, i):
         return grp(out, *[(PZ(j, i), R(src[0], src[1] + j, src[2], 2)) for j in range(2)])
 
-    def lanes(c, bc):
-        tt(G("ym", c), bc, K("M16"), A.mult)
-        mm(*grp(Sb(c, 0, 8), (G("ym", c), BC("B")), ("one", C10)))
-
     ts(R("rf", 0, 256), R("ri", 0, 256), -1280.0)
     for c in range(NC - 1, -1, -1):
         mm(*(to_list(Lb(c, 0, 64), G("rf", c), 0) + to_list(Lb(c, 64, 128), G("rf", c), 1)))
@@ -205,12 +205,10 @@ def make_plan(est):
     ts(col(0), col(6), 15.0, None, A.is_equal)
     ts(col(3), col(0), 99.5, 0.5, A.mult, A.add)
     ts(K("R15"), K("B"), col(0), None, A.mult)
-    for c in range(NC):
-        mm(*grp(Sb(c, 384, 512), (G("rf", c), "R15")))
-        lanes(c, Sb(c, 384, 512))
-        ts(R("rr", 8 * c, 8 * c + 8), Sb(c, 0, 8), 1.0 / 64, 1.0, A.mult, A.add)
-    op("q", "rsend", (), [R("rr", 0, 16)], [], 1.5)
-    op("n", "arr", (), [], [R("rr", 16, 16 * ROUNDS)], 0.0, sem="ar", tdep=(ops[-1], NET))
+    mm(*grp(Sb(0, 0, 256), ("R15", R("rf", 0, 256))))
+    ts(R("rr", 0, 256), Sb(0, 0, 256), 1.0 / 64, 21.0, A.mult, A.add)
+    op("q", "rsend", (), [R("rr", 0, 256)], [], 1.5)
+    op("n", "arr", (), [], [R("rr", 256, 256 * ROUNDS)], 0.0, sem="ar", tdep=(ops[-1], NET + 8.0))
     ms(R("BB", 0, 60), 0.0)
     for i, x in enumerate((1.0, 2.0, -1.0)):
         for a in (0, 12):
@@ -312,6 +310,16 @@ def make_plan(est):
         tt(G("t4", c), Lb(c, 128, 256), sg, A.mult)
         tt(G("so", c), Lb(c, 256, 384), G("t4", c), A.subtract)
 
+    def hashes(t, c, r3):
+        mm(*grp(Lb(c, 0, 128), ("one", C10), ("I", r3)))
+        tt(G("w", c), Lb(c, 0, 128), R("rr", 256 * t + n * c, 256 * t + n * c + n), A.mult)
+        ts(G("hi", c), G("w", c), R("kc", t, t + 1))
+        ts(G("hj", c), G("hi", c), 1023, None, A.bitwise_and)
+        if HS:
+            act(G("hn", c), G("hj", c), F.Copy)
+        else:
+            ts(G("hn", c), G("hj", c), 0.0)
+
     def send(t, c, src, dst, kind):
         sends[t, c].append(op("q", "send", (src, dst, "%s%d_%d" % (kind, t + 1, c)), [src], [], 1.0))
 
@@ -342,6 +350,7 @@ def make_plan(est):
             l0 = 256 * t + n * c
             if t == 0:
                 rin = G("rf", c)
+                hashes(t, c, rin)
                 gathers(c, R("lst", l0, l0 + n), "e1", "d1", "a1", "w1", None, EVEN1[c], ODD0[c], CUT1)
                 group(Sb(c, 0, 128), [[("I", R("zero", 0, 128))]] + steps(c, "e1", "d1", "a1", "w1", EVEN1[c], ODD0[c], 8))
                 ts(G("f", c), Sb(c, 0, 128), 34.5, None, A.is_gt)
@@ -351,42 +360,41 @@ def make_plan(est):
                 ow, r3, sg = [FL("fr", t - 1, c, i) for i in range(3)]
                 rin = G("so", c)
                 gathers(c, R("lst", l0, l0 + n), "e1", "d1", "a1", "w1", "u1", EVEN1[c], ODD1[c], CUT1)
+                hashes(t, c, r3)
                 shortcut(c, r3, sg)
                 pe, pd, pa, pw = steps(c, "e1", "d1", "a1", "w1", EVEN1[c], ODD1[c], 8, True)
                 group(Sb(c, 0, 320), [[] if NOINIT else [("I", R("zero", 0, 320))], pe, sums(c, "u1", range(7), lambda m: 128 + m, 8), pd, pa, pw,
                                       [(ow, K("PO"), Sb(c, x, x + 128)) for x in (0, 192)], [(sg, R("PS", 0, 320))]])
                 a = 320 * c
                 ts(R("bn", a, a + 320), Sb(c, 0, 320), 290.5, None, A.is_gt)
-                o = R(W(c, 0), 1, 128, 2)
-                mm(*grp(K(W(c, 0)), ("I", R("bn", a, a + 128)), ("I", R("bn", a + 128, a + 192), o),
-                        ("I", R("bn", a + 192, a + 320, 2), o), ("I", R("bn", a + 193, a + 320, 2), o)))
-                if FS:
-                    act(G("f", c), K(W(c, 0)), F.Copy)
-                else:
-                    ts(G("f", c), K(W(c, 0)), 0.0)
-            scan(GP("x1", c, 0), G("f", c), K("sg1"), 0.0, A.max, A.mult)
-            group(Sb(c, 128, 256), [[("I", rin), (G("f", c), "I8k")], [(GP("x1", c, 1), "N16k")]])
+                for h in range(2):
+                    o = R(W(c, h), 1 - h, 128, 2)
+                    mm(*grp(K(W(c, h)), ("I", R("bn", a, a + 128)), ("I", R("bn", a + 128, a + 192), o),
+                            ("I", R("bn", a + 192, a + 320, 2), o), ("I", R("bn", a + 193, a + 320, 2), o)))
+                act(G("f", c), K(W(c, 1)), F.Copy)
+            scan(GP("x1", c, 0), K(W(c, 0)) if t else G("f", c), K("sg1"), 0.0, A.max, A.mult)
+            group(Sb(c, 128, 256), [[("I", G("hn", c)), (G("f", c), "I8k")], [(GP("x1", c, 1), "N16k")]])
             ts(G("q", c), Sb(c, 128, 256), 2048.0, -8192.0, A.max, A.add)
-            mm(*grp(Sb(c, 384, 512), ("one", C720), (G("q", c), "B")))
-            lanes(c, Sb(c, 384, 512))
+            mm(*grp(Sb(c, 0, 8), ("one", C720), *[(T1("W16", j), R("q", n * c + j, n * c + n, 16)) for j in range(16)]))
             l8 = lambda nm: R(nm, 8 * c, 8 * c + 8)
-            tt(l8("w"), Sb(c, 0, 8), R("rr", 16 * t + 8 * c, 16 * t + 8 * c + 8), A.mult)
+            ts(l8("hl"), Sb(c, 0, 8), 0.0)
+            act(l8("hf"), Sb(c, 0, 8), F.Abs)
             mm(*grp(Lb(c, 256, 384), (GP("x1", c, 1), "I8k"), ("I", rin)))
             act(G("aa", c), Lb(c, 256, 384), F.Identity, bias=4096.0, scale=-1.0)
-            ts(l8("hi"), l8("w"), R("kc", t, t + 1))
-            ts(l8("hj"), l8("hi"), 1023 + 2 ** 23, None, A.bitwise_and)
-            ts(l8("hl"), l8("hj"), 1023.0, None, A.min)
             tt(G("cm", c), ind(R("cc", 0, 1024), l8("hl")), G("aa", c), A.max)
             tt(G("r2", c), Lb(c, 256, 384), G("cm", c), A.min)
             for i in range(2):
                 mm(*to_list(Sb(c, 128 + 64 * i, 192 + 64 * i), G("r2", c), i))
-            for i in range(2):
-                ts(R("l2", l0 + 64 * i, l0 + 64 * i + 64), Sb(c, 128 + 64 * i, 192 + 64 * i), 1280.0)
+            for x, z in ((0, 128),) if L2ONE else ((0, 64), (64, 128)):
+                ts(R("l2", l0 + x, l0 + z), Sb(c, 128 + x, 128 + z), 1280.0)
             sends[t, c] = []
             if not last:
                 send(t, c, R("l2", l0, l0 + n), R("lst", l0 + 256, l0 + 256 + n), "e")
         H = lambda nm: R(nm, 0, 16)
-        ts(H("hf"), H("hj"), 2048.0, None, A.min)
+        if not last:
+            act(H("sk"), H("hf"), F.Sign, bias=1500.0, scale=-1.0)
+            mm(*grp(Sb(0, 16, 32), ("half", H("sk"))))
+            act(H("kj"), Sb(0, 16, 32), F.Identity, bias=1023.5078125 / 16, acc=R("kc", t + 1, t + 2))
         mm(*sum([grp(Sb(0, 384 + 16 * s, 400 + 16 * s), (T1("DD", s), H("hf"))) for s in range(8)], []))
         ts(K("e3"), Sb(0, 384, 512), 0.0, None, A.is_equal)
         mm(*grp(Sb(0, 0, 16), ("I", H("hf")), *[(T1("MH", s), R("e3", 16 * s, 16 * s + 16)) for s in range(8)]))
@@ -432,10 +440,6 @@ def make_plan(est):
                 shortcut(c, r3, sg)
                 act(G("yo", c), G("so", c), F.Identity, bias=1280.0)
                 dma("oy%d" % c, ("T", "yr", n * c, n * c + n), G("yo", c), [G("yo", c)], [], 2.0)
-            if c == 0 and not last:
-                act(H("sk"), H("hf"), F.Sign, bias=1500.0, scale=-1.0)
-                mm(*grp(Sb(0, 192, 208), ("half", H("sk"))))
-                act(H("kj"), Sb(0, 192, 208), F.Identity, bias=1023.5078125 / 16, acc=R("kc", t + 1, t + 2))
             scan(GP("x2", c, 0), GP("f2", c, 0), K("sg2"), -4096.0, A.max, A.min)
             x, z = (K(W(c, 0)), K(W(c, 1))) if last else (Sb(c, 256, 384), Sb(c, 384, 512))
             group(x, [[(r3, "I"), ("one", C32)], [("NI", GP("x2", c, 1))]])
@@ -735,9 +739,9 @@ def rank_program(g, core, T, topo):
                 d = T.cores[(rank + 3 * t) % N]
                 rid, pid = topo.addr(d, core)
                 ids.append(DstId(rid=rid, pnc=pid))
-                dsts.append(ap(R("rr", 16 * t, 16 * t + 16)))
+                dsts.append(ap(R("rr", 256 * t, 256 * t + 256)))
             Q.remote_dma_fused([RemoteDMATransfer(dst_ids=ids, dma_engine_mask=topo.mask(core, nxt), remote_sem=T.sem["ar"],
-                                                  srcs=[ap(R("rr", 0, 16))], dsts=dsts)], local_sem=T.sem["sent"])
+                                                  srcs=[ap(R("rr", 0, 256))], dsts=dsts)], local_sem=T.sem["sent"])
             sent[0] += len(topo.engines(core, nxt))
             continue
         r.then_inc(T.sem[o["q"]], 1)

import math
from concourse.bass import DstId, RemoteDMATransfer
from concourse.mybir import dt, AluOpType as A, AxisListType, ActivationFunctionType as F

NC = 2
n = 128
ROUNDS = 5
CW = 1152
LEADS = (0.0, 3.0, 5.0, 7.0, 9.0)
TRIES = 4000
EVEN1, EVEN2 = "SV", "SS"
SPLIT = 1
ODD0, ODD1, ODD2 = "PP", "PP", "VV"
CUT1 = CUT2 = [0, 512, 1024]
HS = 0
L2ONE = 0
NOINIT = 0
INORDER = False
PENLAST = True

f16, b16, f32, i32, u16 = "float16", "bfloat16", "float32", "int32", "uint16"
SCRATCH = {
    "xw": ("sbuf", [128, 2560], b16), "ri": ("sbuf", [128, 256], i32), "ci": ("sbuf", [128, 1024], i32),
    "cc": ("sbuf", [128, CW], f32), "cy": ("sbuf", [128, CW], f32), "rf": ("sbuf", [128, 256], f16),
    "lst": ("sbuf", [128, 256 * ROUNDS], u16), "l2": ("sbuf", [128, 256 * ROUNDS], u16),
    "fs": ("sbuf", [128, 768 * ROUNDS], f16), "fr": ("sbuf", [128, 768 * ROUNDS], f16), "bn": ("sbuf", [128, 640], b16),
    "PO": ("sbuf", [128, 192], b16), "PS": ("sbuf", [128, 320], b16), "PG": ("sbuf", [128, 64], b16),
    "BB": ("sbuf", [128, 60], b16),
    "em": ("sbuf", [128, 2048], b16), "yo": ("sbuf", [128, 256], f32), "sv": ("sbuf", [128, 256], f32),
    "t3": ("sbuf", [128, 256], f32), "t4": ("sbuf", [128, 256], f32),
    "rr": ("sbuf", [128, 256 * ROUNDS], f32), "w": ("sbuf", [128, 256], f32), "hi": ("sbuf", [128, 256], i32),
    "hj": ("sbuf", [128, 256], i32), "hl": ("sbuf", [128, 16], u16), "hf": ("sbuf", [128, 16], f16),
    "e3": ("sbuf", [128, 128], b16), "sk": ("sbuf", [128, 16], b16), "off": ("sbuf", [128, 32], u16),
    "kc": ("sbuf", [128, ROUNDS], f32), "kj": ("sbuf", [128, 16], f32), "col": ("sbuf", [128, 8], f32),
    "j256": ("sbuf", [128, 256], b16), "ki": ("sbuf", [128, 4], i32), "Iz": ("sbuf", [128, 272], b16),
    "zero": ("sbuf", [128, 320], b16), "EL": ("sbuf", [128, 72], b16),
    "CC": ("sbuf", [128, 264], b16), "W16": ("sbuf", [128, 2048], b16),
}
for _k in ("e1", "d1", "a1", "w1", "u1", "e2", "d2", "a2", "w2", "u2"):
    SCRATCH[_k] = ("sbuf", [128, 2048], b16)
for _k in ("q", "hn", "aa", "cm", "r2", "qd", "so", "sf"):
    SCRATCH[_k] = ("sbuf", [128, 256], f16)
for _k in ("f", "eq", "fz", "g3"):
    SCRATCH[_k] = ("sbuf", [128, 256], b16)
for _k in ("x1", "f2", "x2"):
    SCRATCH[_k] = ("sbuf", [128, 272], b16)
for _k in ("B8", "UP", "UW", "DD", "ML", "MH"):
    SCRATCH[_k] = ("sbuf", [128, 1024], b16)
for _k in ("one", "km", "B", "I", "NI", "LI", "UI", "SH", "SD", "I8k", "N16k", "R15", "HB", "HI", "NH", "NDS", "ND2",
           "SD64", "DSh", "YAh", "Ie", "I16", "IO", "OD", "sg1", "sg2", "half"):
    SCRATCH[_k] = ("sbuf", [128, 128], b16)
for _k in range(8):
    SCRATCH["b%d" % _k] = ("psum", [128, 512], f32)
SEMAPHORES = ["v", "s", "p", "q", "sent", "ar", "dr", "dx", "dc", "oy0", "oy1", "oc"] + \
    ["%s%d_%d" % (k, t, c) for k in "emo" for t in range(1, ROUNDS) for c in range(NC)]
WIDE = set(k for k in SCRATCH if SCRATCH[k][2] in (f32, i32))

EST = dict(CY=0.00083, PE=0.00042, GA=1.56, SC=3.5, WAKE=0.28, OWN=0.13, NET=4.8, LINK=0.004, LEAD=7.0)
SLOW = dict(CY=0.00125, PE=0.00062, GA=2.0, SC=5.0)


def R(name, a, b, step=1):
    return (name, a, b, (slice(None), slice(a, b, step)))


def size(r):
    s = r[3][-1]
    return len(range(s.start, s.stop, s.step or 1))


def ind(win, off):
    return ("ind", win, off)


def isref(x):
    return isinstance(x, tuple)


def make_plan(est):
    ops, sends = [], {}
    cur = [None]
    CY, PE, GA, NET = est["CY"], est["PE"], est["GA"], est["NET"]

    def op(queue, kind, args, reads, writes, cost, **kw):
        d = dict(i=len(ops), q=queue, kind=kind, args=args, r=[], w=list(writes), cost=cost, sem=None, pb=est["LEAD"] * (cur[0] == 1),
                 c=cur[0], t=len(sends) // 2)
        for x in reads:
            if isref(x):
                d["r"] += [x[1], x[2]] if x[0] == "ind" else [x]
        d.update(kw)
        ops.append(d)
        return d

    def boost(x, o):
        o["pb"] = x

    two = lambda r: r[0] not in WIDE

    def ts(out, in0, s1, s2=None, op0=A.add, op1=None):
        c = max(64, size(in0) * (0.5 if two(out) and two(in0) else 1)) * CY
        return op("v", "ts", (out, in0, s1, s2, op0, op1), [in0, s1, s2], [out], c)

    def tt(out, in0, in1, o):
        if in0[0] == "ind":
            c = 0.05 + size(in1) * GA * CY
        else:
            c = max(64, size(in0) * (1 if in0[0][0] == "b" or in1[0][0] == "b" else 2)) * CY
        return op("v", "tt", (out, in0, in1, o), [in0, in1], [out], c)

    def scan(out, d0, d1, init, op0, op1):
        c = max(64, size(out) * (0.5 if two(out) and two(d0) and two(d1) else 1)) * CY
        return op("v", "scan", (out, d0, d1, init, op0, op1), [d0, d1], [out], c)

    def scatter(win, off, in_):
        return op("v", "cp", (ind(win, off), in_), [in_, off], [win], 0.05 + size(in_) * est["SC"] * CY)

    def ms(out, val):
        return op("v", "ms", (out, val), [], [out], max(64, size(out) * (.5 if two(out) else 1)) * CY)

    def act(out, in_, fn, bias=0.0, scale=1.0, acc=None):
        k = size(out)
        return op("s", "act", (out, in_, fn, bias, scale, acc), [in_, bias], [out] + ([acc] if acc else []),
                  (0.065 + k * GA * CY) if in_[0] == "ind" else max(64, k) * CY + (0.02 if acc else 0))

    def K(name):
        return R(name, 0, 128)

    def grp(out, *pairs):
        last = len(pairs) - 1
        kk = lambda a: K(a) if isinstance(a, str) else a
        return [(p[2] if len(p) > 2 else out, kk(p[0]), kk(p[1]), i == 0, i == last) for i, p in enumerate(pairs)]

    def mm(*mms):
        rd = []
        for m in mms:
            rd += [m[1], m[2]]
        return op("p", "mm", mms, rd, sorted(set((m[0][0], m[0][1], m[0][2]) for m in mms)), sum(max(64, size(m[2])) for m in mms) * PE)

    def iota(out, pat, base, cm):
        return op("q", "iota", (out, pat, base, cm), [], [out], 0.13 + 2 * size(out) * CY)

    def dma(sem, out, in_, reads, writes, cost):
        return op("y", "dma", (out, in_), reads, writes, cost, sem=sem)

    def scaled(out, in_, x):
        return act(K(out), K(in_), F.Copy, scale=x)

    dma("dr", R("ri", 0, 256), ("T", "r0"), [], [R("ri", 0, 256)], 2.2)
    dma("dx", R("xw", 0, 2560), ("T", "x"), [], [R("xw", 0, 2560)], 5.0)
    dma("dc", R("ci", 0, 1024), ("T", "c0"), [R("xw", 0, 2560)], [R("ci", 0, 1024)], 4.5)
    col = lambda i: R("col", i, i + 1)
    boost(1000, iota(R("ki", 0, 1), [[0, 1]], 0, 1))
    boost(900, iota(R("j256", 0, 256), [[-1, 256]], 0, 0))
    boost(800, iota(K("km"), [[-32, 8], [-1, 16]], 0, 0))
    boost(600, iota(R("B8", 0, 1024), [[-1, 8], [-32, 8], [-1, 16]], -1, 0))
    ts(R("ki", 1, 2), R("ki", 0, 1), 15, None, A.bitwise_and)
    ts(col(6), R("ki", 1, 2), 0.0)
    ts(col(7), R("ki", 0, 1), 2.0, col(6), A.mult, A.subtract)
    ts(col(4), R("ki", 0, 1), 1024.0)
    tt(col(5), col(7), col(6), A.subtract)
    for h in range(2):
        a = R("W16", 1024 * h, 1024 * h + 1024)
        boost(500, iota(a, [[1, 8], [-32, 8], [-1, 16]], 8 * h, 0))
        ts(a, a, col(5), 0.0, A.add, A.is_equal)
    ms(K("one"), 1.0)
    ms(R("Iz", 0, 16), 0.0)
    ts(R("Iz", 16, 272), R("j256", 0, 256), col(7), 0.0, A.add, A.is_equal)
    for nm, x in (("I", 0.0), ("SH", 1.0), ("SD", -1.0)):
        ts(K(nm), K("km"), col(7), x, A.add, A.is_equal)
    ts(K("km"), K("km"), col(7))
    for nm, x, z in (("B", 0.0, 16.0), ("LI", 7.5, 8.0), ("UI", -7.5, 8.0)):
        act(K(nm), K("km"), F.Abs, bias=x)
        ts(K(nm), K(nm), z, None, A.is_lt)
    PZ = lambda j, i: R("Iz", 16 - 16 * j + i, 272 - 16 * j, 2)
    T1 = lambda nm, s: R(nm, 128 * s, 128 * s + 128)
    BC = lambda nm: R(nm, 0, 128, 16)
    C10, C32, C720 = R("CC", 0, 128), R("CC", 128, 256), R("CC", 256, 264)

    def W(c, h):
        return "b%d" % (4 * c + h)

    def Lb(c, a, b, step=1):
        return R("b%d" % (4 * c + 2), a, b, step)

    def Sb(c, a, b, step=1):
        return R("b%d" % (4 * c + 3), a, b, step)

    def G(name, c):
        return R(name, n * c, n * c + n)

    def GP(name, c, shift):
        return R(name, 136 * c + 8 - shift, 136 * c + 136 - shift)

    def to_list(out, src, i):
        return grp(out, *[(PZ(j, i), R(src[0], src[1] + j, src[2], 2)) for j in range(2)])

    ts(R("rf", 0, 256), R("ri", 0, 256), -1280.0)
    for c in range(NC - 1, -1, -1):
        mm(*(to_list(Lb(c, 0, 64), G("rf", c), 0) + to_list(Lb(c, 64, 128), G("rf", c), 1)))
        ts(G("lst", c), Lb(c, 0, 128), 1280.0)
    scaled("NI", "I", -1.0)
    ms(C720, 720.0)
    ms(C32, -32.0)
    ms(C10, 10.0)
    ts(col(0), col(6), 15.0, None, A.is_equal)
    ts(col(3), col(0), 99.5, 0.5, A.mult, A.add)
    ts(K("R15"), K("B"), col(0), None, A.mult)
    mm(*grp(Sb(0, 0, 256), ("R15", R("rf", 0, 256))))
    ts(R("rr", 0, 256), Sb(0, 0, 256), 1.0 / 64, 21.0, A.mult, A.add)
    op("q", "rsend", (), [R("rr", 0, 256)], [], 1.5)
    op("n", "arr", (), [], [R("rr", 256, 256 * ROUNDS)], 0.0, sem="ar", tdep=(ops[-1], NET + 8.0))
    ms(R("BB", 0, 60), 0.0)
    for i, x in enumerate((1.0, 2.0, -1.0)):
        for a in (0, 12):
            ts(R("BB", 20 * i + a, 20 * i + a + 8), BC("B"), x, None, A.mult)
    ms(R("zero", 0, 320), 0.0)
    ms(R("EL", 0, 72), 0.0)
    ts(R("EL", 7, 71, 8), BC("B"), -1.0, None, A.mult)
    ts(R("EL", 8, 72, 8), BC("B"), 1.0, None, A.mult)
    scaled("I8k", "I", 8192.0)
    scaled("N16k", "I", -16384.0)
    ms(K("sg1"), 1.0)
    ms(K("sg2"), 0.0)
    for p in (14, 15):
        ms(R("sg1", p, 128, 16), 0.0)
        ms(R("sg2", p, 128, 16), -4096.0)
    ms(R("x1", 0, 272), 0.0)
    ms(R("f2", 0, 272), 0.0)
    ms(R("x2", 0, 272), -4096.0)
    ms(R("fz", 0, 256), 0.0)
    ms(R("kc", 0, 1), -0.4921875)
    ms(K("half"), 0.5)
    act(R("cc", 0, 1024), R("ci", 0, 1024), F.Identity, bias=-1280.0)
    ms(R("cc", 1024, CW), 0.0)
    ms(R("cy", 1024, CW), 0.0)
    ts(R("UP", 0, 1024), R("B8", 0, 1024), col(7), 0.0, A.add, A.is_equal)
    ts(R("UW", 0, 1024), R("B8", 0, 1024), col(7), -16.0, A.add, A.is_equal)
    for nm, x, banks, terms in (
            ("DD", 1.0, "b4 b5", lambda s: (("I", T1("UP", s)), ("I", T1("UW", s)), ("NI", "I"))),
            ("ML", 1.0, "b0 b1", lambda s: (("I", "LI"), (T1("UW", s), "LI"))),
            ("MH", 2048.0, "b2 b6", lambda s: ((T1("UP", s), "I"), (T1("UW", s), T1("UW", s))))):
        for h, e in enumerate(banks.split()):
            mm(*sum([grp(T1(e, i), *terms(4 * h + i)) for i in range(4)], []))
            if h:
                ts(R(nm, 512, 1024), R(e, 0, 512), x, None, A.mult)
            else:
                act(R(nm, 0, 512), R(e, 0, 512), F.Copy, scale=x)
    scaled("HB", "B", 0.5)
    scaled("HI", "I", 0.5)
    scaled("NH", "I", -0.5)
    tt(K("NDS"), K("I"), K("SD"), A.subtract)
    scaled("SD64", "SD", 64.0)
    scaled("Ie", "I", 1.0 / 4096)
    scaled("I16", "I", 16.0)
    even, odd = lambda nm: R(nm, 0, 128, 2), lambda nm: R(nm, 1, 128, 2)
    tt(R("OD", 0, 64), even("I"), odd("I"), A.add)
    ms(even("DSh"), 0.0)
    for out, src, x in ((K("PO"), K("SH"), -128.0), (R("PO", 128, 192), odd("I"), -128.0), (R("PG", 0, 64), odd("NDS"), -256.0),
                        (even("PS"), odd("I"), 128.0), (odd("PS"), odd("I"), 128.0), (R("PS", 128, 192), R("OD", 0, 64), -128.0),
                        (R("PS", 192, 320, 2), odd("NDS"), -128.0), (R("PS", 193, 320, 2), odd("NDS"), -128.0),
                        (odd("DSh"), odd("NDS"), -0.5), (odd("YAh"), R("OD", 0, 64), 0.5), (even("YAh"), even("I"), 1.0),
                        (odd("IO"), odd("I"), 1.0), (even("IO"), odd("I"), 4.0),
                        (odd("ND2"), odd("NDS"), 2.0), (even("ND2"), odd("NDS"), 8.0)):
        act(out, src, F.Copy, scale=x)
    ts(K("OD"), K("R15"), -128.0, None, A.mult)
    tt(R("PS", 192, 320), R("PS", 192, 320), K("OD"), A.add)

    X = R("xw", 0, 2560)

    def gathers(c, lst, e, d, a, w, u, even, odd, cuts, k=8):
        v0 = 1024 * c
        pc = lambda nm, x, z: R(nm, v0 + x, v0 + z)
        p7 = lambda nm, x, z, s=0: R(nm, v0 + x + s, v0 + z + s - 1)
        w7 = lambda h, x=0, z=512: R(W(c, h), x, z - 1)
        pa = p7 if k == 7 else pc
        rest = []
        for h in range(2):
            x, z = 512 * h, 512 * h + 512
            for y0, y1 in zip(cuts, cuts[1:]):
                if y0 // 512 == h:
                    act(pc(e, y0, y1), ind(X, R(lst[0], lst[1] + y0 // 16, lst[1] + y1 // 16)), F.Copy)
            o = grp(w7(h), ("I", p7(e, x, z, 1)), ("NI", p7(e, x, z)), ("NI", p7(d, x, z)))
            if u or odd == "V":
                mm(o[0], o[1][:4] + (True,))
                rest.append(o)
            else:
                mm(*o[:2])
                rest.append(o[2:])
            if u:
                act(p7(u, x, z), w7(h), F.Abs)
        for y0, y1 in zip(cuts, cuts[1:]):
            h = y0 // 512
            tt(pc(d, y0, y1), ind(X, R(lst[0], lst[1] + 64 + y0 // 16, lst[1] + 64 + y1 // 16)), pc(e, y0, y1), A.subtract)
            if odd == "V":
                tt(p7(w, y0, y1), w7(h, y0 - 512 * h, y1 - 512 * h), p7(d, y0, y1), A.max)
            elif y1 % 512 == 0:
                mm(*rest[h])
                act(p7(w, y1 - 512, y1), w7(h), F.Abs)
            if even == "S":
                act(pa(a, y0, y1), pa(d, y0, y1), F.Abs)
            else:
                ts(pa(a, y0, y1), pa(d, y0, y1), 0.0, None, A.max)

    def FL(name, t, c, i):
        a = 768 * t + 384 * c + 128 * i
        return R(name, a, a + 128)

    def shortcut(c, r3, sg):
        mm(*(grp(Lb(c, 128, 256), ("DSh", r3)) + grp(Lb(c, 256, 384), ("YAh", r3))))
        tt(G("t4", c), Lb(c, 128, 256), sg, A.mult)
        tt(G("so", c), Lb(c, 256, 384), G("t4", c), A.subtract)

    def hashes(t, c, r3):
        mm(*grp(Lb(c, 0, 128), ("one", C10), ("I", r3)))
        tt(G("w", c), Lb(c, 0, 128), R("rr", 256 * t + n * c, 256 * t + n * c + n), A.mult)
        ts(G("hi", c), G("w", c), R("kc", t, t + 1))
        ts(G("hj", c), G("hi", c), 1023, None, A.bitwise_and)
        if HS:
            act(G("hn", c), G("hj", c), F.Copy)
        else:
            ts(G("hn", c), G("hj", c), 0.0)

    def send(t, c, src, dst, kind):
        sends[t, c].append(op("q", "send", (src, dst, "%s%d_%d" % (kind, t + 1, c)), [src], [], 1.0))

    def steps(c, e, d, a, w, even, odd, k, twice=False):
        def put(src, ms_, par, x):
            z = 20 if twice else 8
            return [(R(src, 1024 * c + m, 1024 * c + 1024, 8), R("BB", 20 * x, 20 * x + z), Sb(c, 2 * m + par, 2 * m + par + 16 * z - 15, 16))
                    for m in ms_]
        pe = [(R(e, 1024 * c + m, 1024 * c + 1024, 8), R("EL", 8 - m, 72 - m), Sb(c, x + 1, x + 128, 2))
              for m in range(8) for x in ((0, 192) if twice else (0,))] if odd == "V" else []
        pd = (put(d, range(k), 0, 2) if even == "V" else []) + (put(d, range(7), 1, 2) if odd == "V" else [])
        return [pe, pd, put(a, range(k), 0, even == "V"), put(w, range(7), 1, odd == "V")]

    def group(out, parts):
        o = grp(out, *sum(parts, []))
        for p in parts:
            if p:
                mm(*o[:len(p)])
                o = o[len(p):]

    def sums(c, src, ms_, col, step, mat="B"):
        return [(R(src, 1024 * c + m, 1024 * c + 1024, 8), BC(mat), Sb(c, col(m), col(m) + 8 * step - step + 1, step)) for m in ms_]

    for t in range(ROUNDS):
        last = t == ROUNDS - 1
        for c in range(NC - 1, -1, -1):
            cur[0] = c
            l0 = 256 * t + n * c
            if t == 0:
                rin = G("rf", c)
                hashes(t, c, rin)
                gathers(c, R("lst", l0, l0 + n), "e1", "d1", "a1", "w1", None, EVEN1[c], ODD0[c], CUT1)
                group(Sb(c, 0, 128), [[("I", R("zero", 0, 128))]] + steps(c, "e1", "d1", "a1", "w1", EVEN1[c], ODD0[c], 8))
                ts(G("f", c), Sb(c, 0, 128), 34.5, None, A.is_gt)
            else:
                for o in sends[t - 1, c]:
                    op("n", "arr", (), [], [o["args"][1]], 0.0, sem=o["args"][2], tdep=(o, NET + est["LINK"] * size(o["args"][1])))
                ow, r3, sg = [FL("fr", t - 1, c, i) for i in range(3)]
                rin = G("so", c)
                gathers(c, R("lst", l0, l0 + n), "e1", "d1", "a1", "w1", "u1", EVEN1[c], ODD1[c], CUT1)
                hashes(t, c, r3)
                shortcut(c, r3, sg)
                pe, pd, pa, pw = steps(c, "e1", "d1", "a1", "w1", EVEN1[c], ODD1[c], 8, True)
                group(Sb(c, 0, 320), [[] if NOINIT else [("I", R("zero", 0, 320))], pe, sums(c, "u1", range(7), lambda m: 128 + m, 8), pd, pa, pw,
                                      [(ow, K("PO"), Sb(c, x, x + 128)) for x in (0, 192)], [(sg, R("PS", 0, 320))]])
                a = 320 * c
                ts(R("bn", a, a + 320), Sb(c, 0, 320), 290.5, None, A.is_gt)
                for h in range(2):
                    o = R(W(c, h), 1 - h, 128, 2)
                    mm(*grp(K(W(c, h)), ("I", R("bn", a, a + 128)), ("I", R("bn", a + 128, a + 192), o),
                            ("I", R("bn", a + 192, a + 320, 2), o), ("I", R("bn", a + 193, a + 320, 2), o)))
                act(G("f", c), K(W(c, 1)), F.Copy)
            scan(GP("x1", c, 0), K(W(c, 0)) if t else G("f", c), K("sg1"), 0.0, A.max, A.mult)
            group(Sb(c, 128, 256), [[("I", G("hn", c)), (G("f", c), "I8k")], [(GP("x1", c, 1), "N16k")]])
            ts(G("q", c), Sb(c, 128, 256), 2048.0, -8192.0, A.max, A.add)
            mm(*grp(Sb(c, 0, 8), ("one", C720), *[(T1("W16", j), R("q", n * c + j, n * c + n, 16)) for j in range(16)]))
            l8 = lambda nm: R(nm, 8 * c, 8 * c + 8)
            ts(l8("hl"), Sb(c, 0, 8), 0.0)
            act(l8("hf"), Sb(c, 0, 8), F.Abs)
            mm(*grp(Lb(c, 256, 384), (GP("x1", c, 1), "I8k"), ("I", rin)))
            act(G("aa", c), Lb(c, 256, 384), F.Identity, bias=4096.0, scale=-1.0)
            tt(G("cm", c), ind(R("cc", 0, 1024), l8("hl")), G("aa", c), A.max)
            tt(G("r2", c), Lb(c, 256, 384), G("cm", c), A.min)
            for i in range(2):
                mm(*to_list(Sb(c, 128 + 64 * i, 192 + 64 * i), G("r2", c), i))
            for x, z in ((0, 128),) if L2ONE else ((0, 64), (64, 128)):
                ts(R("l2", l0 + x, l0 + z), Sb(c, 128 + x, 128 + z), 1280.0)
            sends[t, c] = []
            if not last:
                send(t, c, R("l2", l0, l0 + n), R("lst", l0 + 256, l0 + 256 + n), "e")
        H = lambda nm: R(nm, 0, 16)
        if not last:
            act(H("sk"), H("hf"), F.Sign, bias=1500.0, scale=-1.0)
            mm(*grp(Sb(0, 16, 32), ("half", H("sk"))))
            act(H("kj"), Sb(0, 16, 32), F.Identity, bias=1023.5078125 / 16, acc=R("kc", t + 1, t + 2))
        mm(*sum([grp(Sb(0, 384 + 16 * s, 400 + 16 * s), (T1("DD", s), H("hf"))) for s in range(8)], []))
        ts(K("e3"), Sb(0, 384, 512), 0.0, None, A.is_equal)
        mm(*grp(Sb(0, 0, 16), ("I", H("hf")), *[(T1("MH", s), R("e3", 16 * s, 16 * s + 16)) for s in range(8)]))
        ts(R("off", 0, 32, 2), Sb(0, 0, 16), R("col", 4, 5), None, A.min)
        if last:
            act(R("cy", 0, 1024), R("cc", 0, 1024), F.Identity, bias=1280.0)
        for c in range(NC - 1, -1, -1):
            cur[0] = c
            for h in range(2):
                e = W(c, h)
                mm(*sum([grp(T1(e, s), (T1("DD", 4 * h + s), G("r2", c))) for s in range(4)], []))
                ts(R("em", 1024 * c + 512 * h, 1024 * c + 512 * h + 512), R(e, 0, 512), 0.0, None, A.is_equal)
            l0 = 256 * t + n * c
            ow, r3, sg = [FL("fs", t, c, i) for i in range(3)]
            g3 = G("g3", c)
            gathers(c, R("l2", l0, l0 + n), "e2", "d2", "a2", "w2", "u2", EVEN2[c], ODD2[c], CUT2, 7)
            ml = [(T1("ML", s), T1("em", 8 * c + s)) for s in range(8)]
            group(Lb(c, 0, 128), [ml[:4], ml[4:]])
            act(g3, Lb(c, 0, 128), F.Sign)
            mm(*grp(Lb(c, 128, 256), ("NDS", g3)))
            tt(G("qd", c), Lb(c, 128, 256), G("r2", c), A.mult)
            mm(*grp(Lb(c, 256, 384), ("NH", G("r2", c)), ("HB", G("qd", c))))
            ts(G("eq", c), Lb(c, 256, 384), 0.0, None, A.is_equal)
            mm(*grp(Lb(c, 0, 128), ("SD64", g3), ("UI", G("eq", c))))
            mm(*grp(Lb(c, 384, 512), ("HB", G("qd", c)), ("HI", G("r2", c))))
            act(ow, Lb(c, 0, 128), F.Sign, bias=-64.5)
            both = lambda nm, i, k: R(nm, FL(nm, t, c, i)[1], FL(nm, t, c, k)[2])
            tt(G("t3", c), Lb(c, 256, 384), ow, A.mult)
            tt(r3, Lb(c, 384, 512), G("t3", c), A.add)
            if SPLIT and not last:
                send(t, c, both("fs", 0, 1), both("fr", 0, 1), "m")
            pe, pd, pa, pw = steps(c, "e2", "d2", "a2", "w2", EVEN2[c], ODD2[c], 7)
            pen = [(ow, R("PO", 0, 192)), (g3, R("PG", 0, 64), Sb(c, 128, 192))]
            group(Sb(c, 0, 192), [[] if NOINIT else [("I", R("zero", 0, 192))], pe, sums(c, "u2", range(7), lambda m: 128 + m, 8), pd, pa] +
                  ([pw, pen] if PENLAST else [pen, pw]))
            ts(GP("f2", c, 0), Sb(c, 0, 128), 162.5, -4096.0, A.is_le, A.mult)
            ts(R("fz", n * c + 1, n * c + n, 2), Sb(c, 128, 192), 162.5, None, A.is_gt)
            group(Lb(c, 0, 128), [[("IO", ow), ("ND2", g3)], [(GP("f2", c, 1), "Ie"), (GP("f2", c, 0), "Ie")], [(G("fz", c), "I16")]])
            act(sg, Lb(c, 0, 128), F.Sign, bias=R("col", 3, 4))
            if not last:
                send(t, c, both("fs", 2 * SPLIT, 2), both("fr", 2 * SPLIT, 2), "o")
            else:
                shortcut(c, r3, sg)
                act(G("yo", c), G("so", c), F.Identity, bias=1280.0)
                dma("oy%d" % c, ("T", "yr", n * c, n * c + n), G("yo", c), [G("yo", c)], [], 2.0)
            scan(GP("x2", c, 0), GP("f2", c, 0), K("sg2"), -4096.0, A.max, A.min)
            x, z = (K(W(c, 0)), K(W(c, 1))) if last else (Sb(c, 256, 384), Sb(c, 384, 512))
            group(x, [[(r3, "I"), ("one", C32)], [("NI", GP("x2", c, 1))]])
            scan(G("sf", c), GP("x2", c, 1), x, 0.0, A.add, A.max)
            mm(*grp(z, (G("sf", c), "I")))
            act(G("sv", c), z, F.Identity, bias=1280.0 if last else 0.0)
            for j in range(8 * c + 7, 8 * c - 1, -1):
                scatter(R("cy" if last else "cc", 0, CW), R("off", 2 * j, 2 * j + 1), R("sv", 16 * j, 16 * j + 16))
    dma("oc", ("T", "yc", 0, 1024), R("cy", 0, 1024), [R("cy", 0, 1024)], [], 4.0)
    return ops


def link(ops):
    seen = {}
    for o in ops:
        dep, keep_order = set(), set()
        acc = [(r, False) for r in o["r"]] + [(w, True) for w in o["w"]]
        for r, wr in acc:
            name, a, b = r[0], r[1], r[2]
            ps = SCRATCH[name][0] == "psum"
            for (x, y, pw, po) in seen.get(name, ()):
                if po is o:
                    continue
                if ps and po["q"] == o["q"] == "p":
                    keep_order.add(po["i"])
                elif INORDER and wr and po["q"] == o["q"] and o["q"] in "vs":
                    if a < y and x < b:
                        keep_order.add(po["i"])
                elif (a < y and x < b and (wr or pw)) or (ps and po["q"] != o["q"]):
                    dep.add(po["i"])
        for r, wr in acc:
            name, a, b = r[0], r[1], r[2]
            full = wr and (len(r) < 4 or r[3][-1].step == 1) and len(r) < 5 and SCRATCH[name][0] != "psum"
            keep = [e for e in seen.get(name, ()) if e[3] is o or not (full and a <= e[0] and e[1] <= b)]
            if SCRATCH[name][0] == "psum":
                keep = keep[-12:]
            keep.append((a, b, wr, o))
            seen[name] = keep
        o["dep"] = sorted(dep)
        o["ord"] = sorted(keep_order)


def schedule(ops, est):
    N = len(ops)
    succ = [[] for _ in range(N)]
    need = [0] * N
    for o in ops:
        for d in o["dep"]:
            succ[d].append((o["i"], est["OWN"] if ops[d]["q"] == o["q"] else est["WAKE"]))
            need[o["i"]] += 1
        for d in o["ord"]:
            succ[d].append((o["i"], 0.0))
            need[o["i"]] += 1
        if o.get("tdep"):
            succ[o["tdep"][0]["i"]].append((o["i"], o["tdep"][1]))
            need[o["i"]] += 1
    pri = [0.0] * N
    for i in range(N - 1, -1, -1):
        pri[i] = ops[i]["cost"] + max([lat + pri[j] for j, lat in succ[i]] + [0.0])
    pri = [x + o["pb"] for x, o in zip(pri, ops)]
    start = [0.0] * N
    ready = {}
    for o in ops:
        if not need[o["i"]]:
            ready.setdefault(o["q"], []).append(o["i"])
    free, busy, order = {}, {}, []
    while len(order) < N:
        best = None
        for q, L in ready.items():
            if L:
                s = max(free.get(q, 0.0), min(start[i] for i in L))
                if best is None or s < best[0]:
                    best = (s, q)
        s, q = best
        i = max([i for i in ready[q] if start[i] <= s + 1e-9], key=lambda k: (pri[k], -k))
        ready[q].remove(i)
        o = ops[i]
        o["t0"] = s
        end = s + o["cost"]
        free[q] = s if o["kind"] == "arr" else (s + 0.05 if o["kind"] == "dma" else end)
        busy[q] = busy.get(q, 0.0) + o["cost"]
        order.append(i)
        for j, lat in succ[i]:
            start[j] = max(start[j], end + lat)
            need[j] -= 1
            if not need[j]:
                ready.setdefault(ops[j]["q"], []).append(j)
    return order, max(o["t0"] + o["cost"] for o in ops), busy


def place(ops, pred, key, back):
    N = len(ops)
    span = range(N - 1, -1, -1) if back else range(N)
    key = list(key)
    for i in span:
        for d, _ in pred[i]:
            if key[d] >= key[i]:
                key[i] = key[d] + 1e-7
    st, end, line = [0.0] * N, [0.0] * N, {}
    for i in sorted(span, key=lambda k: key[k]):
        o = ops[i]
        s = 0.0
        for d, lat in pred[i]:
            if end[d] + lat > s:
                s = end[d] + lat
        hold = o["hold"]
        if hold:
            L = line.setdefault(o["q"], [])
            k = len(L)
            while k and L[k - 1][0] > s:
                k -= 1
            if k and L[k - 1][1] > s:
                s = L[k - 1][1]
            while k < len(L) and L[k][0] < s + hold - 1e-9:
                s = L[k][1]
                k += 1
            L.insert(k, (s, s + hold))
        st[i], end[i] = s, s + o["cost"]
    return st, end


def improve(ops, est, tries):
    N = len(ops)
    pred, succ = [[] for _ in range(N)], [[] for _ in range(N)]
    for o in ops:
        o["hold"] = 0.0 if o["kind"] == "arr" else 0.05 if o["kind"] == "dma" else o["cost"]
        e = [(d, est["OWN"] if ops[d]["q"] == o["q"] else est["WAKE"]) for d in o["dep"]] + [(d, 0.0) for d in o["ord"]]
        if o.get("tdep"):
            e.append((o["tdep"][0]["i"], o["tdep"][1]))
        for d, lat in e:
            pred[o["i"]].append((d, lat))
            succ[d].append((o["i"], lat))

    slow = [o["cost"] for o in make_plan(dict(est, **SLOW))]

    def replay(st):
        end, free = [0.0] * N, {}
        for i in sorted(range(N), key=lambda k: (st[k], k)):
            o = ops[i]
            s = free.get(o["q"], 0.0) if o["hold"] else 0.0
            for d, lat in pred[i]:
                if end[d] + lat > s:
                    s = end[d] + lat
            end[i] = s + slow[i]
            free[o["q"]] = s + (slow[i] if o["hold"] == o["cost"] else o["hold"])
        return max(end)

    def passes(key, k):
        best = None
        for j in range(k):
            st, end = place(ops, pred, key, False)
            if best is None or max(end) < best[0] - 1e-9:
                best = (max(end), st)
            if j < k - 1:
                key = [-e for e in place(ops, succ, [-e for e in end], True)[1]]
        return (math.sqrt(best[0] * replay(best[1]) / 1.4), best[1])

    seed = [1]

    def rnd():
        seed[0] = (seed[0] * 1103515245 + 12345) % 2 ** 31
        return seed[0] / 2 ** 31

    best = cur = passes([o["t0"] for o in ops], 6)
    for k in range(tries):
        lo = rnd() * cur[0]
        if rnd() < 0.5:
            amp, hi = (0.2, 0.5, 1.0, 2.0)[int(4 * rnd())], lo + 3 + 12 * rnd()
            key = [s + (amp * (2 * rnd() - 1) if lo < s < hi else 0.0) for s in cur[1]]
        else:
            c, hi, d, q = int(2 * rnd()), lo + 1 + 8 * rnd(), 5 * (rnd() - rnd()), ("v", "s", "p", "vsp")[int(4 * rnd())]
            key = [s + (d if lo < s < hi and o["c"] == c and o["q"] in q else 0.0) for s, o in zip(cur[1], ops)]
        new = passes(key, 2)
        if new[0] - cur[0] <= -(0.15 * (1 - k / tries) + 0.02) * math.log(1 - rnd()):
            cur = new
        if new[0] < best[0]:
            best = new
    for o in ops:
        o["t0"] = best[1][o["i"]]
    return sorted(range(N), key=lambda i: (best[1][i], i)), best[0]


def waits(ops, order):
    cnt, know = {}, {}
    for i in order:
        o = ops[i]
        q = o["q"]
        kn = know.setdefault(q, {})
        w = {}
        for d in o["dep"]:
            s, v = ops[d]["done"]
            if kn.get(s, 0) < v and w.get(s, (0,))[0] < v:
                w[s] = (v, d)
        o["waits"] = []
        for s in sorted(w, key=lambda k: -ops[w[k][1]]["t0"]):
            v, d = w[s]
            if kn.get(s, 0) >= v:
                continue
            o["waits"].append((s, v))
            for a, z in ops[d]["snap"].items():
                kn[a] = max(kn.get(a, 0), z)
            kn[s] = max(kn.get(s, 0), v)
        if o["kind"] in ("arr", "dma"):
            o["done"] = (o["sem"], 16)
        elif o["kind"] in ("send", "rsend"):
            o["done"] = ("sent", 0)
        else:
            cnt[q] = cnt.get(q, 0) + 1
            o["done"] = (q, cnt[q])
        o["snap"] = dict(kn)
    return cnt


PLAN = {}


def plan():
    if not PLAN:
        first = []
        for lead in LEADS:
            ops = make_plan(dict(EST, LEAD=lead))
            link(ops)
            busy = schedule(ops, EST)[2]
            first.append((improve(ops, EST, TRIES // 20)[1], lead, ops))
        ops = min(first, key=lambda x: x[:2])[2]
        order, total = improve(ops, EST, TRIES)
        PLAN.update(ops=ops, order=order, cnt=waits(ops, order), total=total, busy=busy)
    return PLAN


def rank_program(g, core, T, topo):
    rank = T.rank_of(core)
    if rank is None:
        return
    pl = plan()
    ops = pl["ops"]
    N = len(T.cores)
    queue = {"v": g.vector, "s": g.scalar, "p": g.tensor, "q": g, "y": g.sync}

    def ap(r):
        if not isref(r):
            return r
        if r[0] == "ind":
            return ap(r[1]).indirect(ap(r[2]))
        return T[r[0]][r[3]]

    def side(r):
        if r[0] == "T":
            return T[r[1]][:, r[2]:r[3]] if len(r) > 2 else T[r[1]][:]
        return ap(r)

    nxt = T.cores[(rank + 3) % N]
    sent = [0]
    narr = {}
    for t in range(1, ROUNDS):
        for c in range(NC):
            for k in "emo":
                narr["%s%d_%d" % (k, t, c)] = len(topo.engines(T.cores[(rank - 3) % N], core))
    narr["ar"] = sum(len(topo.engines(T.cores[(rank - 3 * t) % N], core)) for t in range(1, ROUNDS))
    for i in pl["order"]:
        o = ops[i]
        k, a = o["kind"], o["args"]
        if k == "arr":
            continue
        Q = queue[o["q"]]
        for s, v in o["waits"]:
            Q.wait_ge(T.sem[s], narr.get(s, v))
        if k == "ts":
            r = Q.tensor_scalar(ap(a[0]), ap(a[1]), ap(a[2]), ap(a[3]), a[4]) if a[5] is None else \
                Q.tensor_scalar(ap(a[0]), ap(a[1]), ap(a[2]), ap(a[3]), a[4], a[5])
        elif k == "tt":
            r = Q.tensor_tensor(ap(a[0]), ap(a[1]), ap(a[2]), a[3])
        elif k == "scan":
            r = Q.tensor_tensor_scan(ap(a[0]), ap(a[1]), ap(a[2]), a[3], a[4], a[5])
        elif k == "cp":
            r = Q.tensor_copy(ap(a[0]), ap(a[1]))
        elif k == "ms":
            r = Q.memset(ap(a[0]), a[1])
        elif k == "act":
            r = Q.activation(ap(a[0]), ap(a[1]), a[2], bias=ap(a[3]), scale=a[4], accum_out=ap(a[5]))
        elif k == "mm":
            for m in a:
                r = Q.matmul(ap(m[0]), ap(m[1]), ap(m[2]), m[3], m[4])
        elif k == "iota":
            r = Q.iota(ap(a[0]), a[1], a[2], a[3], allow_small_or_imprecise_dtypes=True)
        elif k == "dma":
            Q.dma_start(side(a[0]), side(a[1])).then_inc(T.sem[o["sem"]], 16)
            continue
        elif k == "send":
            rid, pid = topo.addr(nxt, core)
            Q.remote_dma(ap(a[1]), ap(a[0]), T.sem[a[2]], T.sem["sent"], pid, rid, topo.mask(core, nxt))
            sent[0] += len(topo.engines(core, nxt))
            continue
        else:
            ids, dsts = [], []
            for t in range(1, ROUNDS):
                d = T.cores[(rank + 3 * t) % N]
                rid, pid = topo.addr(d, core)
                ids.append(DstId(rid=rid, pnc=pid))
                dsts.append(ap(R("rr", 256 * t, 256 * t + 256)))
            Q.remote_dma_fused([RemoteDMATransfer(dst_ids=ids, dma_engine_mask=topo.mask(core, nxt), remote_sem=T.sem["ar"],
                                                  srcs=[ap(R("rr", 0, 256))], dsts=dsts)], local_sem=T.sem["sent"])
            sent[0] += len(topo.engines(core, nxt))
            continue
        r.then_inc(T.sem[o["q"]], 1)
    for s in sorted(pl["cnt"]):
        g.wait_ge(T.sem[s], pl["cnt"][s])
    g.wait_ge(T.sem["sent"], sent[0])
    for s in ("dr", "dx", "dc", "oy0", "oy1", "oc"):
        g.sync.wait_ge(T.sem[s], 16)
